import numpy as np, ml_dtypes
CORES = [40,41,42,43,44,45,46,47]
N = 8
BF = ml_dtypes.bfloat16
def gentries(a):
    return np.ascontiguousarray(a.reshape(8, 16, -1).transpose(0, 2, 1)).reshape(8, -1)
def gtable(e):
    e = np.asarray(e); return np.ascontiguousarray(e.reshape(8, -1, 16).transpose(0, 2, 1)).reshape(128, -1).astype(np.int32)
B, J, CAP, RO, Q = 3072, 4096, 32, 4, 4096
LN, LJ = 3, 12
M = N * CAP; W = B + RO * M
WT = (14 * np.arange(16) + 9)[:, None]
def decode(n):
    C = np.add.accumulate((n * n[..., ::-1]) >> 12, axis=-1)
    x = (C[..., -1:] * np.arange(J)) >> LJ
    return np.add.reduce((C[..., None] <= x[..., None, :]).astype(np.int64), axis=-2)
def combine(x, y, z):
    q = x.shape[-1] // 4
    k = np.concatenate([np.minimum(x[..., :q], y[..., :q]), np.maximum(x[..., q:2 * q], y[..., q:2 * q]), np.abs(x[..., 2 * q:3 * q] - y[..., 2 * q:3 * q]), x[..., 3 * q:] + y[..., 3 * q:]], axis=-1)
    return np.minimum(k, z)
def sizes(c):
    c = np.sort(c, axis=-1); z = np.zeros(c.shape[:-1] + (1,), np.int64)
    return np.diff(np.concatenate([z, c, z + B - 256], axis=-1), axis=-1) + 64
def span(rng, v, share):
    o = rng.integers(0, B, (3, N, 8, 1, 2048)); x, y, z = [np.take_along_axis(v, i, 3) for i in o]
    s = np.sort(np.add.reduce(combine(x, y, z), axis=2), axis=-1)
    m = np.minimum(np.maximum((2048 * share).astype(np.int64), 1), 2048); k = (rng.random((N, 8)) * (2048 - m)).astype(np.int64)
    return np.concatenate([np.take_along_axis(s, k[..., None], 2), np.take_along_axis(s, (k + m - 1)[..., None], 2)], axis=2)
def shares(rng):
    return CAP * N * 2.0 ** -LJ * rng.choice(np.array([0.4, 0.8, 1.0, 1.5]), (N, 8))
def parts(rng):
    e = rng.choice(np.array([0.5, 1.0, 1.0, 2.0]), (N, 8, 16, 1))
    v = np.minimum((256 * rng.random((N, 8, 16, B)) ** e).astype(np.int64), 255)
    n = sizes(rng.integers(0, B - 255, (N, 8, 3))); r = rng.integers(0, 4096, (3, N, 8, RO, J))
    u = (rng.random((N, 8, Q)) < rng.choice(np.array([0.05, 0.2, 0.5]), (N, 8, 1))).astype(np.int64)
    return v, n, span(rng, v, shares(rng)), r, u
def pack(v, n, lim, r, u):
    t = [np.stack([gtable(a.reshape(8, -1)) for a in b]) for b in r]
    return {"bank": np.ascontiguousarray(v.reshape(N, 128, B)).astype(np.float32).astype(BF), "ncl": n.astype(np.int32), "lim": lim.astype(np.int32),
            "ra": t[0], "rb": t[1], "rc": t[2], "used": u.astype(np.int32)}
def goals(rng, k):
    return np.stack([rng.permutation(Q - 1)[:k] + 1 for p in range(N)]) * N + np.arange(N)[:, None]
def keyed(rng, d):
    c = rng.integers(1, 256, (16, d.size)); c[[0, 1, 15]] = rng.integers(40, 101, (3, d.size))
    e = (d - np.add.reduce(c * WT, axis=0)) & (N * Q - 1)
    c[15] += e // 219; e = e % 219; c[0] += e // 9 - 5 * (e % 9); c[1] += 2 * (e % 9)
    return c
def put(rng, v, n, q, g, d):
    s = np.add.accumulate(n[q, g]) - n[q, g]; v[q, g][:, s] = 255; v[q, g][:, s + 1] = 0
    w = rng.permutation(np.setdiff1d(np.arange(B), np.concatenate([s, s + 1])))[:d.size]
    v[q, g][:, w] = keyed(rng, d.reshape(-1)); return w.reshape(d.shape)
def deal(rng, col, at, w):
    o = rng.permutation(np.repeat(np.arange(N), CAP)); at = np.sort(rng.permutation(at)[:M])
    for p in range(N): col[at[o == p]] = w[p]
def play(r, n, q, g, t, col):
    h = J // 4; k = B + t * M; r[:2, q, g, t] = 0; r[2, q, g, t] = (col * 4096 + k - 1) // k
    if t == 0:
        m = n[q, g][3 - decode(n[q, g])[2 * h:3 * h]]; r[1, q, g, 0, 2 * h:3 * h] = (4096 + m - 1) // m
def setup_inputs(rng):
    return pack(*parts(rng))
def setup_inputs_room(rng):
    v, n, lim, r, u = parts(rng); lim[:] = (1500, 2600)
    for q in range(N):
        for g in range(8):
            m = n[q, g]; p = np.concatenate([np.arange(k) for k in m]); live = p >= np.repeat(m // 2, m)
            c = np.where(live, rng.integers(110, 150, (16, B)), rng.integers(0, 90, (16, B)))
            c[0] += (p - np.add.reduce(c * WT, axis=0)) & (N - 1)
            c[:, p == 0] = 0; c[:, p == 1] = 255; v[q, g] = c
            t = rng.choice(np.array([0, 1, CAP - 1, CAP, CAP + 1, 2 * CAP]), N)
            if q == 0: t[1] = (CAP, CAP + 1, CAP - 1, CAP, 0, 1, 2 * CAP, CAP)[g]
            if g == 6: t[2] = 0
            own = np.full(J, -1); own[rng.permutation(J)[:int(np.sum(t))]] = rng.permutation(np.repeat(np.arange(N), t))
            a = decode(m); na = m[a]; nb = m[3 - a]; h = na // 2
            dead = 2 + (rng.random(J) * (h - 2)).astype(np.int64)
            good = h + (own - h) % N + N * (rng.random(J) * ((na - h - N) // N + 1)).astype(np.int64)
            i = np.where(own < 0, dead, good); y = (np.arange(J) < J // 4).astype(np.int64)
            r[0, q, g, 0] = (i * 4096 + na - 1) // na; r[1, q, g, 0] = (y * 4096 + nb - 1) // nb; r[2, q, g, 0] = (4096 + B - 1) // B
    return pack(v, n, lim, r, u)
def setup_inputs_ends(rng):
    v, n, lim, r, u = parts(rng); v[..., 0] = 0; v[..., B - 1] = 255
    for g in range(4):
        n[:, g] = 64; n[:, g, g] = B - 192
    n[:, 5] = n[:, 2]; lim[0, 5] = (1, 4080)
    for g in (0, 2, 4): r[:, :, g] = rng.choice(np.array([0, 1, 4094, 4095]), (3, N, RO, J))
    lim[:, 0] = (0, 4080); lim[:, 2] = (4080, 4080); lim[:, 4] = (0, 0); lim[:, 6, 0] = lim[:, 6, 1]
    r[:, :, 2, 0, J - 1] = 4095; r[2, :, 4, 0, :8] = 0; u[:, 2] = 0; u[:, 4] = 0
    r[2, :, 0, 0, :8] = 0; u[:, 0] = 0
    lim[:, 1] = (1, 4080); lim[:, 3] = (1, 4080); lim[:, 7] = (0, 4079); u[:, 1] = 0; u[:, 3] = 0; u[:, 7] = 0
    full = goals(rng, RO * M).reshape(N, RO, N, CAP)
    grid = goals(rng, M).reshape(N, N, CAP); grid[1:, N - 1, CAP - 1] = grid[1:, 0, 0]
    many = goals(rng, 2 * CAP); at = np.concatenate([np.arange(J // 4, J // 2), np.arange(3 * J // 4, J)])
    for q in range(N):
        w = put(rng, v, n, q, 3, full[:, :, q])
        for t in range(RO):
            col = np.full(J, 1); deal(rng, col, at, w[:, t]); play(r, n, q, 3, t, col)
        i = J // 8 + rng.permutation(J // 8)[:4]; r[0, q, 3, RO - 1, i] = rng.integers(1000, 4096, 4); r[2, q, 3, RO - 1, i] = 0
        w = put(rng, v, n, q, 7, grid[:, q])
        if q == N - 1: w[0, CAP - 1] = 1
        col = np.zeros(J, np.int64); deal(rng, col, np.arange(J), w); play(r, n, q, 7, 0, col)
        w = put(rng, v, n, q, 1, many[(q + 1) % N]); col = np.full(J, 1); k = J // 4
        if q > 0: k += int(rng.integers(0, CAP))
        i = np.sort(rng.permutation(J // 2)[:k]); col[i] = w[rng.integers(0, CAP, k)]; col[i[:CAP]] = w[:CAP]
        col[J // 2 + rng.permutation(J // 2)[:2 * CAP]] = np.tile(w[CAP:], 2); play(r, n, q, 1, 0, col)
    return pack(v, n, lim, r, u)
def setup_inputs_alike(rng):
    v, n, lim, r, u = parts(rng)
    a = rng.integers(1, 255, (8, 16, 3)); tw = np.zeros((16, 1), np.int64); tw[:4, 0] = (1, -1, -1, 1)
    pool = np.concatenate([a, a + tw], axis=2)
    for g in range(1, 8, 2):
        v[:, g] = pool[g][:, rng.integers(0, 6, (N, B))].transpose(1, 0, 2)
        for q in range(N):
            e = np.add.accumulate(n[q, g]); v[q, g][:, e - n[q, g]] = pool[g][:, :1]; v[q, g][:, e - 1] = pool[g][:, 3:4]
    lim[:, 1::2] = (0, 4080); u[:, 1::2] = 0; r[:, :, 1::2, 0, 0] = 0; r[:, :, 1::2, 0, 1] = 4095
    v[:, 2] = v[0, 2]; n[:, 2] = n[0, 2]; lim[:, 2] = lim[0, 2]; r[:, :, 2] = r[:, :1, 2]
    return pack(v, n, lim, r, u)
def setup_inputs_cold(rng):
    v, n, lim, r, u = parts(rng); o = rng.permutation(N); g = int(rng.integers(0, 8))
    lim[o[0]] = (1, 0); lim[o[0], 1::2] = (1600, 1000); lim[o[1]] = (0, 4080)
    lim[:, g] = (1700, 1100); lim[o[0], g] = (2000, 1999); lim[o[1], g] = (4080, 0); u[:, (g + 1) % 8] = 1; u[:, (g + 2) % 8] = 0
    u[o[2], (g + 3) % 8] = 1
    return pack(v, n, lim, r, u)
def setup_inputs_spread(rng):
    v, n, lim, r, u = parts(rng)
    v = np.minimum((np.exp2(8 * rng.random((N, 8, 1, B))) * rng.random((N, 8, 16, B))).astype(np.int64), 255)
    n = sizes(((B - 256) * rng.random((N, 8, 3)) ** 4).astype(np.int64))
    e = rng.choice(np.array([0.5, 1.0, 2.0, 3.0]), (3, N, 8, RO, 1)); r = np.minimum((4096 * rng.random((3, N, 8, RO, J)) ** e).astype(np.int64), 4095)
    u = (rng.random((N, 8, Q)) < 0.8 * rng.random((N, 8, 1))).astype(np.int64)
    return pack(v, n, span(rng, v, shares(rng)), r, u)
def check_inputs(d):
    bad = []; b = np.asarray(d["bank"]).astype(np.float32)
    if not np.all((b >= 0) & (b <= 255) & (b == np.floor(b))): bad.append("bank: whole numbers from 0 to 255")
    for k, lo, hi in (("ncl", 64, B), ("lim", 0, 4080), ("ra", 0, 4095), ("rb", 0, 4095), ("rc", 0, 4095), ("used", 0, 1)):
        if np.min(d[k]) < lo or np.max(d[k]) > hi: bad.append("range of " + k)
    if np.any(np.sum(np.asarray(d["ncl"]).astype(np.int64), axis=-1) != B): bad.append("sums of ncl")
    return bad
def reference(bank, ncl, lim, ra, rb, rc, used):
    v = np.zeros((N, 8, 16, W), np.int32); v[..., :B] = bank.astype(np.float32).astype(np.int32).reshape(N, 8, 16, B)
    n = np.zeros((N, 8, 4 + RO), np.int64); n[:, :, :4] = ncl
    la, lb, lc = [np.stack([gentries(a) for a in b]).astype(np.int64).reshape(N, 8, RO, J) for b in (ra, rb, rc)]
    free = used == 0; lo = lim[:, :, :1]; hi = lim[:, :, 1:]; take = np.take_along_axis
    for t in range(RO):
        s = 4 + t; m = n[:, :, :s].copy(); start = np.add.accumulate(m, axis=2) - m; tot = np.add.reduce(m, axis=2)
        a = decode(m); b = s - 1 - a
        ix = take(start, a, 2) + ((take(m, a, 2) * la[:, :, t]) >> 12)
        iy = take(start, b, 2) + ((take(m, b, 2) * lb[:, :, t]) >> 12)
        iz = (tot[:, :, None] * lc[:, :, t]) >> 12
        x, y, z = [take(v, i[:, :, None, :], 3) for i in (ix, iy, iz)]
        k = combine(x, y, z)
        total = np.add.reduce(k, axis=2); key = np.add.reduce(k * WT, axis=2)
        alive = (total >= lo) & (total <= hi); owner = key & (N - 1); bucket = (key >> LN) & (Q - 1)
        for p in range(N):
            for g in range(8):
                got = [np.flatnonzero(alive[q, g] & (owner[q, g] == p))[:CAP] for q in range(N)]
                c = np.concatenate([k[q, g][:, got[q]] for q in range(N)], axis=1); bu = np.concatenate([bucket[q, g, got[q]] for q in range(N)])
                first = np.sort(np.unique(bu, return_index=True)[1])
                keep = first[free[p, g, bu[first]]]; e = int(tot[p, g])
                v[p, g][:, e:e + len(keep)] = c[:, keep]; free[p, g, bu[keep]] = False; n[p, g, s] = len(keep)
    return {"y": np.ascontiguousarray(v[..., B:]).reshape(N, 128, RO * M).astype(np.float32).astype(BF)}

@@ -1,0 +1,501 @@
+from concourse.bass import DstId, RemoteDMATransfer
+from concourse.mybir import dt, AluOpType as ALU, AxisListType as AX, ActivationFunctionType as AF
+
+B, J, CAP, RO, NR = 3072, 4096, 32, 4, 8
+M1 = 1.5 * 2.0 ** 23
+MN = 1.5 * 2.0 ** 16
+M256 = 1.5 * 2.0 ** 15
+M32 = 1.5 * 2.0 ** 28
+M4096 = 1.5 * 2.0 ** 35
+MID = 1920
+NA = 12
+SEG = 41
+f32, bf, i32, u16, f16 = "float32", "bfloat16", "int32", "uint16", "float16"
+
+SCRATCH = {}
+for _d, _l in (
+    (bf, "bankS 4352,K 4112,YG 4096,FX 4096,XG 4096,ZG 512,ONE 256,ZERO 256,TRI 128,BID 128,DG 128,NDG 128,WCP 16,W0C 8,WBL 128,BON 128,W0 128,LI 2048,LP 2048,"
+         "COLT 256,CL 128,DM 16 16,RS 512,RSS 144,MSK 144,MI 256,JC 1,RH 256,IND 128,LQ 1024,OWN 256,O 2048,S4 256,U 2048,Z 328,EO 512,CU 512,IN 512,C2 512,SMM 144,SS 144,UG 256,"
+         "E3 16 272,POS 256,X 256,send 1024,land 1024"),
+    (i32, "USED 4368,RA 1024,RB 1024,RC 1024,PID 1,TI 8,ONEI 256,OI 256,OJ 256,KLI 16,KLJ 16"),
+    (f32, "CC 32,IR 256,IG 128,II 128,GB 256,I16 16 16,IF 256,I9 144,JL 16,ONEF 128,MK 8,MD 8,MS 8,MQ 128,RQ 32,NEGM 8,IT 128,MIDT 256,HALF 256,F4 32,R8 8,TC 8,PP 8,PR 8,"
+          "SEL 16,SM 8,CS 16,DQ 32,DS 32,HI 4,LO 4,RCF 1024,OA 256,W1 256,V1 256,Z1 256,J16 16,R32 16,INV 16,BL 16,ZT 16,WJ 16,D1 16,UJ 16,E1 16"),
+    (u16, "OX 256,OY 256,OZ 256,OFJ 16,BU 16,DU 16,EU 16,OC 16"),
+    (f16, "RP 8,LJ 256,KBH 256"),
+):
+    for _x in _l.split(","):
+        _x = _x.split()
+        SCRATCH[_x[0]] = ("sbuf", [128] + [int(v) for v in _x[1:]], _d)
+SCRATCH.update({"NL": ("sbuf", [8, 4], i32), "LM": ("sbuf", [8, 2], i32), "NLF": ("sbuf", [8, 4], f32), "LMF": ("sbuf", [8, 8], f32),
+                "SL8": ("sbuf", [8, 128], f32), "DM8": ("sbuf", [8, 512], f32)})
+for _k in range(8):
+    SCRATCH["b%d" % _k] = ("psum", [128, 512], f32)
+_DMAS = ["ncl", "lim", "bank", "ra0", "rb0", "rc0", "ra1", "rb1", "rc1", "used", "out"]
+SEMAPHORES = ["sV", "sA", "sP", "sG"] + ["d_" + n for n in _DMAS] + ["arr%d" % t for t in range(RO)] + ["sent%d" % t for t in range(RO)]
+BANKS = tuple("b%d" % k for k in range(8))
+
+
+def rank_program(g, core, T, topo):
+    rank = T.rank_of(core)
+    if rank is None:
+        return
+    eng = {"V": g.vector, "A": g.scalar, "P": g.tensor, "G": g, "S": g.sync}
+    cnt = {"V": 0, "A": 0, "P": 0, "G": 0}
+    seen = {e: {} for e in eng}
+    lastw, readers = {}, {}
+
+    def wait(e, sem, val):
+        if seen[e].get(sem, 0) < val:
+            eng[e].wait_ge(T.sem[sem], val)
+            seen[e][sem] = val
+
+    def order(e, r, w):
+        req = {}
+        me = "s" + e
+
+        def add(ev):
+            if ev is not None:
+                req[ev[0]] = max(req.get(ev[0], 0), ev[1])
+        for k in r:
+            add(lastw.get(k))
+        for k in list(w) + [k for k in r if k in BANKS]:
+            add(lastw.get(k))
+            for ev in readers.get(k, {}).items():
+                if ev[0] != me:
+                    add(ev)
+        if e == "P":
+            req.pop("sP", None)
+        for sem in sorted(req):
+            wait(e, sem, req[sem])
+
+    def note(ev, r, w):
+        for k in r:
+            readers.setdefault(k, {})[ev[0]] = ev[1]
+        for k in w:
+            lastw[k] = ev
+            readers[k] = {}
+
+    def do(e, call, r, w):
+        r, w = r.split(), w.split()
+        order(e, r, w)
+        cnt[e] += 1
+        call(eng[e]).then_inc(T.sem["s" + e], 1)
+        note(("s" + e, cnt[e]), r, w)
+
+    def dma(e, name, out, in_, r, w):
+        r, w = r.split(), w.split()
+        order(e, r, w)
+        eng[e].dma_start(out, in_).then_inc(T.sem["d_" + name], 16)
+        note(("d_" + name, 16), r, w)
+
+    def ts(out, in0, s1, op0, r, w, s2=None, op1=None):
+        if op1 is None:
+            do("V", lambda v: v.tensor_scalar(out, in0, s1, None, op0), r, w)
+        else:
+            do("V", lambda v: v.tensor_scalar(out, in0, s1, s2, op0, op1), r, w)
+
+    def tt(out, a, b, op, r, w):
+        do("V", lambda v: v.tensor_tensor(out, a, b, op), r, w)
+
+    def cp(out, a, r, w):
+        do("V", lambda v: v.tensor_copy(out, a), r, w)
+
+    def ms(ap, c, w):
+        do("V", lambda v: v.memset(ap, c), "", w)
+
+    def mm(out, l, rh, r, w, start=True, stop=True):
+        do("P", lambda p: p.matmul(out, l, rh, start, stop), r, w)
+
+    def act(out, a, fn, r, w, scale=1.0, bias=0.0):
+        do("A", lambda s: s.activation(out, a, fn, bias=bias, scale=scale), r, w)
+
+    def iota(ap, pat, cm, w, base=0):
+        do("G", lambda q: q.iota(ap, pat, base, cm, allow_small_or_imprecise_dtypes=True), "", w)
+
+    def scan(out, d0, d1, op0, op1, r, w):
+        do("V", lambda v: v.tensor_tensor_scan(out, d0, d1, 0.0, op0, op1), r, w)
+
+    dma("S", "ncl", T.NL[:, :], T.ncl[:, :], "", "NL")
+    dma("S", "lim", T.LM[:, :], T.lim[:, :], "", "LM")
+    dma("A", "rb0", T.RB[:, 0:256], T.rb[:, 0:256], "", "RB0")
+    dma("A", "ra0", T.RA[:, 0:256], T.ra[:, 0:256], "", "RA0")
+    dma("A", "rc0", T.RC[:, 0:256], T.rc[:, 0:256], "", "RC0")
+    dma("S", "bank", T.bankS[:, 0:B], T.bank[:, :], "", "bk")
+    iota(T.PID[:, :], [[1, 1]], 1, "PID")
+    iota(T.IG[:, :], [[1, 8], [0, 16]], 0, "IG")
+    iota(T.II[:, :], [[0, 8], [1, 16]], 0, "II")
+    iota(T.IR[:, :], [[1, 256]], 0, "IR")
+    ms(T.ONE[:, :], 1.0, "ONE")
+    for n in ("b", "a", "c"):
+        dma("S", "r%s1" % n, T["R" + n.upper()][:, 256:1024], T["r" + n][:, 256:1024], "", "R%s1" % n.upper())
+    do("G", lambda q: q.affine_select(T.DG[:, :], T.ONE[:, 0:128], [[1, 128]], ALU.is_equal, 0.0, 0, -1), "ONE", "DG")
+    iota(T.bankS[:, B:4096], [[0, 1024]], 0, "bkz")
+    iota(T.GB[:, :], [[1, 8], [0, 32]], 0, "GB")
+    do("G", lambda q: q.affine_select(T.TRI[:, :], T.ONE[:, 0:128], [[1, 128]], ALU.is_gt, 0.0, 0, -1), "ONE", "TRI")
+    do("G", lambda q: q.affine_select(T.BID[:, :], T.DG[:, :], [[1, 128]], ALU.not_equal, -1.0, -1, -1), "DG", "BID")
+    iota(T.IF[:, :], [[0, 16], [1, 16]], 0, "IF")
+    iota(T.I9[:, :], [[0, 16], [1, 9]], 0, "I9")
+    iota(T.I16[:, :, :], [[0, 16], [1, 16]], 0, "I16")
+    iota(T.JL[:, :], [[16, 16]], 0, "JL")
+    iota(T.LI[:, :], [[0, 2048]], 0, "LI")
+    iota(T.LP[:, :], [[0, 2048]], 0, "LP")
+    iota(T.USED[:, 0:4096], [[0, 4096]], 0, "USED")
+    iota(T.USED[:, 4096:4112], [[0, 16]], 0, "USEDx", 1)
+    iota(T.ONEI[:, :], [[0, 256]], 0, "ONEI", 1)
+    dma("S", "used", T.USED[0:128:16, 0:4096], T.used[:, :], "", "USED")
+
+    CC = T.CC
+    col = {n: CC[:, k:k + 1] for k, n in enumerate(
+        ["pid", "i", "m", "typ", "grp", "p8", "c16", "wt", "podd", "sgs", "msg", "off", "tm1", "cval", "i0",
+         "mm1", "sm0", "sm1", "sm2", "sm3", "t0", "t1", "c32", "m15", "on1"])}
+    for k, (sh, an) in enumerate([(0, 255), (0, 15), (1, 7), (0, 1), (4, 7), (0, 7), (3, 15)]):
+        ts(T.TI[:, k:k + 1], T.PID[:, :], sh, ALU.arith_shift_right, "PID", "TI%d" % k, an, ALU.bitwise_and)
+    cp(CC[:, 0:7], T.TI[:, 0:7], "TI0 TI1 TI2 TI3 TI4 TI5 TI6", "CC")
+    for n, src, a, b, key in (("tm1", "typ", 1.0 / 256, -1.0 / 256, "CCt"), ("sm0", "m", -1.0, 3.0, "CCx0"), ("mm1", "m", 1.0, -1.0, "CCn"), ("msg", "typ", -2.0, 1.0, "CCm"),
+                              ("off", "typ", -1.0, 1.0, "CCf"), ("wt", "i", 14.0, 9.0, "CCw"), ("sm1", "m", -1.0, 4.0, "CCx1"), ("sm2", "m", -1.0, 5.0, "CCx2"),
+                              ("sm3", "m", -1.0, 6.0, "CCx3"), ("podd", "p8", 2.0, 1.0, "CCo"), ("c32", "c16", 1.0, 16.0, "CC2"),
+                              ("m15", "pid", 0.0, -15.0, "CCg"), ("on1", "pid", 0.0, 1.0, "CCh")):
+        act(col[n], col[src], AF.Copy, "CC", key, a, b)
+        if n == "mm1":
+            act(T.COLT[:, :], T.IR[:, :], AF.Identity, "IR CCt", "COLT", 1.0 / 256, col["tm1"])
+    act(T.JC[:, :], col["pid"], AF.Copy, "CC", "JC")
+    ts(col["sgs"], col["typ"], 2.0 / 4096, ALU.mult, "CC", "CCs", -1.0 / 4096, ALU.add)
+    ts(T.BON[:, :], T.IG[:, :], col["grp"], ALU.is_equal, "IG CC", "BON")
+    ts(T.SL8[:, :], T.IG[0:8, :], CC[0:8, 0:1], ALU.is_equal, "IG CC", "SL8")
+    ts(T.IT[:, :], T.II[:, :], col["sgs"], ALU.mult, "II CCs", "IT", 9999.0 / 4096, ALU.add)
+    ts(T.MK[:, :], T.IR[:, 0:8], col["m"], ALU.is_equal, "IR CC", "MK")
+    ts(col["i0"], col["i"], 0.0, ALU.is_equal, "CC", "CCi")
+    tt(T.IT[:, :], T.IT[:, :], T.BON[:, :], ALU.mult, "IT BON", "IT")
+    ts(T.MS[:, :], T.IR[:, 0:8], col["mm1"], ALU.is_equal, "IR CCn", "MS")
+    ms(T.RQ[:, :], 1.0, "RQ")
+    ts(T.IT[:, :], T.IT[:, :], -9999.0 / 4096, ALU.add, "IT", "IT")
+    ms(T.RQ[:, 0:32:8], 0.0, "RQ")
+    tt(T.MD[:, :], T.MK[:, :], T.MS[:, :], ALU.subtract, "MK MS", "MD")
+    cp(T.NLF[:, :], T.NL[:, :], "NL", "NLF")
+    for b in ("b0", "b7"):
+        mm(T[b][:, 0:4], T.SL8[:, :], T.NLF[:, :], "SL8 NLF", b)
+
+    def masks(t):
+        q, s = 32 * t, 4 + t
+        ts(T.PR[:, :], T.IR[:, 0:8], col["sm%d" % t], ALU.is_equal, "IR CCx%d" % t, "PR")
+        ts(T.DS[:, 0:8], T.IR[:, 0:8], 1.0, ALU.subtract, "IR CCx%d" % t, "DS", col["sm%d" % t], ALU.is_equal)
+        ts(T.DS[:, 24:32], T.IR[:, 0:8], float(s - 1), ALU.is_le, "IR", "DSd")
+        ts(T.MQ[:, q:q + 8], T.MD[:, :], 1.0 / 4096, ALU.mult, "MD", "MQ%d" % t)
+        tt(T.DS[:, 8:16], T.PR[:, :], T.DS[:, 0:8], ALU.subtract, "PR DS", "DSb")
+        ts(T.DQ[:, 0:8], T.DS[:, 24:32], T.MK[:, 0:1], ALU.mult, "DSd MK", "DQ")
+        cp(T.MQ[:, q + 16:q + 24], T.MS[:, :], "MS", "MQ%da" % t)
+        ts(T.MQ[:, q + 8:q + 16], T.DS[:, 8:16], 1.0 / 4096, ALU.mult, "DSb", "MQ%db" % t)
+        tt(T.MQ[:, q + 24:q + 32], T.DQ[:, 0:8], T.PR[:, :], ALU.subtract, "DQ PR", "MQ%dc" % t)
+    masks(0)
+    ms(T.F4[:, :], 0.0, "F4")
+    ms(T.R8[:, :], 0.0, "R8")
+    ms(T.SEL[:, :], 0.0, "SEL")
+    for k in range(4):
+        cp(T.F4[:, 8 * k:8 * k + 4], T.b0[:, 0:4], "b0 F4", "F4%d" % k)
+        act(T.R8[:, 7 - k:8 - k], T.b7[:, k:k + 1], AF.Copy, "b7 R8", "R8%d" % k)
+    ms(T.NEGM[:, :], -M4096, "NEGM")
+    ts(col["t0"], col["i"], 1.0, ALU.is_equal, "CC", "CC0", 2.0 ** -13, ALU.mult)
+    ts(col["t1"], col["i"], 2.0, ALU.is_equal, "CC", "CC1", -float(MID), ALU.mult)
+    ms(T.TC[:, 0:1], float(B), "TC")
+    ts(col["cval"], col["i0"], -0.5, ALU.mult, "CCi CC0", "CCv", col["t0"], ALU.add)
+    ms(T.TC[:, 1:2], B / 4096.0, "TC1")
+    tt(col["cval"], col["cval"], col["t1"], ALU.add, "CCv CC1", "CCv")
+
+    bankk = "bk bkz"
+    win = T.bankS[:, 0:4096]
+    c0 = -(MID + 0.5) + 2.0 ** -13
+    F4k, R8k = "F4 F40 F41 F42 F43", "R8 R80 R81 R82 R83"
+
+    def prep(t, app=()):
+        app = list(app) + [lambda: None] * (5 - len(app))
+        s = 4 + t
+        CS, SEL = T.CS, T.SEL
+        ct = SEL[:, s:s + 1]
+        c = slice(256 * t, 256 * t + 256)
+        tt(T.DQ[:, :], T.F4[:, :], T.MQ[:, 32 * t:32 * t + 32], ALU.mult, F4k + " MQ%d MQ%da MQ%db MQ%dc" % (t, t, t, t), "DQ")
+        tt(T.PP[:, 0:s], T.F4[:, 0:s], T.R8[:, 8 - s:8], ALU.mult, F4k + " " + R8k, "PP")
+        scan(T.DS[:, :], T.RQ[:, :], T.DQ[:, :], ALU.mult, ALU.add, "RQ DQ", "DS")
+        ts(T.PR[:, 0:s], T.PP[:, 0:s], -2047.5, ALU.add, "PP", "PR", M4096, ALU.add)
+        scan(SEL[:, 1:s + 1], T.PR[:, 0:s], T.NEGM[:, 0:s], ALU.add, ALU.add, "PR NEGM", "SEL")
+        ts(T.HI[:, 0:2], T.DS[:, 7:16:8], MN, ALU.add, "DS", "HI", MN, ALU.subtract)
+        tt(T.SM[:, :], SEL[:, 0:8], T.MK[:, :], ALU.mult, "SEL MK", "SM")
+        do("V", lambda v: v.reciprocal(CS[:, 1:2], ct), "SEL", "CS1")
+        do("V", lambda v: v.tensor_reduce(CS[:, 2:3], T.SM[:, :], AX.X, ALU.add), "SM", "CS2")
+        ts(T.HI[:, 2:4], T.DS[:, 23:32:8], M32, ALU.add, "DS", "HI2", M32, ALU.subtract)
+        app[0]()
+        ts(CS[:, 3:4], CS[:, 2:3], CS[:, 1:2], ALU.mult, "CS1 CS2", "CS3", -0.46875 / 256, ALU.add)
+        app[1]()
+        tt(T.LO[:, :], T.DS[:, 7:32:8], T.HI[:, :], ALU.subtract, "DS HI HI2", "LO")
+        ts(CS[:, 4:5], CS[:, 3:4], M256, ALU.add, "CS3", "CS4", M256, ALU.subtract)
+        if t:
+            act(T.Z1[:, :], T.RCF[:, c], AF.Copy, "RCF TC1", "Z1", T.TC[:, 1:2], c0)
+        else:
+            ts(T.Z1[:, :], T.RC[:, c], T.TC[:, 1:2], ALU.mult, "RC0 TC1", "Z1", c0, ALU.add)
+        app[2]()
+        ts(CS[:, 5:6], CS[:, 4:5], ct, ALU.mult, "SEL CS2 CS4", "CS5", CS[:, 2:3], ALU.subtract)
+        app[3]()
+        ts(T.OZ[:, :], T.Z1[:, :], M1, ALU.add, "Z1", "OZ", M1 - MID, ALU.subtract)
+        ts(CS[:, 6:7], CS[:, 5:6], col["msg"], ALU.mult, "CS5 CCm CCf", "CS6", col["off"], ALU.add)
+        app[4]()
+
+    def lists(t):
+        CS, ct, k = T.CS, T.SEL[:, 4 + t:5 + t], "%d" % (t > 0)
+        c = slice(256 * t, 256 * t + 256)
+        ts(T.RH[:, :], T.COLT[:, :], CS[:, 4:5], ALU.is_ge, "COLT CS4", "RH")
+        ts(T.IND[:, :], T.IT[:, :], ct, ALU.mult, "IT SEL CS6", "IND", CS[:, 6:7], ALU.is_ge)
+        for b in ("b2", "b4"):
+            mm(T[b][:, 0:256], T.CL[:, :], T.ONE[:, :], "CL ONE", b, True, False)
+        for q, b in ((1, "b1"), (3, "b2"), (0, "b3"), (2, "b4")):
+            for h in (0, 1):
+                n = 2 * q + h
+                if h == 0:
+                    ts(T.LQ[:, 128 * n:128 * n + 128], T.IND[:, :], T.HI[:, q:q + 1], ALU.mult, "IND HI HI2", "LQ%d" % n)
+                else:
+                    act(T.LQ[:, 128 * n:128 * n + 128], T.IND[:, :], AF.Copy, "IND LO", "LQ%d" % n, T.LO[:, q:q + 1])
+                mm(T[b][:, 0:256], T.LQ[:, 128 * n:128 * n + 128], T.RH[:, :], "LQ%d RH" % n, b, q < 2 and h == 0, h == 1)
+        act(T.ZG[:, :], win.indirect(T.OZ[:, 192:224]), AF.Copy, "OZ " + bankk, "ZG")
+        for w, r, o, bn, bs in (("V1", "RB", "OY", "b1", "b2"), ("W1", "RA", "OX", "b3", "b4")):
+            tt(T[w][:, :], T[bn][:, 0:256], T[r][:, c], ALU.mult, bn + " " + r + k, w)
+            tt(T[w][:, :], T[w][:, :], T[bs][:, 0:256], ALU.add, w + " " + bs, w)
+            ts(T[o][:, :], T[w][:, :], M1, ALU.add, w, o, M1 - MID, ALU.subtract)
+
+    def build(t, h0, h1):
+        def y(q, dst="YG", lst="OY", a=0, n=1024):
+            o = 1024 * q + a
+            act(T[dst][:, o:o + n], win.indirect(T[lst][:, o // 16:(o + n) // 16]), AF.Copy, lst + " " + bankk, "%s%d%d" % (dst, q, a))
+
+        def x(q, a=0, n=1024):
+            o = slice(1024 * q + a, 1024 * q + a + n)
+            tt(T.FX[:, o], win.indirect(T.OX[:, 64 * q + a // 16:64 * q + (a + n) // 16]), T.YG[:, o], (ALU.min, ALU.max, None, ALU.add)[q], "OX YG%d%d " % (q, a) + bankk, "FX%d%d" % (q, a))
+
+        def both(q, b, o, lh):
+            k = (q, o - 1024 * q)
+            mm(T[b][:, :], T.DG[:, :], T.XG[:, o:o + 512], "DG XG%d%d" % k, b, True, False)
+            mm(T[b][:, :], T[lh][:, :], T.YG[:, o:o + 512], lh + " YG%d%d" % k, b, False, True)
+
+        def z(q, a=0, n=1024):
+            o = 1024 * q + a
+            tt(T.K[:, o:o + n], win.indirect(T.OZ[:, o // 16:(o + n) // 16]), T.FX[:, o:o + n], ALU.min, "OZ FX%d%d FX%d512 " % (q, a, q) + bankk, "K%d%d" % (q, a))
+
+        def sums(q, n=1024):
+            for b in range(32):
+                mm(T.b0[32 * q:32 * q + n // 32, b:512:32], T.K[:, 1024 * q + b:1024 * q + n:32], T.WCP[:, :], "WCP K%d0 K%d512" % (q, q), "b0")
+        y(0, n=512)
+        y(0, a=512, n=512)
+        y(1)
+        x(0, 0, 512)
+        x(0, 512, 512)
+        h0()
+        h1()
+        z(0)
+        sums(0)
+        for a, b in ((0, "b5"), (512, "b6")):
+            y(2, a=a, n=512)
+            y(2, "XG", "OX", a=a, n=512)
+            both(2, b, 2048 + a, "NDG")
+        x(1)
+        z(1)
+        y(3, a=512, n=512)
+        act(T.FX[:, 2048:2560], T.b5[:, :], AF.Abs, "b5", "FX20")
+        act(T.FX[:, 2560:3072], T.b6[:, :], AF.Abs, "b6", "FX2512")
+        sums(1)
+        x(3, 512, 512)
+        z(3, 512, 512)
+        if t:
+            sums(3)
+        y(3, n=512)
+        y(3, "XG", "OX", n=512)
+        both(3, "b7", 3072, "DG")
+        z(2)
+        sums(2)
+        tt(T.K[:, 3072:3584], T.b7[:, :], T.ZG[:, :], ALU.min, "b7 ZG", "K30")
+        sums(3, 512 if t else 1024)
+
+    def pick(t, h):
+        tt(T.Z1[:, :], T.b0[:, 0:256], T.MIDT[:, :], ALU.subtract, "b0 MIDT", "Z1")
+        act(T.b7[:, 0:256], T.Z1[:, :], AF.Abs, "Z1", "b7")
+        ts(T.OI[:, :], T.b0[:, 256:512], 2.0, ALU.mult, "b0", "OI", 1.0, ALU.add)
+        ts(T.OJ[:, :], T.OI[:, :], 15, ALU.bitwise_and, "OI", "OJ")
+        tt(T.b7[:, 256:512], T.b7[:, 0:256], T.HALF[:, :], ALU.is_le, "b7 HALF", "b7")
+        tt(T.OWN[:, :], T.OJ[:, :], T.b7[:, 256:512], ALU.mult, "OJ b7", "OWN")
+        act(T.OA[:, :], T.OWN[:, :], AF.Abs, "OWN CCg", "OA", 1.0, col["m15"])
+        act(T.O[:, 1792:2048], T.OA[:, :], AF.Relu, "OA CCh", "O7", -1.0, col["on1"])
+        for p in range(7):
+            ts(T.O[:, 256 * p:256 * p + 256], T.OWN[:, :], 2.0 * p + 1, ALU.is_equal, "OWN", "O%d" % p)
+        h()
+        for q in range(8):
+            mm(T.b6[:, SEG * q + 9:SEG * q + SEG], T.BID[:, :], T.OWN[:, 32 * q:32 * q + 32], "BID OWN", "b6")
+            mm(T.b6[:, SEG * q + 8:SEG * q + 9], T.BID[:, :], T.JC[:, :], "BID JC", "b6")
+        for b in range(32):
+            mm(T.b5[:, 0:64], T.TRI[:, :], T.O[:, b:2048:32], "TRI O0 O1 O2 O3 O4 O5 O6 O7", "b5", b == 0, b == 31)
+        for r in range(4):
+            ts(T.S4[:, 64 * r:64 * r + 64], T.b5[:, 0:64], -float(r), ALU.add, "b5", "S4%d" % r, 100.0, ALU.min)
+        for q in range(8):
+            mm(T.b6[:, SEG * q:SEG * q + 8], T.BID[:, :], T.S4[:, q:64:8], "BID S40", "b6")
+        act(T.Z[:, :], T.b6[:, 0:8 * SEG], AF.Copy, "b6", "Z")
+        for c in range(8):
+            ts(T.U[:, 256 * c:256 * c + 256], T.S4[:, :], 4.0 * c, ALU.is_le, "S40 S41 S42 S43", "U%d" % c)
+        for ch in (0, 1):
+            for lo, hi, b in ((0, 9, "b%d" % (3 + ch)), (9, SEG, "b%d" % (1 + ch))):
+                for q in range(8):
+                    mm(T[b][:, (hi - lo) * q:(hi - lo) * (q + 1)], T.U[:, 1024 * ch + q:1024 * ch + 1024:8], T.Z[:, SEG * q + lo:SEG * q + hi],
+                       "Z U%d U%d U%d U%d" % tuple(range(4 * ch, 4 * ch + 4)), b)
+        for ch in (0, 1):
+            d, b = slice(72 * ch, 72 * ch + 72), T["b%d" % (3 + ch)]
+            tt(T.SMM[:, d], b[:, 0:72], T.MSK[:, d], ALU.mult, "b%d MSK" % (3 + ch), "SMM%d" % ch)
+            act(T.R32[:, 8 * ch:8 * ch + 8], b[:, 8:72:9], AF.Copy, "b%d" % (3 + ch), "R32%d" % ch, 32.0, -2048.0)
+            if ch:
+                scan(T.SS[:, :], T.RSS[:, :], T.SMM[:, :], ALU.mult, ALU.add, "RSS SMM0 SMM1", "SS")
+            ts(T.EO[:, 256 * ch:256 * ch + 256], T["b%d" % (1 + ch)][:, 0:256], col["podd"], ALU.is_equal, "b%d CCo" % (1 + ch), "EO%d" % ch)
+        tt(T.EO[:, 0:512:32], T.EO[:, 0:512:32], T.SS[:, 8:144:9], ALU.add, "SS EO0 EO1", "EO0 EO1")
+        scan(T.CU[:, :], T.RS[:, :], T.EO[:, :], ALU.mult, ALU.add, "RS EO0 EO1", "CU")
+        ts(T.IN[:, 0:256], T.CU[:, 0:256], col["c16"], ALU.is_le, "CU CC", "IN0")
+        ts(T.IN[:, 256:512], T.CU[:, 256:512], col["c32"], ALU.is_le, "CU CC2", "IN1")
+        scan(T.C2[:, :], T.RS[:, :], T.IN[:, :], ALU.mult, ALU.add, "RS IN0 IN1", "C2")
+        tt(T.J16[:, :], T.C2[:, 31:512:32], T.R32[:, :], ALU.add, "C2 R320 R321", "J16")
+        do("V", lambda v: v.tensor_tensor(T.LJ[:, :], T.J16[:, :].indirect(T.OC[:, :]), T.MI[:, :], ALU.mult), "J16 OC MI", "LJ")
+        for ch in (0, 1):
+            mm(T.b5[:, ch:16:2], T.LJ[:, 128 * ch:128 * ch + 128], T.RP[:, :], "LJ RP", "b5")
+        ts(T.OFJ[:, :], T.b5[:, 0:16], 2048.0, ALU.add, "b5", "OFJ")
+        o = 256 * t
+        do("V", lambda v: v.tensor_copy(T.send[:, o:o + 256], T.K[:, 0:4112].indirect(T.OFJ[:, :])), "OFJ K00 K10 K20 K30 K3512 kinv", "snd%d" % t)
+        tr, k = [], 0
+        for p in range(NR):
+            if p == rank:
+                continue
+            dst = T.cores[p]
+            e = topo.engines(core, dst)
+            rid, pid, _se = topo.addr(dst)
+            tr.append(RemoteDMATransfer(dst_ids=[DstId(rid=rid, pnc=pid)], dma_engine_mask=(1 << e[2 * k]) | (1 << e[2 * k + 1]), remote_sem=T.sem["arr%d" % t],
+                                        srcs=[T.send[:, o + 32 * p:o + 32 * p + 32]], dsts=[T.land[:, o + 32 * rank:o + 32 * rank + 32]]))
+            k += 1
+        order("G", ["snd%d" % t], [])
+        g.remote_dma_fused(tr, local_sem=T.sem["sent%d" % t])
+        cp(T.land[:, o + 32 * rank:o + 32 * rank + 32], T.send[:, o + 32 * rank:o + 32 * rank + 32], "snd%d" % t, "lnd%d" % t)
+
+    def keep(t):
+        s, last = 4 + t, t == RO - 1
+        o, lk = 256 * t, "lnd%d" % t
+        lnd = T.land[:, o:o + 256]
+        ts(T.TC[:, 3:4], T.TC[:, 0:1], -1.0, ALU.add, "TC", "TB")
+        ts(T.WJ[:, :], T.JL[:, :], T.TC[:, 0:1], ALU.subtract, "JLx TC", "WJ", 4097.0, ALU.add)
+        wait("P", "arr%d" % t, 14)
+        mm(T.b3[:, 0:256], T.WBL[:, :], lnd, "WBL " + lk, "b3")
+        for i in range(16):
+            mm(T.b4[:, 0:16], T.LI[:, 128 * i:128 * i + 128], T.land[:, o + i:o + 256:16], "LI LI%d " % i + lk, "b4", i == 0, i == 15)
+        cp(T.OI[:, :], T.b3[:, 0:256], "b3", "OI")
+        ts(T.OJ[:, :], T.OI[:, :], 3, ALU.arith_shift_right, "OI", "OJ", 4095, ALU.bitwise_and)
+        cp(T.KLI[:, :], T.b4[:, 0:16], "b4", "KLI")
+        ts(T.KBH[:, :], T.OJ[:, :], -2048.0, ALU.add, "OJ", "KBH")
+        ts(T.KLJ[:, :], T.KLI[:, :], 3, ALU.arith_shift_right, "KLI", "KLJ", 4095, ALU.bitwise_and)
+        ts(T.INV[:, :], T.b4[:, 0:16], 0.0, ALU.is_lt, "b4", "INV", 4096.0, ALU.mult)
+        tt(T.BL[:, :], T.KLJ[:, :], T.INV[:, :], ALU.max, "KLJ INV", "BL")
+
+        def ed(a, b):
+            return " ".join("Ed%d" % m for m in range(a, b))
+
+        def later(a, b):
+            tt(T.E3[:, a:b, 0:16], T.E3[:, a:b, 0:16], T.DM[:, a:b, :], ALU.mult, ed(a, b) + " DM", ed(a, b))
+        for m in range(16):
+            ts(T.E3[:, m, 0:256 - 16 * m], T.KBH[:, 16 * m:256], 2048.0, ALU.add, "KBH BL", "E%d Ed%d" % (m, m), T.BL[:, m:m + 1], ALU.is_equal)
+            if m == 0:
+                cp(T.BU[:, :], T.BL[:, :], "BL", "BU")
+            if m == 1:
+                do("V", lambda v: v.tensor_copy(T.UG[:, :], T.USED[:, 0:4112].indirect(T.BU[:, :])), "USED USEDx BU", "UG")
+                mm(T.b6[:, 0:256], T.W0[:, :], T.UG[:, :], "W0 UG", "b6", True, False)
+            if m == NA + 1:
+                later(0, NA)
+        later(NA, 16)
+        for m in range(15):
+            mm(T.b6[:, 16 * m + 16:256], T.BON[:, :], T.E3[:, m, 16:256 - 16 * m], "BON E%d" % m, "b6", False, False)
+        mm(T.b6[:, 0:256], T.BON[:, :], T.E3[:, :, 0:16], "BON " + ed(0, 16), "b6", False, True)
+        ts(T.b7[:, 0:256], T.b6[:, 0:256], 0.5, ALU.is_lt, "b6", "b7")
+        scan(T.POS[:, :], T.ZERO[:, :], T.b7[:, 0:256], ALU.max, ALU.add, "ZERO b7", "POS")
+        n = T.POS[:, 255:256]
+        if not last:
+            tt(T.TC[:, 0:1], T.TC[:, 0:1], n, ALU.add, "TC POS", "TC")
+            ts(T.F4[:, s:32:8], T.ONEF[:, 0:4], n, ALU.mult, "ONEF POS", "F4")
+            cp(T.R8[:, 7 - s:8 - s], n, "POS", "R8")
+        tt(T.X[:, :], T.b7[:, 0:256], T.POS[:, :], ALU.mult, "b7 POS", "X")
+        if not last:
+            ts(T.TC[:, 1:2], T.TC[:, 0:1], 1.0 / 4096, ALU.mult, "TC", "TC1")
+        for i in range(16):
+            mm(T.b5[:, 0:16], T.LP[:, 128 * i:128 * i + 128], T.X[:, i:256:16], "LP LP%d X" % i, "b5", i == 0, i == 15)
+        app = (lambda: ts(T.ZT[:, :], T.b5[:, 0:16], 0.0, ALU.is_equal, "b5", "ZT"),
+               lambda: tt(T.D1[:, :], T.ZT[:, :], T.WJ[:, :], ALU.mult, "ZT WJ", "D1"),
+               lambda: tt(T.D1[:, :], T.D1[:, :], T.b5[:, 0:16], ALU.add, "D1 b5", "D1"),
+               lambda: ts(T.DU[:, :], T.D1[:, :], T.TC[:, 3:4], ALU.add, "D1 TB", "DU"),
+               lambda: do("V", lambda v: v.tensor_copy(T.bankS[:, 0:4352].indirect(T.DU[:, :]), lnd), lk + " DU", "bk bkz"))
+        if last:
+            for f in app:
+                f()
+        else:
+            prep(t + 1, app)
+
+    def mark(t):
+        tt(T.UJ[:, :], T.JL[:, :], T.BL[:, :], ALU.subtract, "JLx BL", "UJ")
+        ts(T.E1[:, :], T.UJ[:, :], 4112.0, ALU.add, "UJ", "E1")
+        tt(T.E1[:, :], T.E1[:, :], T.ZT[:, :], ALU.mult, "E1 ZT", "E1")
+        tt(T.E1[:, :], T.E1[:, :], T.BL[:, :], ALU.add, "E1 BL", "E1")
+        cp(T.EU[:, :], T.E1[:, :], "E1", "EU")
+        do("V", lambda v: v.tensor_copy(T.USED[:, 0:4368].indirect(T.EU[:, :]), T.ONEI[:, :]), "EU ONEI", "USED USEDx")
+
+    prep(0)
+    ts(T.CL[:, :], T.BON[:, :], col["cval"], ALU.mult, "BON CCv", "CL")
+    lists(0)
+
+    def h0():
+        cp(T.LMF[:, 0:2], T.LM[:, :], "LM", "LMF")
+        ms(T.ONEF[:, :], 1.0, "ONEF")
+        tt(T.LMF[:, 2:3], T.LMF[:, 0:1], T.LMF[:, 1:2], ALU.add, "LMF", "LMF2")
+        tt(T.LMF[:, 3:4], T.LMF[:, 1:2], T.LMF[:, 0:1], ALU.subtract, "LMF", "LMF3")
+        ts(T.NDG[:, :], T.DG[:, :], -1.0, ALU.mult, "DG", "NDG")
+        ts(T.LMF[:, 4:6], T.LMF[:, 2:4], 0.5, ALU.mult, "LMF2 LMF3", "LMF4")
+
+    def h1():
+        ts(T.WCP[:, 0:8], T.IR[:, 0:8], col["grp"], ALU.is_equal, "IR CC", "WCPa")
+        ts(T.WCP[:, 8:16], T.IR[:, 0:8], col["grp"], ALU.is_equal, "IR CC CCw WCPa", "WCP", col["wt"], ALU.mult)
+        for h in (0, 1):
+            ts(T.DM8[:, 256 * h:256 * h + 256], T.GB[0:8, :], CC[0:8, 0:1], ALU.is_equal, "GB CC LMF4", "DM8%d" % h, T.LMF[:, 4 + h:5 + h], ALU.mult)
+
+    def h2():
+        ms(T.RS[:, :], 1.0, "RS")
+        ms(T.RSS[:, :], 1.0, "RSS")
+        ms(T.ZERO[:, :], 0.0, "ZERO")
+        ms(T.RS[:, 0:512:32], 0.0, "RS")
+        ms(T.RSS[:, 0:144:9], 0.0, "RSS")
+        ms(T.K[:, 4096:4112], -32.0, "kinv")
+        cp(T.OC[:, :], T.IR[:, 0:16], "IR", "OC")
+        ts(T.MSK[:, :], T.I9[:, :], col["p8"], ALU.is_equal, "I9 CC", "MSK")
+        ts(T.MI[:, :], T.IF[:, :], col["c16"], ALU.is_equal, "IF CC", "MI")
+        ts(T.RP[:, :], T.IR[:, 0:8], col["p8"], ALU.is_equal, "IR CC", "RP")
+        ts(T.W0C[:, :], T.IR[:, 0:8], col["grp"], ALU.is_equal, "IR CC CCi", "W0C", col["i0"], ALU.mult)
+    build(0, h0, h1)
+    mm(T.b1[:, :], T.ONEF[0:8, :], T.DM8[:, :], "ONEF DM80 DM81", "b1")
+    act(T.MIDT[:, :], T.b1[:, 0:256], AF.Copy, "b1", "MIDT")
+    act(T.HALF[:, :], T.b1[:, 256:512], AF.Copy, "b1", "HALF")
+    pick(0, h2)
+    for i in range(16):
+        act(T.LI[:, 129 * i:128 * i + 128:16], T.WCP[:, 8:16], AF.Copy, "WCP LI", "LI%d" % i)
+    for i in range(16):
+        act(T.LP[:, 129 * i:128 * i + 128:16], T.W0C[:, :], AF.Copy, "W0C LP", "LP%d" % i)
+    ts(T.WBL[:, :], T.IG[:, :], col["grp"], ALU.is_equal, "IG CC CCw", "WBL", col["wt"], ALU.mult)
+    ts(T.W0[:, :], T.BON[:, :], col["i0"], ALU.mult, "BON CCi", "W0")
+    ts(T.DM[:, :, :], T.I16[:, :, :], col["i"], ALU.is_gt, "I16 CC", "DM")
+    ts(T.JL[:, :], T.JL[:, :], col["i"], ALU.add, "JL CC", "JLx")
+    masks(1)
+    cp(T.RCF[:, 256:1024], T.RC[:, 256:1024], "RC1", "RCF")
+    keep(0)
+    for t in range(1, RO):
+        lists(t)
+        build(t, lambda: None, lambda: None)
+        pick(t, lambda: masks(t + 1) if t + 1 < RO else None)
+        mark(t - 1)
+        keep(t)
+    dma("S", "out", T.y[:, :], T.bankS[:, B:4096], "bk bkz", "out")
+    for t in range(RO):
+        g.wait_ge(T.sem["sent%d" % t], 14)
+    for e in ("V", "A", "P", "G"):
+        g.wait_ge(T.sem["s" + e], cnt[e])
+    for n in _DMAS:
+        g.wait_ge(T.sem["d_" + n], 16)

@@ -1,38 +1,52 @@
+import math
 from concourse.bass import DstId, RemoteDMATransfer
 from concourse.mybir import dt, AluOpType as ALU, AxisListType as AX, ActivationFunctionType as AF
 
-B, J, CAP, RO, NR = 3072, 4096, 32, 4, 8
+B, CAP, RO, NR = 3072, 32, 4, 8
 M1 = 1.5 * 2.0 ** 23
-MN = 1.5 * 2.0 ** 16
-M256 = 1.5 * 2.0 ** 15
+M7 = 1.5 * 2.0 ** 16
+M8 = 1.5 * 2.0 ** 26
 M32 = 1.5 * 2.0 ** 28
 M4096 = 1.5 * 2.0 ** 35
 MID = 1920
-NA = 12
-SEG = 41
+MARK = 74.5
+HALF = -0.5 + 2.0 ** -13
+MODE = "aaca"
+LAG = 14000
+PASSES = 1
+ORDER = (0, 1, 3, 2)
+CUT = (2, 1, 1, 1)
 f32, bf, i32, u16, f16 = "float32", "bfloat16", "int32", "uint16", "float16"
 
 SCRATCH = {}
-for _d, _l in (
-    (bf, "bankS 4352,K 4112,YG 4096,FX 4096,XG 4096,ZG 512,ONE 256,ZERO 256,TRI 128,BID 128,DG 128,NDG 128,WCP 16,W0C 8,WBL 128,BON 128,W0 128,LI 2048,LP 2048,"
-         "COLT 256,CL 128,DM 16 16,RS 512,RSS 144,MSK 144,MI 256,JC 1,RH 256,IND 128,LQ 1024,OWN 256,O 2048,S4 256,U 2048,Z 328,EO 512,CU 512,IN 512,C2 512,SMM 144,SS 144,UG 256,"
-         "E3 16 272,POS 256,X 256,send 1024,land 1024"),
-    (i32, "USED 4368,RA 1024,RB 1024,RC 1024,PID 1,TI 8,ONEI 256,OI 256,OJ 256,KLI 16,KLJ 16"),
-    (f32, "CC 32,IR 256,IG 128,II 128,GB 256,I16 16 16,IF 256,I9 144,JL 16,ONEF 128,MK 8,MD 8,MS 8,MQ 128,RQ 32,NEGM 8,IT 128,MIDT 256,HALF 256,F4 32,R8 8,TC 8,PP 8,PR 8,"
-          "SEL 16,SM 8,CS 16,DQ 32,DS 32,HI 4,LO 4,RCF 1024,OA 256,W1 256,V1 256,Z1 256,J16 16,R32 16,INV 16,BL 16,ZT 16,WJ 16,D1 16,UJ 16,E1 16"),
-    (u16, "OX 256,OY 256,OZ 256,OFJ 16,BU 16,DU 16,EU 16,OC 16"),
-    (f16, "RP 8,LJ 256,KBH 256"),
-):
-    for _x in _l.split(","):
-        _x = _x.split()
-        SCRATCH[_x[0]] = ("sbuf", [128] + [int(v) for v in _x[1:]], _d)
-SCRATCH.update({"NL": ("sbuf", [8, 4], i32), "LM": ("sbuf", [8, 2], i32), "NLF": ("sbuf", [8, 4], f32), "LMF": ("sbuf", [8, 8], f32),
-                "SL8": ("sbuf", [8, 128], f32), "DM8": ("sbuf", [8, 512], f32)})
+_SET = (
+    (bf, "bank 4096,K 4112,XG 2048,YG 2048,ZG 2048,FX 2048,V 128,IND 128,DS 256,O 32 32,S4 128,U 32 32,Z 164,EC 256,WN 528,RJ 192,"
+         "send 1024,land 1024,LF 256,E 9 256,PK 2 256,USED 4224"),
+    (i32, "R 3 1024,WI 1"),
+    (f32, "F 8,ST 4 6,UP 4 6,CS 24,W 384,SM 8 16"),
+    (u16, "OF 384,OS 4 16"),
+    (f16, "KB 256"),
+)
+_ALL = (
+    (bf, "ONE 512,MX 15 128,WCP 24,LP 144,MI 176,MH 176,RPM 192,"
+         "LI 144,RS32 256,ZERO 32,PRE 768,GB 128,RI 512,LC 128,LY 128,LN 128,NTH 256,UB 256"),
+    (i32, "PID 1,TI 12,NL 4,LM 2,UC 256"),
+    (f32, "CC 48,IR 256,IG 128,IL 128,I64 128,IA 28,IB 28,EQ 6 28,MQ 7 16,T5 160,BS 32,RS5 80,HI 32,KA 16,KC 16,KT 2 16,KN 2 16,W16 16,PB 32,RS4 32,POW 32,Q25 32,"
+          "NLF 4,SL 128,LMF 8,WJ 16,ND 8,I8 192,OCF 12"),
+    (u16, "OC 12"),
+)
+for _names, _tab in ((("0", "1"), _SET), (("",), _ALL)):
+    for _d, _l in _tab:
+        for _x in _l.split(","):
+            _x = _x.split()
+            for _s in _names:
+                SCRATCH[_x[0] + _s] = ("sbuf", [128] + [int(v) for v in _x[1:]], _d)
 for _k in range(8):
     SCRATCH["b%d" % _k] = ("psum", [128, 512], f32)
-_DMAS = ["ncl", "lim", "bank", "ra0", "rb0", "rc0", "ra1", "rb1", "rc1", "used", "out"]
-SEMAPHORES = ["sV", "sA", "sP", "sG"] + ["d_" + n for n in _DMAS] + ["arr%d" % t for t in range(RO)] + ["sent%d" % t for t in range(RO)]
+_DMAS = ["ncl", "lim", "uc"] + [n + s for s in "01" for n in ("bank", "ra", "rb", "rc", "rl", "used", "out")]
+SEMAPHORES = ["sV", "sA", "sP", "sG"] + ["d_" + n for n in _DMAS] + [n + "%d%d" % (s, t) for n in ("arr", "sent") for s in (0, 1) for t in range(RO)]
 BANKS = tuple("b%d" % k for k in range(8))
+HOP, GATHER, SCATTER, PE, FLIGHT = 240, 1.56, 3.8, 0.54, 5700
 
 
 def rank_program(g, core, T, topo):
@@ -40,462 +54,558 @@ def rank_program(g, core, T, topo):
     if rank is None:
         return
     eng = {"V": g.vector, "A": g.scalar, "P": g.tensor, "G": g, "S": g.sync}
-    cnt = {"V": 0, "A": 0, "P": 0, "G": 0}
-    seen = {e: {} for e in eng}
-    lastw, readers = {}, {}
+    ops, lastw, readers, S = [], {}, {}, [0]
 
-    def wait(e, sem, val):
-        if seen[e].get(sem, 0) < val:
-            eng[e].wait_ge(T.sem[sem], val)
-            seen[e][sem] = val
+    share = {"UG": "DS", "RR": "W", "OW": "IND", "CU": "LF"}
+    DG, NDG, D512, D4, D8, TRI, BID, BON, FOLD, W8, BW, B4, W04, COLT, IT = [T.MX[:, k, :] for k in range(15)]
 
-    def order(e, r, w):
-        req = {}
-        me = "s" + e
+    def keys(s):
+        return ["b%d" % (4 * S[0] + "abcd".index(k)) if k in ("a", "b", "c", "d") else share.get(k[:-1], k[:-1]) + k[-1].replace("@", str(S[0])) for k in s.split()]
 
-        def add(ev):
-            if ev is not None:
-                req[ev[0]] = max(req.get(ev[0], 0), ev[1])
+    def do(e, call, r, w, c, lat=0, sem=None):
+        r, w, dep = keys(r), keys(w), {}
         for k in r:
-            add(lastw.get(k))
-        for k in list(w) + [k for k in r if k in BANKS]:
-            add(lastw.get(k))
-            for ev in readers.get(k, {}).items():
-                if ev[0] != me:
-                    add(ev)
-        if e == "P":
-            req.pop("sP", None)
-        for sem in sorted(req):
-            wait(e, sem, req[sem])
-
-    def note(ev, r, w):
+            for d in lastw.get(k, ()):
+                dep[d] = True
+        for k in w + [k for k in r if k in BANKS]:
+            for d in lastw.get(k, ()):
+                dep[d] = True
+            for d in readers.get(k, ()):
+                if ops[d][0] != e or k in w:
+                    dep[d] = True
+        n = len(ops)
+        ops.append((e, call, dep, c, lat, sem))
         for k in r:
-            readers.setdefault(k, {})[ev[0]] = ev[1]
+            readers.setdefault(k, []).append(n)
         for k in w:
-            lastw[k] = ev
-            readers[k] = {}
+            lastw[k], readers[k] = [n], []
+        return n
 
-    def do(e, call, r, w):
-        r, w = r.split(), w.split()
-        order(e, r, w)
-        cnt[e] += 1
-        call(eng[e]).then_inc(T.sem["s" + e], 1)
-        note(("s" + e, cnt[e]), r, w)
+    def X(name):
+        return T[share.get(name, name) + str(S[0])]
 
-    def dma(e, name, out, in_, r, w):
-        r, w = r.split(), w.split()
-        order(e, r, w)
-        eng[e].dma_start(out, in_).then_inc(T.sem["d_" + name], 16)
-        note(("d_" + name, 16), r, w)
+    def bank(k):
+        return T["b%d" % (4 * S[0] + "abcd".index(k))]
 
-    def ts(out, in0, s1, op0, r, w, s2=None, op1=None):
+    def dma(name, pairs, r, w, c=2500):
+        do("S", lambda q: [q.dma_start(o, i).then_inc(T.sem["d_" + name], 16) for o, i in pairs], r, w, 60 * len(pairs), c, ("d_" + name, 16 * len(pairs)))
+
+    def ts(out, in0, s1, op0, r, w, s2=None, op1=None, c=64):
         if op1 is None:
-            do("V", lambda v: v.tensor_scalar(out, in0, s1, None, op0), r, w)
+            do("V", lambda v: v.tensor_scalar(out, in0, s1, None, op0), r, w, c)
         else:
-            do("V", lambda v: v.tensor_scalar(out, in0, s1, s2, op0, op1), r, w)
+            do("V", lambda v: v.tensor_scalar(out, in0, s1, s2, op0, op1), r, w, c)
 
-    def tt(out, a, b, op, r, w):
-        do("V", lambda v: v.tensor_tensor(out, a, b, op), r, w)
+    def tt(out, a, b, op, r, w, c=64):
+        do("V", lambda v: v.tensor_tensor(out, a, b, op), r, w, c)
 
-    def cp(out, a, r, w):
-        do("V", lambda v: v.tensor_copy(out, a), r, w)
+    def cp(out, a, r, w, c=64):
+        do("V", lambda v: v.tensor_copy(out, a), r, w, c)
 
-    def ms(ap, c, w):
-        do("V", lambda v: v.memset(ap, c), "", w)
+    def ms(ap, x, w, c=64):
+        do("V", lambda v: v.memset(ap, x), "", w, c)
 
-    def mm(out, l, rh, r, w, start=True, stop=True):
-        do("P", lambda p: p.matmul(out, l, rh, start, stop), r, w)
+    def mm(out, l, rh, r, w, start=True, stop=True, c=64):
+        do("P", lambda p: p.matmul(out, l, rh, start, stop), r, w, c * PE)
 
-    def act(out, a, fn, r, w, scale=1.0, bias=0.0):
-        do("A", lambda s: s.activation(out, a, fn, bias=bias, scale=scale), r, w)
+    def act(out, a, fn, r, w, scale=1.0, bias=0.0, c=64):
+        do("A", lambda s: s.activation(out, a, fn, bias=bias, scale=scale), r, w, c)
 
-    def iota(ap, pat, cm, w, base=0):
-        do("G", lambda q: q.iota(ap, pat, base, cm, allow_small_or_imprecise_dtypes=True), "", w)
+    def lin(e, out, a, scale, bias, r, w, c=64):
+        if e == "V":
+            ts(out, a, scale, ALU.mult, r, w, bias, ALU.add, c)
+        else:
+            act(out, a, AF.Identity, r, w, scale, bias, c)
 
-    def scan(out, d0, d1, op0, op1, r, w):
-        do("V", lambda v: v.tensor_tensor_scan(out, d0, d1, 0.0, op0, op1), r, w)
+    def iota(ap, pat, w, cm=0, base=0):
+        do("G", lambda q: q.iota(ap, pat, base, cm, allow_small_or_imprecise_dtypes=True), "", w, 160 + 2 * math.prod(p[1] for p in pat))
 
-    dma("S", "ncl", T.NL[:, :], T.ncl[:, :], "", "NL")
-    dma("S", "lim", T.LM[:, :], T.lim[:, :], "", "LM")
-    dma("A", "rb0", T.RB[:, 0:256], T.rb[:, 0:256], "", "RB0")
-    dma("A", "ra0", T.RA[:, 0:256], T.ra[:, 0:256], "", "RA0")
-    dma("A", "rc0", T.RC[:, 0:256], T.rc[:, 0:256], "", "RC0")
-    dma("S", "bank", T.bankS[:, 0:B], T.bank[:, :], "", "bk")
-    iota(T.PID[:, :], [[1, 1]], 1, "PID")
-    iota(T.IG[:, :], [[1, 8], [0, 16]], 0, "IG")
-    iota(T.II[:, :], [[0, 8], [1, 16]], 0, "II")
-    iota(T.IR[:, :], [[1, 256]], 0, "IR")
-    ms(T.ONE[:, :], 1.0, "ONE")
-    for n in ("b", "a", "c"):
-        dma("S", "r%s1" % n, T["R" + n.upper()][:, 256:1024], T["r" + n][:, 256:1024], "", "R%s1" % n.upper())
-    do("G", lambda q: q.affine_select(T.DG[:, :], T.ONE[:, 0:128], [[1, 128]], ALU.is_equal, 0.0, 0, -1), "ONE", "DG")
-    iota(T.bankS[:, B:4096], [[0, 1024]], 0, "bkz")
-    iota(T.GB[:, :], [[1, 8], [0, 32]], 0, "GB")
-    do("G", lambda q: q.affine_select(T.TRI[:, :], T.ONE[:, 0:128], [[1, 128]], ALU.is_gt, 0.0, 0, -1), "ONE", "TRI")
-    do("G", lambda q: q.affine_select(T.BID[:, :], T.DG[:, :], [[1, 128]], ALU.not_equal, -1.0, -1, -1), "DG", "BID")
-    iota(T.IF[:, :], [[0, 16], [1, 16]], 0, "IF")
-    iota(T.I9[:, :], [[0, 16], [1, 9]], 0, "I9")
-    iota(T.I16[:, :, :], [[0, 16], [1, 16]], 0, "I16")
-    iota(T.JL[:, :], [[16, 16]], 0, "JL")
-    iota(T.LI[:, :], [[0, 2048]], 0, "LI")
-    iota(T.LP[:, :], [[0, 2048]], 0, "LP")
-    iota(T.USED[:, 0:4096], [[0, 4096]], 0, "USED")
-    iota(T.USED[:, 4096:4112], [[0, 16]], 0, "USEDx", 1)
-    iota(T.ONEI[:, :], [[0, 256]], 0, "ONEI", 1)
-    dma("S", "used", T.USED[0:128:16, 0:4096], T.used[:, :], "", "USED")
+    def scan(out, d0, d1, op0, op1, r, w, c=64, init=0.0):
+        do("V", lambda v: v.tensor_tensor_scan(out, d0, d1, init, op0, op1), r, w, c)
+
+    EQ, MUL, ADD, SUB = ALU.is_equal, ALU.mult, ALU.add, ALU.subtract
+
+    dma("ncl", [(T.NL[0:8, :], T.ncl[:, :])], "", "NL")
+    for s in (0, 1):
+        S[0] = s
+        rows = slice(64 * s, 64 * s + 64)
+        for k, n in ((1, "rb"), (0, "ra"), (2, "rc")):
+            dma(n + str(s), [(X("R")[0:64, k, 0:256], T[n][rows, 0:256]), (X("R")[64:128, k, 0:255], T[n][rows, 1:256])], "", "R%d0@" % k)
+            if n == "rb":
+                dma("bank%d" % s, [(X("bank")[64 * h:64 * h + 64, 0:B], T.bank[rows, :]) for h in (0, 1)], "", "bk@", 4500)
+        if s == 0:
+            dma("lim", [(T.LM[8 * h:8 * h + 8, :], T.lim[:, :]) for h in (0, 1)], "", "LM")
+    for s in (0, 1):
+        S[0] = s
+        rows = slice(64 * s, 64 * s + 64)
+        dma("rl%d" % s, [(X("R")[64 * h:64 * h + 64, k, 256:1024 - h], T[n][rows, 256 + h:1024]) for k, n in enumerate(("ra", "rb", "rc")) for h in (0, 1)], "bk1", "R01@ R11@ R21@", 6000)
+    dma("uc", [(T.UC[:, :], T.used[:, :])], "bk1", "UC")
+    cp(T.UB[:, :], T.UC[:, :], "UC", "UB", 256)
+
+    iota(T.PID[:, :], [[1, 1]], "PID", 1)
+    iota(T.IR[:, :], [[1, 256]], "IR")
+    iota(T.IA[:, :], [[1, 7], [0, 4]], "IA")
+    iota(T.IB[:, :], [[-1, 7], [1, 4]], "IB", 0, 3)
+    iota(T.IG[:, :], [[0, 2], [1, 4], [0, 16]], "IG")
+    iota(T.KA[:, :], [[0, 4], [1, 4]], "KA")
+    iota(T.KC[:, :], [[1, 4], [-1, 4]], "KC", 0, 3)
+    iota(T.IL[:, :], [[16, 2], [0, 4], [1, 16]], "IL")
+    iota(T.I64[:, :], [[0, 2], [1, 64]], "I64")
+    iota(T.GB[0:16, :], [[1, 4], [0, 32]], "GB")
+    iota(T.I8[:, :], [[0, 24], [1, 8]], "I8")
+    iota(T.OCF[:, :], [[0, 3], [1, 4]], "OCF")
+    iota(T.WJ[:, :], [[16, 16]], "WJ0", 0, -256)
+    iota(T.ND[:, :], [[-16, 8]], "ND0", 0, -2048)
+    iota(T.ZERO[:, :], [[0, 32]], "ZERO")
+    ms(T.ONE[:, :], 1.0, "ONE", 256)
+    do("G", lambda q: q.affine_select(DG, T.ONE[:, 0:128], [[1, 128]], EQ, 0.0, 0, -1), "ONE", "DG", 460)
+    do("G", lambda q: q.affine_select(TRI, T.ONE[:, 0:128], [[1, 128]], ALU.is_gt, 0.0, 0, -1), "ONE", "TRI", 460)
+    do("G", lambda q: q.affine_select(BID, DG, [[1, 128]], ALU.not_equal, -1.0, -1, -1), "DG", "BID", 460)
+    for s in (0, 1):
+        S[0] = s
+        for a in range(0, 4096, 1024):
+            iota(X("K")[:, a:a + 1024:2], [[0, 512]], "Kz%d@" % a)
+        iota(X("K")[:, 4096:4112], [[0, 16]], "Ke@")
+        for a in range(0, 4224, 528):
+            iota(X("USED")[:, a:a + 528], [[0, 528]], "Uz%d@" % a)
+        dma("used%d" % s, [(X("USED")[64 * h:64 * h + 64:16, 0:4096], T.UB[64 * s:64 * s + 64, :]) for h in (0, 1)], "UB", " ".join("Uz%d@" % a for a in range(0, 4224, 528)) + " US@")
+        iota(X("bank")[:, B + 256:B + 640], [[0, 384]], "bz1@")
+        iota(X("bank")[:, B + 640:4096], [[0, 384]], "bz2@")
 
     CC = T.CC
-    col = {n: CC[:, k:k + 1] for k, n in enumerate(
-        ["pid", "i", "m", "typ", "grp", "p8", "c16", "wt", "podd", "sgs", "msg", "off", "tm1", "cval", "i0",
-         "mm1", "sm0", "sm1", "sm2", "sm3", "t0", "t1", "c32", "m15", "on1"])}
-    for k, (sh, an) in enumerate([(0, 255), (0, 15), (1, 7), (0, 1), (4, 7), (0, 7), (3, 15)]):
+    names = ["pid", "i", "m", "typ", "g", "h", "p8", "c32", "p64", "p4", "q8", "b3", "wt", "w8", "l", "sg", "off", "nsg", "sg4", "tm", "i0", "n7", "h1", "hs", "pv0", "pv1", "lpc", "mic",
+             "pw", "mk", "cP", "t0", "t1", "G8", "pt", "pts", "r0", "hc", "G0", "G1", "lic"]
+    col = {n: CC[:, k:k + 1] for k, n in enumerate(names)}
+    for k, (sh, an) in enumerate([(0, 255), (0, 15), (1, 7), (0, 1), (4, 3), (6, 1), (0, 7), (0, 31), (0, 63), (5, 3), (4, 7), (3, 1)]):
         ts(T.TI[:, k:k + 1], T.PID[:, :], sh, ALU.arith_shift_right, "PID", "TI%d" % k, an, ALU.bitwise_and)
-    cp(CC[:, 0:7], T.TI[:, 0:7], "TI0 TI1 TI2 TI3 TI4 TI5 TI6", "CC")
-    for n, src, a, b, key in (("tm1", "typ", 1.0 / 256, -1.0 / 256, "CCt"), ("sm0", "m", -1.0, 3.0, "CCx0"), ("mm1", "m", 1.0, -1.0, "CCn"), ("msg", "typ", -2.0, 1.0, "CCm"),
-                              ("off", "typ", -1.0, 1.0, "CCf"), ("wt", "i", 14.0, 9.0, "CCw"), ("sm1", "m", -1.0, 4.0, "CCx1"), ("sm2", "m", -1.0, 5.0, "CCx2"),
-                              ("sm3", "m", -1.0, 6.0, "CCx3"), ("podd", "p8", 2.0, 1.0, "CCo"), ("c32", "c16", 1.0, 16.0, "CC2"),
-                              ("m15", "pid", 0.0, -15.0, "CCg"), ("on1", "pid", 0.0, 1.0, "CCh")):
-        act(col[n], col[src], AF.Copy, "CC", key, a, b)
-        if n == "mm1":
-            act(T.COLT[:, :], T.IR[:, :], AF.Identity, "IR CCt", "COLT", 1.0 / 256, col["tm1"])
-    act(T.JC[:, :], col["pid"], AF.Copy, "CC", "JC")
-    ts(col["sgs"], col["typ"], 2.0 / 4096, ALU.mult, "CC", "CCs", -1.0 / 4096, ALU.add)
-    ts(T.BON[:, :], T.IG[:, :], col["grp"], ALU.is_equal, "IG CC", "BON")
-    ts(T.SL8[:, :], T.IG[0:8, :], CC[0:8, 0:1], ALU.is_equal, "IG CC", "SL8")
-    ts(T.IT[:, :], T.II[:, :], col["sgs"], ALU.mult, "II CCs", "IT", 9999.0 / 4096, ALU.add)
-    ts(T.MK[:, :], T.IR[:, 0:8], col["m"], ALU.is_equal, "IR CC", "MK")
-    ts(col["i0"], col["i"], 0.0, ALU.is_equal, "CC", "CCi")
-    tt(T.IT[:, :], T.IT[:, :], T.BON[:, :], ALU.mult, "IT BON", "IT")
-    ts(T.MS[:, :], T.IR[:, 0:8], col["mm1"], ALU.is_equal, "IR CCn", "MS")
-    ms(T.RQ[:, :], 1.0, "RQ")
-    ts(T.IT[:, :], T.IT[:, :], -9999.0 / 4096, ALU.add, "IT", "IT")
-    ms(T.RQ[:, 0:32:8], 0.0, "RQ")
-    tt(T.MD[:, :], T.MK[:, :], T.MS[:, :], ALU.subtract, "MK MS", "MD")
-    cp(T.NLF[:, :], T.NL[:, :], "NL", "NLF")
-    for b in ("b0", "b7"):
-        mm(T[b][:, 0:4], T.SL8[:, :], T.NLF[:, :], "SL8 NLF", b)
+    cp(CC[:, 0:6], T.TI[:, 0:6], " ".join("TI%d" % k for k in range(6)), "CC")
+    cp(CC[:, 6:12], T.TI[:, 6:12], " ".join("TI%d" % k for k in range(6, 12)), "CD cp4 cb3")
 
-    def masks(t):
-        q, s = 32 * t, 4 + t
-        ts(T.PR[:, :], T.IR[:, 0:8], col["sm%d" % t], ALU.is_equal, "IR CCx%d" % t, "PR")
-        ts(T.DS[:, 0:8], T.IR[:, 0:8], 1.0, ALU.subtract, "IR CCx%d" % t, "DS", col["sm%d" % t], ALU.is_equal)
-        ts(T.DS[:, 24:32], T.IR[:, 0:8], float(s - 1), ALU.is_le, "IR", "DSd")
-        ts(T.MQ[:, q:q + 8], T.MD[:, :], 1.0 / 4096, ALU.mult, "MD", "MQ%d" % t)
-        tt(T.DS[:, 8:16], T.PR[:, :], T.DS[:, 0:8], ALU.subtract, "PR DS", "DSb")
-        ts(T.DQ[:, 0:8], T.DS[:, 24:32], T.MK[:, 0:1], ALU.mult, "DSd MK", "DQ")
-        cp(T.MQ[:, q + 16:q + 24], T.MS[:, :], "MS", "MQ%da" % t)
-        ts(T.MQ[:, q + 8:q + 16], T.DS[:, 8:16], 1.0 / 4096, ALU.mult, "DSb", "MQ%db" % t)
-        tt(T.MQ[:, q + 24:q + 32], T.DQ[:, 0:8], T.PR[:, :], ALU.subtract, "DQ PR", "MQ%dc" % t)
-    masks(0)
-    ms(T.F4[:, :], 0.0, "F4")
-    ms(T.R8[:, :], 0.0, "R8")
-    ms(T.SEL[:, :], 0.0, "SEL")
-    for k in range(4):
-        cp(T.F4[:, 8 * k:8 * k + 4], T.b0[:, 0:4], "b0 F4", "F4%d" % k)
-        act(T.R8[:, 7 - k:8 - k], T.b7[:, k:k + 1], AF.Copy, "b7 R8", "R8%d" % k)
-    ms(T.NEGM[:, :], -M4096, "NEGM")
-    ts(col["t0"], col["i"], 1.0, ALU.is_equal, "CC", "CC0", 2.0 ** -13, ALU.mult)
-    ts(col["t1"], col["i"], 2.0, ALU.is_equal, "CC", "CC1", -float(MID), ALU.mult)
-    ms(T.TC[:, 0:1], float(B), "TC")
-    ts(col["cval"], col["i0"], -0.5, ALU.mult, "CCi CC0", "CCv", col["t0"], ALU.add)
-    ms(T.TC[:, 1:2], B / 4096.0, "TC1")
-    tt(col["cval"], col["cval"], col["t1"], ALU.add, "CCv CC1", "CCv")
-
-    bankk = "bk bkz"
-    win = T.bankS[:, 0:4096]
-    c0 = -(MID + 0.5) + 2.0 ** -13
-    F4k, R8k = "F4 F40 F41 F42 F43", "R8 R80 R81 R82 R83"
-
-    def prep(t, app=()):
-        app = list(app) + [lambda: None] * (5 - len(app))
-        s = 4 + t
-        CS, SEL = T.CS, T.SEL
-        ct = SEL[:, s:s + 1]
-        c = slice(256 * t, 256 * t + 256)
-        tt(T.DQ[:, :], T.F4[:, :], T.MQ[:, 32 * t:32 * t + 32], ALU.mult, F4k + " MQ%d MQ%da MQ%db MQ%dc" % (t, t, t, t), "DQ")
-        tt(T.PP[:, 0:s], T.F4[:, 0:s], T.R8[:, 8 - s:8], ALU.mult, F4k + " " + R8k, "PP")
-        scan(T.DS[:, :], T.RQ[:, :], T.DQ[:, :], ALU.mult, ALU.add, "RQ DQ", "DS")
-        ts(T.PR[:, 0:s], T.PP[:, 0:s], -2047.5, ALU.add, "PP", "PR", M4096, ALU.add)
-        scan(SEL[:, 1:s + 1], T.PR[:, 0:s], T.NEGM[:, 0:s], ALU.add, ALU.add, "PR NEGM", "SEL")
-        ts(T.HI[:, 0:2], T.DS[:, 7:16:8], MN, ALU.add, "DS", "HI", MN, ALU.subtract)
-        tt(T.SM[:, :], SEL[:, 0:8], T.MK[:, :], ALU.mult, "SEL MK", "SM")
-        do("V", lambda v: v.reciprocal(CS[:, 1:2], ct), "SEL", "CS1")
-        do("V", lambda v: v.tensor_reduce(CS[:, 2:3], T.SM[:, :], AX.X, ALU.add), "SM", "CS2")
-        ts(T.HI[:, 2:4], T.DS[:, 23:32:8], M32, ALU.add, "DS", "HI2", M32, ALU.subtract)
-        app[0]()
-        ts(CS[:, 3:4], CS[:, 2:3], CS[:, 1:2], ALU.mult, "CS1 CS2", "CS3", -0.46875 / 256, ALU.add)
-        app[1]()
-        tt(T.LO[:, :], T.DS[:, 7:32:8], T.HI[:, :], ALU.subtract, "DS HI HI2", "LO")
-        ts(CS[:, 4:5], CS[:, 3:4], M256, ALU.add, "CS3", "CS4", M256, ALU.subtract)
-        if t:
-            act(T.Z1[:, :], T.RCF[:, c], AF.Copy, "RCF TC1", "Z1", T.TC[:, 1:2], c0)
+    def cl(n, src, a, b, e="A"):
+        if e == "A":
+            act(col[n], col[src], AF.Copy, "CC c" + src, "c" + n, a, b)
         else:
-            ts(T.Z1[:, :], T.RC[:, c], T.TC[:, 1:2], ALU.mult, "RC0 TC1", "Z1", c0, ALU.add)
-        app[2]()
-        ts(CS[:, 5:6], CS[:, 4:5], ct, ALU.mult, "SEL CS2 CS4", "CS5", CS[:, 2:3], ALU.subtract)
-        app[3]()
-        ts(T.OZ[:, :], T.Z1[:, :], M1, ALU.add, "Z1", "OZ", M1 - MID, ALU.subtract)
-        ts(CS[:, 6:7], CS[:, 5:6], col["msg"], ALU.mult, "CS5 CCm CCf", "CS6", col["off"], ALU.add)
-        app[4]()
+            ts(col[n], col[src], a, MUL, "CC c" + src, "c" + n, b, ADD)
+    for x in (("wt", "i", 14.0, 9.0), ("w8", "i", 14 / 8, 9 / 8), ("sg", "typ", 2.0, -1.0), ("off", "typ", 2.0 ** -12, -2.0 ** -12), ("nsg", "typ", -2.0, 1.0),
+              ("sg4", "typ", 2.0 / 4096, -1.0 / 4096), ("tm", "typ", 1.0 / 128, -1.0 / 128), ("h1", "h", -1.0, 1.0), ("hs", "h", -2.0, 1.0), ("pv0", "p4", 1.0, -3.875),
+              ("pv1", "p4", 1.0, 0.125), ("mic", "i", 1.0, 48.0), ("hc", "b3", 4.0, 0.0), ("lic", "g", 16.0, 15.0)):
+        cl(*x)
+    lin("A", col["l"], col["h"], 16.0, col["i"], "CC", "cl")
+    ts(col["i0"], col["i"], 0.0, EQ, "CC", "ci0")
+    ts(col["n7"], col["m"], 7.0, ALU.not_equal, "CC", "cn7")
+    ts(col["t0"], col["m"], 0.0, ALU.not_equal, "CC cn7", "ct0", col["n7"], MUL)
+    cl("cP", "t0", 256.0, -256.0)
+    ts(BON, T.IG[:, :], col["g"], EQ, "IG CC", "BON", c=128)
+    ts(T.IL[:, :], T.IL[:, :], col["sg4"], MUL, "IL csg4", "ITF", 1.0, ADD, 128)
+    tt(T.IL[:, :], T.IL[:, :], BON, MUL, "ITF BON", "ITF", 256)
+    ts(IT, T.IL[:, :], -1.0, ADD, "ITF", "IT", c=128)
+    act(COLT, T.IR[:, 0:128], AF.Identity, "IR ctm", "COLT", 1.0 / 128, col["tm"], 128)
+    ms(T.RI[0:3, 0:256], 0.0, "RIa", 128)
+    ms(T.RI[0:3, 256:512], 1.0, "RI", 128)
+    for n, x in ((3, 2.0 ** -13), (2, -float(MID)), (1, -0.5)):
+        ms(T.LC[0:n, :], x, "LC")
+    for n, x in ((2, 0.5 - rank / 8), (1, -2048.0)):
+        ms(T.LY[0:n, :], x, "LY")
+    ms(T.LN[0:1, :], -512.0, "LN")
+    m, E6, MQ = col["m"], T.EQ, T.MQ
+    ts(E6[:, 0, :], T.IA[:, :], m, EQ, "IA CC", "E0")
+    ts(E6[:, 1, :], T.IA[:, :], 1.0, ADD, "IA CC", "E1", m, EQ)
+    ts(E6[:, 2, :], T.IB[:, :], m, EQ, "IB CC", "E2")
+    ts(E6[:, 3, :], T.IB[:, :], 1.0, ADD, "IB CC", "E3", m, EQ)
+    ts(E6[:, 3, :], E6[:, 3, :], m, MUL, "E3 CC", "E3", 0.0, ALU.is_gt)
+    tt(E6[:, 4, :], T.IA[:, :], T.IB[:, :], ADD, "IA IB", "E4")
+    ts(E6[:, 5, :], T.IB[:, :], 1.0, ALU.is_ge, "IB", "E5")
+    ts(E6[:, 4, :], E6[:, 4, :], m, ALU.is_ge, "E4 CC", "E4")
+    tt(E6[:, 0, :], E6[:, 0, :], E6[:, 1, :], SUB, "E0 E1", "E0")
+    tt(E6[:, 3, :], E6[:, 2, :], E6[:, 3, :], SUB, "E2 E3", "E3")
+    ts(col["t1"], m, 0.0, EQ, "CC", "ct1")
+    tt(MQ[:, :, 0:16:4], E6[:, 0, :], E6[:, 4, :], MUL, "E0 E4", "MQ0")
+    tt(MQ[:, :, 1:16:4], E6[:, 3, :], E6[:, 4, :], MUL, "E3 E4", "MQ1")
+    tt(MQ[:, :, 2:16:4], E6[:, 1, :], E6[:, 4, :], MUL, "E1 E4", "MQ2")
+    ts(E6[:, 2, :], E6[:, 2, :], m, MUL, "E2 E3 CC", "E2", 0.0, ALU.is_gt)
+    ts(E6[:, 0, :], E6[:, 5, :], col["t1"], MUL, "E5 ct1 MQ0", "E0")
+    tt(MQ[:, :, 3:16:4], E6[:, 0, :], E6[:, 2, :], SUB, "E0 E2", "MQ3")
+    MQk = "MQ0 MQ1 MQ2 MQ3"
+    tt(T.HI[:, 0:16], MQ[:, 4, :], MQ[:, 5, :], ADD, MQk, "HI")
+    tt(T.HI[:, 0:16], T.HI[:, 0:16], MQ[:, 6, :], ADD, MQk + " HI", "HI")
+    for s in (0, 1):
+        act(T.T5[:, 80 * s + 4:80 * s + 80:5], T.HI[:, 0:16], AF.Copy, "HI", "T5c%d" % s, 128.0)
+    ts(col["r0"], m, 7.0, EQ, "CC ct1", "cr0", col["t1"], SUB)
+    ts(E6[:, 5, 16:28], E6[:, 5, 16:28], col["r0"], MUL, "E5 E0 cr0", "E5")
+    tt(MQ[:, 4:7, 3:16:4], MQ[:, 4:7, 3:16:4], E6[:, 5, 16:28], ADD, "MQ3 E5 HI", "MQn")
+    for a in (4, 5, 6):
+        ts(MQ[:, a, :], MQ[:, a, :], col["h" if a % 2 == 0 else "h1"], MUL, MQk + " MQn HI CC ch1", "CF%d" % a, 0.5, MUL)
+        for q in (0, 1):
+            act(MQ[:, a, q:16:4], MQ[:, a, q:16:4], AF.Copy, "CF%d" % a, "CF%d" % a, 1.0 / 4096)
+    ts(T.KN[:, 0, :], T.KA[:, :], m, ALU.is_lt, "KA CC cn7", "KN0", col["n7"], MUL)
+    ts(T.KN[:, 1, :], T.KC[:, :], m, ALU.is_lt, "KC CC cn7", "KN1", col["n7"], MUL)
+    tt(T.W16[:, :], T.KA[:, :], T.KC[:, :], ALU.not_equal, "KA KC", "NE")
+    tt(T.KN[:, 1, :], T.KN[:, 1, :], T.W16[:, :], MUL, "KN1 NE", "KN1")
+    tt(T.KN[:, 0, :], T.KN[:, 0, :], T.KN[:, 1, :], ADD, "KN0 KN1", "KN0")
+    ts(T.KN[:, 1, :], T.W16[:, :], 1.0, ADD, "NE", "KN1")
+    act(T.KT[:, :, :], T.KN[:, :, :], AF.Copy, "KN0 KN1", "KT", 1.0 / 4096)
+    ms(T.RS5[:, :], 1.0, "RS5", 80)
+    ms(T.RS5[:, 0:80:5], 0.0, "RS5")
+    ms(T.RS4[:, :], 1.0, "RS4")
+    ms(T.RS4[:, 0:32:4], 0.0, "RS4")
+    cp(T.NLF[0:8, :], T.NL[0:8, :], "NL", "NLF")
+    ms(T.W16[:, :], 0.0, "NE W16")
+    for s in (0, 1):
+        S[0] = s
+        F, ST, CS = X("F"), X("ST"), X("CS")
+        ts(T.SL[0:8, :], T.IG[0:8, :], 4.0 * s, ADD, "IG CC", "SL", CC[0:8, 0:1], EQ, 128)
+        mm(bank("a")[:, 0:4], T.SL[0:8, :], T.NLF[0:8, :], "SL NLF", "a", c=256)
+        cp(F[:, 0:4], bank("a")[:, 0:4], "a", "F@")
+        for a in range(4):
+            act(T.T5[:, 80 * s + a:80 * s + 80:5], MQ[:, a, :], AF.Copy, MQk + " F@", "T5%d@" % a, F[:, a:a + 1])
+        o, base = slice(16 * s, 16 * s + 16), X("W")[:, 4:80:5]
+        scan(X("W")[:, 0:80], T.RS5[:, :], T.T5[:, 80 * s:80 * s + 80], MUL, ADD, "RS5 T5c@ T50@ T51@ T52@ T53@", "W@", 80)
+        ts(T.BS[:, o], base, M32, ADD, "W@", "BS@", M32, SUB)
+        act(T.HI[:, o], base, AF.Copy, "W@ CC T5c0 T5c1 MQn", "T5h@", col["h"])
+        ts(T.BS[:, o], T.BS[:, o], col["hs"], MUL, "BS@ chs", "BS@")
+        tt(ST[:, :, 0:4], T.BS[:, o], T.HI[:, o], ADD, "BS@ T5h@", "ST@")
+        ts(ST[:, :, 0:2], ST[:, :, 0:2], 1.0 / 4096, MUL, "ST@", "ST@ SV0@ SV1@ SV2@ SV3@")
+        ts(CS[:, 16:20], F[:, 0:4], F[:, 3:4], MUL, "F@", "p3@", -2047.5, ADD)
+        ts(CS[:, 20:22], F[:, 1:3], F[:, 2:3], MUL, "F@", "p2@", -2047.5, ADD)
+        ts(T.W16[:, 0:16:5], CS[:, 16:20], M4096, ADD, "p3@ W16", "W16a", M4096, SUB)
+        ts(T.W16[:, 1:7:5], CS[:, 20:22], M4096, ADD, "p2@ W16", "W16b", M4096, SUB)
+        for k in (0, 1):
+            tt(T.PB[:, 16 * k:16 * k + 16], T.KT[:, k, :], T.W16[:, :], MUL, "KT W16a W16b", "PB%d" % k)
+        PB = X("W")
+        scan(PB[:, 256:288], T.RS4[:, :], T.PB[:, :], MUL, ADD, "RS4 PB0 PB1", "Wz@")
+        ts(CS[:, 1:2], PB[:, 259:260], col["cP"], ADD, "Wz@ ccP", "Cl@")
+        cp(CS[:, 2:3], PB[:, 275:276], "Wz@", "Ct@")
+        act(ST[:, :, 5], PB[:, 275:288:4], AF.Copy, "Wz@", "SB1@ SB2@ SB3@")
+        lin("A", ST[:, :, 4], PB[:, 259:272:4], 1.0, col["cP"], "Wz@ ccP", "SA1@ SA2@ SA3@")
+        act(F[:, 4:5], F[:, 0:1], AF.Copy, "F@", "a0@", 1.0 / 8192)
+        act(F[:, 5:6], F[:, 0:1], AF.Copy, "F@", "b0@", 1.0 / 32, HALF)
+        act(F[:, 6:8], F[:, 1:3], AF.Copy, "F@", "F12@", 1.0 / 4096)
+        ms(CS[:, 10:11], B / 4096.0, "T4@")
+    ts(T.WCP[:, 0:8:2], T.IR[:, 0:4], col["g"], EQ, "IR CC ch1", "WCa", col["h1"], MUL)
+    ts(T.WCP[:, 1:8:2], T.IR[:, 0:4], col["g"], EQ, "IR CC", "WCb", col["h"], MUL)
+    act(T.WCP[:, 8:16], T.WCP[:, 0:8], AF.Copy, "WCa WCb", "WCc", -1.0)
+    act(T.WCP[:, 16:24], T.WCP[:, 0:8], AF.Copy, "WCa WCb cwt", "WCP", col["wt"])
+    for ap, k, x in ((NDG, "NDG", -1.0), (D512, "D512", 512.0), (D4, "D4", 0.25), (D8, "D8", 0.125)):
+        ts(ap, DG, x, MUL, "DG", k)
+    LMF = T.LMF
+    cp(LMF[0:16, 0:2], T.LM[0:16, :], "LM", "LMF")
+    ts(LMF[0:16, 2:3], LMF[0:16, 1:2], -1.0, MUL, "LMF", "LM2", -0.5, ADD)
+    ts(LMF[0:16, 3:4], LMF[0:16, 0:1], -0.5, ADD, "LMF", "LM3")
+    ts(LMF[0:16, 4:6], LMF[0:16, 2:4], M32, ADD, "LM2 LM3", "LM4", M32, SUB)
+    ts(CC[0:16, 34:35], CC[0:16, 0:1], 8.0, ALU.is_ge, "CC", "cpt")
+    ts(CC[0:16, 35:36], CC[0:16, 34:35], -2.0, MUL, "cpt", "cpts", 1.0, ADD)
+    ts(LMF[0:16, 4:6], LMF[0:16, 4:6], CC[0:16, 35:36], MUL, "LM4 cpts", "LM4")
+    ts(LMF[0:16, 2:4], LMF[0:16, 2:4], CC[0:16, 34:35], MUL, "LM2 LM3 LM4 cpt", "LM2 LM3")
+    tt(LMF[0:16, 4:6], LMF[0:16, 4:6], LMF[0:16, 2:4], ADD, "LM2 LM4", "LM4")
+    ts(LMF[0:16, 6:7], CC[0:16, 34:35], 3.5, MUL, "cpt", "LM6", -3.5, ADD)
+    for s in (0, 1):
+        ts(CC[0:16, 38 + s:39 + s], CC[0:16, 6:7], -4.0 * s, ADD, "CD", "cG%d" % s)
+        for k in range(3):
+            ts(T.PRE[0:16, 384 * s + 128 * k:384 * s + 128 * k + 128], T.GB[0:16, :], CC[0:16, 38 + s:39 + s], EQ, "GB LM4 LM6 cG%d" % s, "PRE%d%d" % (k, s), LMF[0:16, 4 + k:5 + k], MUL)
+    ts(FOLD, T.I64[:, :], col["p64"], EQ, "I64 CD", "FOLD", c=128)
+    ts(W8, BON, col["w8"], MUL, "BON cw8", "W8")
+    ts(B4, BON, 4.0, MUL, "BON", "B4")
+    ts(W04, BON, col["i0"], MUL, "BON ci0", "W04", 4.0, MUL)
+    ms(T.Q25[:, :], 0.25, "Q25")
+    scan(T.POW[:, :], T.Q25[:, :], T.ZERO[:, 0:32], MUL, ADD, "Q25 ZERO", "POW", init=4.0)
+    ts(T.Q25[:, :], T.IR[:, 0:32], col["l"], EQ, "IR cl POW", "Q25")
+    tt(T.Q25[:, :], T.Q25[:, :], T.POW[:, :], MUL, "Q25 POW", "Q25")
+    do("V", lambda v: v.tensor_reduce(col["pw"], T.Q25[:, :], AX.X, ADD), "Q25", "cpw", 64)
+    ts(BW, BON, col["pw"], MUL, "BON cpw", "BW")
+    act(T.NTH[0:1, 0:32], T.POW[0:1, :], AF.Copy, "POW", "NTH", -2.0)
+    for n in (32, 64, 128):
+        act(T.NTH[0:1, n:2 * n], T.NTH[0:1, 0:n], AF.Copy, "NTH", "NTH", c=max(64, n))
+    lin("V", col["lpc"], col["pid"], 1.0, 15.0, "CC", "clpc")
+    ts(col["mk"], col["i0"], col["h1"], MUL, "ci0 ch1", "cmk")
+    ts(T.LP[:, 0:80], T.IR[:, 0:80], col["lpc"], EQ, "IR clpc cmk", "LPa", col["mk"], MUL, 80)
+    ts(T.LP[:, 79:144], T.IR[:, 15:80], col["lpc"], EQ, "IR clpc cmk LPa", "LP", col["mk"], MUL)
+    ts(T.LI[:, 0:80], T.IR[:, 0:80], col["lic"], EQ, "IR clic cw8", "LIa", col["w8"], MUL, 80)
+    ts(T.LI[:, 79:144], T.IR[:, 15:80], col["lic"], EQ, "IR clic cw8 LIa", "LI", col["w8"], MUL)
+    ts(T.MI[:, 0:112], T.IR[:, 0:112], col["mic"], EQ, "IR cmic", "MIa", c=112)
+    ts(T.MI[:, 112:176], T.IR[:, 48:112], col["mic"], EQ, "IR cmic", "MIb")
+    act(T.MH[:, 0:112], T.MI[:, 0:112], AF.Copy, "MIa", "MHa", -33.0, c=112)
+    act(T.MH[:, 112:176], T.MI[:, 112:176], AF.Copy, "MIb", "MHb", -31.0)
+    for k, x in enumerate((2.0, 32.0, 1.0)):
+        ts(T.RPM[:, 64 * k:64 * k + 64], T.I8[:, 64 * k:64 * k + 64], col["q8"], EQ, "I8 CD", "RPM%d" % k, x, MUL)
+    ts(T.OCF[:, :], T.OCF[:, :], col["hc"], ADD, "OCF chc", "OCF")
+    for k, (x, y) in enumerate(((32.0, 256.0 + 31), (1.0, 512.0), (32.0, 15.0))):
+        ts(T.OC[:, 4 * k:4 * k + 4], T.OCF[:, 4 * k:4 * k + 4], x, MUL, "OCF", "OC%d" % k, y, ADD)
+    ms(T.RS32[:, :], 1.0, "RS32", 128)
+    ms(T.RS32[:, 0:256:32], 0.0, "RS32")
+    ts(T.WJ[:, :], T.WJ[:, :], col["i"], ADD, "WJ0 CC", "WJ")
+    ts(T.ND[:, :], T.ND[:, :], col["i"], SUB, "ND0 CC", "ND", -0.5, ADD)
+    ts(col["G8"], col["l"], 31.0, EQ, "cl", "cG8", MARK, MUL)
+    for s in (0, 1):
+        S[0] = s
+        cp(X("K")[:, 4097:4098], col["G8"], "cG8 Ke@", "Km@")
+        ts(X("Z")[:, 160:161], T.ONE[:, 0:1], col["pid"], MUL, "ONE CC", "Zr@", 0.5, ALU.is_gt)
+        ms(X("WN")[:, 520:528], 0.0, "WNz@")
 
     def lists(t):
-        CS, ct, k = T.CS, T.SEL[:, 4 + t:5 + t], "%d" % (t > 0)
-        c = slice(256 * t, 256 * t + 256)
-        ts(T.RH[:, :], T.COLT[:, :], CS[:, 4:5], ALU.is_ge, "COLT CS4", "RH")
-        ts(T.IND[:, :], T.IT[:, :], ct, ALU.mult, "IT SEL CS6", "IND", CS[:, 6:7], ALU.is_ge)
-        for b in ("b2", "b4"):
-            mm(T[b][:, 0:256], T.CL[:, :], T.ONE[:, :], "CL ONE", b, True, False)
-        for q, b in ((1, "b1"), (3, "b2"), (0, "b3"), (2, "b4")):
-            for h in (0, 1):
-                n = 2 * q + h
-                if h == 0:
-                    ts(T.LQ[:, 128 * n:128 * n + 128], T.IND[:, :], T.HI[:, q:q + 1], ALU.mult, "IND HI HI2", "LQ%d" % n)
+        CS, ST, W, OF, R, d = X("CS"), X("ST"), X("W"), X("OF"), X("R"), bank("d")
+        k, c = "%d@" % (t > 0), slice(256 * t, 256 * t + 256, 2)
+        cl_, ct = CS[:, 1:2], CS[:, 2:3]
+        mm(d[:, :], T.LC[0:3, :], T.RI[0:3, :], "LC RI RIa", "d", True, False, 512)
+        do("V", lambda v: v.reciprocal(CS[:, 3:4], ct), "Ct@", "rc@", 240)
+        lin("A", CS[:, 6:7], ct, -0.484375 / 128, cl_, "Cl@ Ct@", "c1@")
+        lin("A", CS[:, 4:5], cl_, col["nsg"], col["off"], "Cl@ cnsg coff", "SC@")
+        act(CS[:, 5:6], ct, AF.Copy, "Ct@ cnsg", "NC@", col["nsg"])
+        ts(CS[:, 0:1], CS[:, 6:7], CS[:, 3:4], MUL, "c1@ rc@", "cb@", M7, ADD)
+        lin("A", W[:, 0:128], IT, ct, CS[:, 4:5], "IT Ct@ SC@", "W@", 128)
+        ts(CS[:, 8:9], CS[:, 0:1], M7, SUB, "cb@ NC@", "X@", CS[:, 5:6], MUL)
+        ts(CS[:, 7:8], CS[:, 0:1], M7, SUB, "cb@", "c2@")
+        ts(X("IND")[:, :], W[:, 0:128], CS[:, 8:9], ALU.is_ge, "W@ X@", "IND@", c=128)
+        for q in range(4):
+            val = CS[:, 12 + q:13 + q] if t and q < 2 else ST[:, t, q:q + 1]
+            ts(X("ZG")[:, 128 * q:128 * q + 128], COLT, CS[:, 7:8], ALU.is_ge, "COLT c2@ SV%d@ VL%d@" % (t, q), "RQ%d@" % q, val, MUL)
+        mm(d[:, 0:256], X("IND")[:, :], X("ZG")[:, 0:256], "IND@ RQ0@ RQ1@", "d", False, False, 256)
+        mm(d[:, 256:512], X("IND")[:, :], X("ZG")[:, 256:512], "IND@ RQ2@ RQ3@", "d", False, True, 256)
+        ts(W[:, 256:384], R[:, 2, c], CS[:, 10:11], MUL, "R2" + k + " T4@", "Wz@", HALF - MID, ADD, 128)
+        ts(OF[:, 256:384], W[:, 256:384], M1, ADD, "Wz@", "OZ@", M1 - MID, SUB, 128)
+        tt(W[:, 0:256], d[:, 0:256], R[:, 0:2, c], MUL, "d R0" + k + " R1" + k, "W@", 256)
+        tt(W[:, 0:256], W[:, 0:256], d[:, 256:512], ADD, "W@ d", "W@", 256)
+        ts(OF[:, 128:256], W[:, 128:256], M1, ADD, "W@", "OY@", M1 - MID, SUB, 128)
+        ts(OF[:, 0:128], W[:, 0:128], M1, ADD, "W@", "OX@", M1 - MID, SUB, 128)
+
+    def pieces(q):
+        return [(p, 512 // CUT[q]) for p in range(0, 512, 512 // CUT[q])]
+
+    def build(t):
+        win, OF, K, XG, YG, ZG, FX, a = X("bank")[:, 0:B + 256 * t], X("OF"), X("K"), X("XG"), X("YG"), X("ZG"), X("FX"), bank("a")
+        bk = " bk@ bz1@ bz2@" if t > 1 else " bk@"
+        mm(a[:, 0:256], T.ONE[0:16, 0:128], T.PRE[0:16, 384 * S[0]:384 * S[0] + 256], "ONE PRE0@ PRE1@", "a", True, False, 256)
+        mm(bank("d")[:, 0:128], T.ONE[0:16, 0:128], T.PRE[0:16, 384 * S[0] + 256:384 * S[0] + 384], "ONE PRE2@", "d", True, False, 128)
+        tmp, n0 = 0, len(ops)
+        for q in ORDER:
+            mode, op = MODE[q], (ALU.min, ALU.max, None, ADD)[q]
+            for p, PIECE in pieces(q):
+                gc_ = 70 + GATHER * PIECE
+                o, k = 512 * q + p, "%d%d@" % (q, p)
+                c, ko = slice(o, o + PIECE), K[:, 2 * o + 1:2 * (o + PIECE):2]
+                x, y, z = [win.indirect(OF[:, b + o // 16:b + (o + PIECE) // 16]) for b in (0, 128, 256)]
+                act(YG[:, c], y, AF.Copy, "OY@" + bk, "YG" + k, c=gc_)
+                if mode == "a":
+                    tt(FX[:, c], x, YG[:, c], op, "OX@ YG" + k + bk, "FX" + k, gc_)
                 else:
-                    act(T.LQ[:, 128 * n:128 * n + 128], T.IND[:, :], AF.Copy, "IND LO", "LQ%d" % n, T.LO[:, q:q + 1])
-                mm(T[b][:, 0:256], T.LQ[:, 128 * n:128 * n + 128], T.RH[:, :], "LQ%d RH" % n, b, q < 2 and h == 0, h == 1)
-        act(T.ZG[:, :], win.indirect(T.OZ[:, 192:224]), AF.Copy, "OZ " + bankk, "ZG")
-        for w, r, o, bn, bs in (("V1", "RB", "OY", "b1", "b2"), ("W1", "RA", "OX", "b3", "b4")):
-            tt(T[w][:, :], T[bn][:, 0:256], T[r][:, c], ALU.mult, bn + " " + r + k, w)
-            tt(T[w][:, :], T[w][:, :], T[bs][:, 0:256], ALU.add, w + " " + bs, w)
-            ts(T[o][:, :], T[w][:, :], M1, ALU.add, w, o, M1 - MID, ALU.subtract)
+                    b = "bc"[tmp % 2]
+                    tmp += 1
+                    pb = bank(b)[:, 0:PIECE]
+                    act(XG[:, c], x, AF.Copy, "OX@" + bk, "XG" + k, c=gc_)
+                    mm(pb, DG, XG[:, c], "DG XG" + k, b, True, False, PIECE)
+                    mm(pb, DG if q == 3 else NDG, YG[:, c], "DG NDG YG" + k, b, False, True, PIECE)
+                    if q < 2:
+                        act(FX[:, c], pb, AF.Relu, b, "FX" + k, c=PIECE)
+                        mm(pb, DG, (XG, YG)[q][:, c], "DG XG" + k + " YG" + k, b, True, False, PIECE)
+                        mm(pb, (NDG, DG)[q], FX[:, c], "DG NDG FX" + k, b, False, True, PIECE)
+                    if mode == "b":
+                        act(FX[:, c], pb, AF.Abs, b, "FX" + k, c=PIECE)
+                    elif q == 2:
+                        act(pb, pb, AF.Abs, b, b, c=PIECE)
+                if mode == "c":
+                    act(ZG[:, c], z, AF.Copy, "OZ@" + bk, "ZG" + k, c=gc_)
+                    tt(ko, pb, ZG[:, c], ALU.min, b + " ZG" + k, "K" + k, PIECE)
+                else:
+                    tt(ko, z, FX[:, c], ALU.min, "OZ@ FX" + k + bk, "K" + k, gc_)
+            for b_ in range(16):
+                kq, kk = K[:, 1024 * q + 2 * b_ + 1:1024 * q + 1024:32], " ".join("K%d%d@" % (q, p) for p, _ in pieces(q))
+                mm(a[32 * q:32 * q + 32, b_:256:16], kq, T.WCP[:, 0:16], "WCa WCb WCc " + kk, "a", False, b_ == 15, 32)
+            for b_ in range(16):
+                kq = K[:, 1024 * q + 2 * b_ + 1:1024 * q + 1024:32]
+                mm(bank("d")[32 * q:32 * q + 32, b_:128:16], kq, T.WCP[:, 16:24], "WCP " + kk, "d", False, b_ == 15, 32)
+        for e in "VA":
+            row = [k for k in range(n0, len(ops)) if ops[k][0] == e and ops[k][3] > 70 + GATHER * 100 and ops[k][3] not in (256, 512)]
+            for k, j in zip(row, row[1:]):
+                ops[j][2].setdefault(k, False)
 
-    def build(t, h0, h1):
-        def y(q, dst="YG", lst="OY", a=0, n=1024):
-            o = 1024 * q + a
-            act(T[dst][:, o:o + n], win.indirect(T[lst][:, o // 16:(o + n) // 16]), AF.Copy, lst + " " + bankk, "%s%d%d" % (dst, q, a))
-
-        def x(q, a=0, n=1024):
-            o = slice(1024 * q + a, 1024 * q + a + n)
-            tt(T.FX[:, o], win.indirect(T.OX[:, 64 * q + a // 16:64 * q + (a + n) // 16]), T.YG[:, o], (ALU.min, ALU.max, None, ALU.add)[q], "OX YG%d%d " % (q, a) + bankk, "FX%d%d" % (q, a))
-
-        def both(q, b, o, lh):
-            k = (q, o - 1024 * q)
-            mm(T[b][:, :], T.DG[:, :], T.XG[:, o:o + 512], "DG XG%d%d" % k, b, True, False)
-            mm(T[b][:, :], T[lh][:, :], T.YG[:, o:o + 512], lh + " YG%d%d" % k, b, False, True)
-
-        def z(q, a=0, n=1024):
-            o = 1024 * q + a
-            tt(T.K[:, o:o + n], win.indirect(T.OZ[:, o // 16:(o + n) // 16]), T.FX[:, o:o + n], ALU.min, "OZ FX%d%d FX%d512 " % (q, a, q) + bankk, "K%d%d" % (q, a))
-
-        def sums(q, n=1024):
-            for b in range(32):
-                mm(T.b0[32 * q:32 * q + n // 32, b:512:32], T.K[:, 1024 * q + b:1024 * q + n:32], T.WCP[:, :], "WCP K%d0 K%d512" % (q, q), "b0")
-        y(0, n=512)
-        y(0, a=512, n=512)
-        y(1)
-        x(0, 0, 512)
-        x(0, 512, 512)
-        h0()
-        h1()
-        z(0)
-        sums(0)
-        for a, b in ((0, "b5"), (512, "b6")):
-            y(2, a=a, n=512)
-            y(2, "XG", "OX", a=a, n=512)
-            both(2, b, 2048 + a, "NDG")
-        x(1)
-        z(1)
-        y(3, a=512, n=512)
-        act(T.FX[:, 2048:2560], T.b5[:, :], AF.Abs, "b5", "FX20")
-        act(T.FX[:, 2560:3072], T.b6[:, :], AF.Abs, "b6", "FX2512")
-        sums(1)
-        x(3, 512, 512)
-        z(3, 512, 512)
-        if t:
-            sums(3)
-        y(3, n=512)
-        y(3, "XG", "OX", n=512)
-        both(3, "b7", 3072, "DG")
-        z(2)
-        sums(2)
-        tt(T.K[:, 3072:3584], T.b7[:, :], T.ZG[:, :], ALU.min, "b7 ZG", "K30")
-        sums(3, 512 if t else 1024)
-
-    def pick(t, h):
-        tt(T.Z1[:, :], T.b0[:, 0:256], T.MIDT[:, :], ALU.subtract, "b0 MIDT", "Z1")
-        act(T.b7[:, 0:256], T.Z1[:, :], AF.Abs, "Z1", "b7")
-        ts(T.OI[:, :], T.b0[:, 256:512], 2.0, ALU.mult, "b0", "OI", 1.0, ALU.add)
-        ts(T.OJ[:, :], T.OI[:, :], 15, ALU.bitwise_and, "OI", "OJ")
-        tt(T.b7[:, 256:512], T.b7[:, 0:256], T.HALF[:, :], ALU.is_le, "b7 HALF", "b7")
-        tt(T.OWN[:, :], T.OJ[:, :], T.b7[:, 256:512], ALU.mult, "OJ b7", "OWN")
-        act(T.OA[:, :], T.OWN[:, :], AF.Abs, "OWN CCg", "OA", 1.0, col["m15"])
-        act(T.O[:, 1792:2048], T.OA[:, :], AF.Relu, "OA CCh", "O7", -1.0, col["on1"])
-        for p in range(7):
-            ts(T.O[:, 256 * p:256 * p + 256], T.OWN[:, :], 2.0 * p + 1, ALU.is_equal, "OWN", "O%d" % p)
-        h()
-        for q in range(8):
-            mm(T.b6[:, SEG * q + 9:SEG * q + SEG], T.BID[:, :], T.OWN[:, 32 * q:32 * q + 32], "BID OWN", "b6")
-            mm(T.b6[:, SEG * q + 8:SEG * q + 9], T.BID[:, :], T.JC[:, :], "BID JC", "b6")
-        for b in range(32):
-            mm(T.b5[:, 0:64], T.TRI[:, :], T.O[:, b:2048:32], "TRI O0 O1 O2 O3 O4 O5 O6 O7", "b5", b == 0, b == 31)
+    def pick(t):
+        a, b, c, d = [bank(k) for k in "abcd"]
+        DS, V, O, S4, U, Z, EC, CU, WN, RJ, RR = [X(n) for n in ("DS", "V", "O", "S4", "U", "Z", "EC", "CU", "WN", "RJ", "RR")]
+        act(DS[:, :], a[:, 0:256], AF.Sign, "a", "DS@", c=256)
+        mm(b[:, 0:128], D4, DS[:, 0:128], "D4 DS@", "b", True, False, 128)
+        mm(b[:, 0:128], D8, DS[:, 128:256], "D8 DS@", "b", False, True, 128)
+        ts(RR[:, 0:128], d[:, 0:128], M8, ADD, "d", "RR@", M8, SUB, 128)
+        tt(X("OW")[:, :], d[:, 0:128], RR[:, 0:128], SUB, "d RR@", "OW@", 128)
+        tt(V[:, :], b[:, 0:128], X("OW")[:, :], ADD, "b OW@", "V@", 128)
+        for p in range(8):
+            ts(O[:, 16 * (p // 4) + p % 4:16 * (p // 4) + 16:4, :], V[:, :], p - 3.875, EQ, "V@", "O%d@" % p)
+        mm(c[:, 0:128], BID, V[:, :], "BID V@", "c", c=128)
+        act(Z[:, 0:128], c[:, 0:128], AF.Copy, "c", "Zv@", c=128)
+        for k in range(32):
+            mm(b[:, 0:32], TRI, O[:, :, k], "TRI " + " ".join("O%d@" % p for p in range(8)), "b", k == 0, k == 31)
         for r in range(4):
-            ts(T.S4[:, 64 * r:64 * r + 64], T.b5[:, 0:64], -float(r), ALU.add, "b5", "S4%d" % r, 100.0, ALU.min)
-        for q in range(8):
-            mm(T.b6[:, SEG * q:SEG * q + 8], T.BID[:, :], T.S4[:, q:64:8], "BID S40", "b6")
-        act(T.Z[:, :], T.b6[:, 0:8 * SEG], AF.Copy, "b6", "Z")
-        for c in range(8):
-            ts(T.U[:, 256 * c:256 * c + 256], T.S4[:, :], 4.0 * c, ALU.is_le, "S40 S41 S42 S43", "U%d" % c)
-        for ch in (0, 1):
-            for lo, hi, b in ((0, 9, "b%d" % (3 + ch)), (9, SEG, "b%d" % (1 + ch))):
-                for q in range(8):
-                    mm(T[b][:, (hi - lo) * q:(hi - lo) * (q + 1)], T.U[:, 1024 * ch + q:1024 * ch + 1024:8], T.Z[:, SEG * q + lo:SEG * q + hi],
-                       "Z U%d U%d U%d U%d" % tuple(range(4 * ch, 4 * ch + 4)), b)
-        for ch in (0, 1):
-            d, b = slice(72 * ch, 72 * ch + 72), T["b%d" % (3 + ch)]
-            tt(T.SMM[:, d], b[:, 0:72], T.MSK[:, d], ALU.mult, "b%d MSK" % (3 + ch), "SMM%d" % ch)
-            act(T.R32[:, 8 * ch:8 * ch + 8], b[:, 8:72:9], AF.Copy, "b%d" % (3 + ch), "R32%d" % ch, 32.0, -2048.0)
-            if ch:
-                scan(T.SS[:, :], T.RSS[:, :], T.SMM[:, :], ALU.mult, ALU.add, "RSS SMM0 SMM1", "SS")
-            ts(T.EO[:, 256 * ch:256 * ch + 256], T["b%d" % (1 + ch)][:, 0:256], col["podd"], ALU.is_equal, "b%d CCo" % (1 + ch), "EO%d" % ch)
-        tt(T.EO[:, 0:512:32], T.EO[:, 0:512:32], T.SS[:, 8:144:9], ALU.add, "SS EO0 EO1", "EO0 EO1")
-        scan(T.CU[:, :], T.RS[:, :], T.EO[:, :], ALU.mult, ALU.add, "RS EO0 EO1", "CU")
-        ts(T.IN[:, 0:256], T.CU[:, 0:256], col["c16"], ALU.is_le, "CU CC", "IN0")
-        ts(T.IN[:, 256:512], T.CU[:, 256:512], col["c32"], ALU.is_le, "CU CC2", "IN1")
-        scan(T.C2[:, :], T.RS[:, :], T.IN[:, :], ALU.mult, ALU.add, "RS IN0 IN1", "C2")
-        tt(T.J16[:, :], T.C2[:, 31:512:32], T.R32[:, :], ALU.add, "C2 R320 R321", "J16")
-        do("V", lambda v: v.tensor_tensor(T.LJ[:, :], T.J16[:, :].indirect(T.OC[:, :]), T.MI[:, :], ALU.mult), "J16 OC MI", "LJ")
-        for ch in (0, 1):
-            mm(T.b5[:, ch:16:2], T.LJ[:, 128 * ch:128 * ch + 128], T.RP[:, :], "LJ RP", "b5")
-        ts(T.OFJ[:, :], T.b5[:, 0:16], 2048.0, ALU.add, "b5", "OFJ")
-        o = 256 * t
-        do("V", lambda v: v.tensor_copy(T.send[:, o:o + 256], T.K[:, 0:4112].indirect(T.OFJ[:, :])), "OFJ K00 K10 K20 K30 K3512 kinv", "snd%d" % t)
-        tr, k = [], 0
+            act(S4[:, r:128:4], b[:, 0:32], AF.Copy, "b", "S%d@" % r, 1.0, -float(r))
+        mm(c[:, 128:160], BID, S4[:, 0:128:4], "BID S0@", "c")
+        act(Z[:, 128:160], c[:, 128:160], AF.Copy, "c", "Zs@")
+        for k in range(8):
+            ts(U[:, :, 4 * k:4 * k + 4], S4[:, :], 4.0 * k, ALU.is_le, "S0@ S1@ S2@ S3@", "U%d@" % k)
+        uk = " " + " ".join("U%d@" % k for k in range(8))
+        for n in range(8):
+            mm(b[:, 32 * n:32 * n + 32], U[:, 4 * n:4 * n + 4, :], Z[:, 32 * (n % 4):32 * (n % 4) + 32], "Zv@" + uk, "b")
+        for n in range(8):
+            for p in range(4):
+                k = 4 * n + p
+                mm(d[32 * p:32 * p + 32, n:16:8], U[:, k, :], Z[:, 128 + k:161:32 - k], "Zs@ Zr@" + uk, "d", c=32)
+        for h in (0, 1):
+            ts(EC[:, 128 * h:128 * h + 128], b[:, 128 * h:128 * h + 128], col["pv%d" % h], EQ, "b cpv%d" % h, "EO%d@" % h, c=128)
+        tt(EC[:, 0:256:32], d[:, 0:8], EC[:, 0:256:32], ADD, "EO0@ EO1@ d", "EO0@ EO1@")
+        act(WN[:, 512:520], d[:, 8:16], AF.Copy, "d", "WR@")
+        scan(CU[:, :], T.RS32[:, :], EC[:, :], MUL, ADD, "RS32 EO0@ EO1@", "CU@", 128)
+        ts(WN[:, 0:256], CU[:, :], col["c32"], ALU.is_le, "CU@ CD", "IN@", c=128)
+        scan(WN[:, 256:512], T.RS32[:, :], WN[:, 0:256], MUL, ADD, "RS32 IN@", "C2@", 128)
+        tt(RJ[:, :], WN[:, :].indirect(T.OC[:, :]), T.RPM[:, :], MUL, "IN@ C2@ WR@ WNz@ OC0 OC1 OC2 RPM0 RPM1 RPM2", "RJ@", 50 + 192 * GATHER)
+        for n in range(12):
+            q = n % 4
+            mm(c[:, 0:16], (T.MH if n >= 8 else T.MI)[:, 48 - 16 * q:176 - 16 * q], RJ[:, 16 * n:16 * n + 16], "MIa MIb MHa MHb RJ@", "c", n == 0, n == 11)
+        ts(X("OS")[:, 0, :], c[:, 0:16], col["h1"], ADD, "c ch1", "OJ@")
+        o, send, land = 256 * t, X("send"), X("land")
+        kk = " ".join("K%d%d@" % (q, p) for q in range(4) for p, _ in pieces(q)) + " Kz0@ Kz1024@ Kz2048@ Kz3072@ Ke@ Km@"
+        act(send[:, o:o + 256], X("K")[:, :].indirect(X("OS")[:, 0, :]), AF.Copy, "OJ@ " + kk, "snd%d@" % t, c=75 + 256 * GATHER)
+        tr, k, name = [], 0, "%d%d" % (S[0], t)
         for p in range(NR):
-            if p == rank:
-                continue
-            dst = T.cores[p]
-            e = topo.engines(core, dst)
-            rid, pid, _se = topo.addr(dst)
-            tr.append(RemoteDMATransfer(dst_ids=[DstId(rid=rid, pnc=pid)], dma_engine_mask=(1 << e[2 * k]) | (1 << e[2 * k + 1]), remote_sem=T.sem["arr%d" % t],
-                                        srcs=[T.send[:, o + 32 * p:o + 32 * p + 32]], dsts=[T.land[:, o + 32 * rank:o + 32 * rank + 32]]))
-            k += 1
-        order("G", ["snd%d" % t], [])
-        g.remote_dma_fused(tr, local_sem=T.sem["sent%d" % t])
-        cp(T.land[:, o + 32 * rank:o + 32 * rank + 32], T.send[:, o + 32 * rank:o + 32 * rank + 32], "snd%d" % t, "lnd%d" % t)
+            if p != rank:
+                e = topo.engines(core, T.cores[p])
+                rid, pid, _se = topo.addr(T.cores[p])
+                tr.append(RemoteDMATransfer(dst_ids=[DstId(rid=rid, pnc=pid)], dma_engine_mask=(1 << e[2 * k]) | (1 << e[2 * k + 1]), remote_sem=T.sem["arr" + name],
+                                            srcs=[send[:, o + 32 * p:o + 32 * p + 32]], dsts=[land[:, o + 32 * rank:o + 32 * rank + 32]]))
+                k += 1
+        do("G", lambda q: g.remote_dma_fused(tr, local_sem=T.sem["sent" + name]), "snd%d@" % t, "arr%d@" % t, 600, FLIGHT, ("arr" + name, 14))
+        act(land[:, o + 32 * rank:o + 32 * rank + 32], send[:, o + 32 * rank:o + 32 * rank + 32], AF.Copy, "snd%d@" % t, "own%d@" % t)
 
     def keep(t):
-        s, last = 4 + t, t == RO - 1
-        o, lk = 256 * t, "lnd%d" % t
-        lnd = T.land[:, o:o + 256]
-        ts(T.TC[:, 3:4], T.TC[:, 0:1], -1.0, ALU.add, "TC", "TB")
-        ts(T.WJ[:, :], T.JL[:, :], T.TC[:, 0:1], ALU.subtract, "JLx TC", "WJ", 4097.0, ALU.add)
-        wait("P", "arr%d" % t, 14)
-        mm(T.b3[:, 0:256], T.WBL[:, :], lnd, "WBL " + lk, "b3")
-        for i in range(16):
-            mm(T.b4[:, 0:16], T.LI[:, 128 * i:128 * i + 128], T.land[:, o + i:o + 256:16], "LI LI%d " % i + lk, "b4", i == 0, i == 15)
-        cp(T.OI[:, :], T.b3[:, 0:256], "b3", "OI")
-        ts(T.OJ[:, :], T.OI[:, :], 3, ALU.arith_shift_right, "OI", "OJ", 4095, ALU.bitwise_and)
-        cp(T.KLI[:, :], T.b4[:, 0:16], "b4", "KLI")
-        ts(T.KBH[:, :], T.OJ[:, :], -2048.0, ALU.add, "OJ", "KBH")
-        ts(T.KLJ[:, :], T.KLI[:, :], 3, ALU.arith_shift_right, "KLI", "KLJ", 4095, ALU.bitwise_and)
-        ts(T.INV[:, :], T.b4[:, 0:16], 0.0, ALU.is_lt, "b4", "INV", 4096.0, ALU.mult)
-        tt(T.BL[:, :], T.KLJ[:, :], T.INV[:, :], ALU.max, "KLJ INV", "BL")
-
-        def ed(a, b):
-            return " ".join("Ed%d" % m for m in range(a, b))
-
-        def later(a, b):
-            tt(T.E3[:, a:b, 0:16], T.E3[:, a:b, 0:16], T.DM[:, a:b, :], ALU.mult, ed(a, b) + " DM", ed(a, b))
-        for m in range(16):
-            ts(T.E3[:, m, 0:256 - 16 * m], T.KBH[:, 16 * m:256], 2048.0, ALU.add, "KBH BL", "E%d Ed%d" % (m, m), T.BL[:, m:m + 1], ALU.is_equal)
-            if m == 0:
-                cp(T.BU[:, :], T.BL[:, :], "BL", "BU")
-            if m == 1:
-                do("V", lambda v: v.tensor_copy(T.UG[:, :], T.USED[:, 0:4112].indirect(T.BU[:, :])), "USED USEDx BU", "UG")
-                mm(T.b6[:, 0:256], T.W0[:, :], T.UG[:, :], "W0 UG", "b6", True, False)
-            if m == NA + 1:
-                later(0, NA)
-        later(NA, 16)
-        for m in range(15):
-            mm(T.b6[:, 16 * m + 16:256], T.BON[:, :], T.E3[:, m, 16:256 - 16 * m], "BON E%d" % m, "b6", False, False)
-        mm(T.b6[:, 0:256], T.BON[:, :], T.E3[:, :, 0:16], "BON " + ed(0, 16), "b6", False, True)
-        ts(T.b7[:, 0:256], T.b6[:, 0:256], 0.5, ALU.is_lt, "b6", "b7")
-        scan(T.POS[:, :], T.ZERO[:, :], T.b7[:, 0:256], ALU.max, ALU.add, "ZERO b7", "POS")
-        n = T.POS[:, 255:256]
-        if not last:
-            tt(T.TC[:, 0:1], T.TC[:, 0:1], n, ALU.add, "TC POS", "TC")
-            ts(T.F4[:, s:32:8], T.ONEF[:, 0:4], n, ALU.mult, "ONEF POS", "F4")
-            cp(T.R8[:, 7 - s:8 - s], n, "POS", "R8")
-        tt(T.X[:, :], T.b7[:, 0:256], T.POS[:, :], ALU.mult, "b7 POS", "X")
-        if not last:
-            ts(T.TC[:, 1:2], T.TC[:, 0:1], 1.0 / 4096, ALU.mult, "TC", "TC1")
-        for i in range(16):
-            mm(T.b5[:, 0:16], T.LP[:, 128 * i:128 * i + 128], T.X[:, i:256:16], "LP LP%d X" % i, "b5", i == 0, i == 15)
-        app = (lambda: ts(T.ZT[:, :], T.b5[:, 0:16], 0.0, ALU.is_equal, "b5", "ZT"),
-               lambda: tt(T.D1[:, :], T.ZT[:, :], T.WJ[:, :], ALU.mult, "ZT WJ", "D1"),
-               lambda: tt(T.D1[:, :], T.D1[:, :], T.b5[:, 0:16], ALU.add, "D1 b5", "D1"),
-               lambda: ts(T.DU[:, :], T.D1[:, :], T.TC[:, 3:4], ALU.add, "D1 TB", "DU"),
-               lambda: do("V", lambda v: v.tensor_copy(T.bankS[:, 0:4352].indirect(T.DU[:, :]), lnd), lk + " DU", "bk bkz"))
+        a, b, c, d = [bank(k) for k in "abcd"]
+        RR, KB, E, UG, PK, SM, OS, LF, CS, ST, UP, F = [X(n) for n in ("RR", "KB", "E", "UG", "PK", "SM", "OS", "LF", "CS", "ST", "UP", "F")]
+        last, lnd, lk = t == RO - 1, X("land")[:, 256 * t:256 * t + 256], " arr%d@ own%d@" % (t, t)
+        act(CS[:, 11:12], CS[:, 10:11], AF.Copy, "T4@", "TB@", 4096.0, 127.5 - B)
+        act(CS[:, 9:10], CS[:, 10:11], AF.Copy, "T4@", "T4b@", 1.0, 1.0 / 32)
+        mm(a[:, :], T.LY[0:2, :], T.ONE[0:2, :], "LY ONE", "a", True, False, 512)
+        mm(a[:, :], T.LC[0:1, :], T.RI[0:1, :], "LC RI RIa", "a", False, False, 512)
+        mm(a[:, 0:256], W8, lnd, "W8" + lk, "a", False, False, 256)
+        mm(a[:, 256:512], W8, lnd, "W8" + lk, "a", False, True, 256)
         if last:
-            for f in app:
-                f()
-        else:
-            prep(t + 1, app)
-
-    def mark(t):
-        tt(T.UJ[:, :], T.JL[:, :], T.BL[:, :], ALU.subtract, "JLx BL", "UJ")
-        ts(T.E1[:, :], T.UJ[:, :], 4112.0, ALU.add, "UJ", "E1")
-        tt(T.E1[:, :], T.E1[:, :], T.ZT[:, :], ALU.mult, "E1 ZT", "E1")
-        tt(T.E1[:, :], T.E1[:, :], T.BL[:, :], ALU.add, "E1 BL", "E1")
-        cp(T.EU[:, :], T.E1[:, :], "E1", "EU")
-        do("V", lambda v: v.tensor_copy(T.USED[:, 0:4368].indirect(T.EU[:, :]), T.ONEI[:, :]), "EU ONEI", "USED USEDx")
-
-    prep(0)
-    ts(T.CL[:, :], T.BON[:, :], col["cval"], ALU.mult, "BON CCv", "CL")
-    lists(0)
-
-    def h0():
-        cp(T.LMF[:, 0:2], T.LM[:, :], "LM", "LMF")
-        ms(T.ONEF[:, :], 1.0, "ONEF")
-        tt(T.LMF[:, 2:3], T.LMF[:, 0:1], T.LMF[:, 1:2], ALU.add, "LMF", "LMF2")
-        tt(T.LMF[:, 3:4], T.LMF[:, 1:2], T.LMF[:, 0:1], ALU.subtract, "LMF", "LMF3")
-        ts(T.NDG[:, :], T.DG[:, :], -1.0, ALU.mult, "DG", "NDG")
-        ts(T.LMF[:, 4:6], T.LMF[:, 2:4], 0.5, ALU.mult, "LMF2 LMF3", "LMF4")
-
-    def h1():
-        ts(T.WCP[:, 0:8], T.IR[:, 0:8], col["grp"], ALU.is_equal, "IR CC", "WCPa")
-        ts(T.WCP[:, 8:16], T.IR[:, 0:8], col["grp"], ALU.is_equal, "IR CC CCw WCPa", "WCP", col["wt"], ALU.mult)
+            mm(d[:, 0:256], T.LN[0:1, :], T.ONE[0:1, 0:256], "LN ONE", "d", True, False, 256)
+        mm(d[:, 0:256], FOLD, lnd, "FOLD" + lk, "d", not last, not last, 256)
+        if not last:
+            act(LF[:, :], d[:, 0:256], AF.Copy, "d", "LF@", c=256)
+        mm(c[:, 0:256], T.ONE[0:1, 0:128], T.NTH[0:1, :], "ONE NTH", "c", True, False, 256)
+        ts(RR[:, 0:256], a[:, 0:256], M4096, ADD, "a", "RR@", M4096, SUB, 256)
+        tt(KB[:, :], a[:, 256:512], RR[:, 0:256], SUB, "a RR@", "KB@", 256)
+        mm(b[:, 0:16], T.LY[0:2, :], T.ONE[0:2, 0:16], "LY ONE", "b", True, False)
+        for i in range(16):
+            mm(b[:, 0:16], T.LI[:, 15 - i:143 - i], X("land")[:, 256 * t + i:256 * t + 256:16], "LI" + lk, "b", False, i == 15)
+        ts(SM[:, 5, :], b[:, 0:16], M4096, ADD, "b", "r16@", M4096, SUB)
+        ts(E[:, 8, :], KB[:, :], MARK * 219 / 8 - rank / 8 - 2048, EQ, "KB@", "EM@", c=128)
+        mm(c[:, 0:256], W04, E[:, 8, :], "W04 EM@", "c", False, False, 256)
         for h in (0, 1):
-            ts(T.DM8[:, 256 * h:256 * h + 256], T.GB[0:8, :], CC[0:8, 0:1], ALU.is_equal, "GB CC LMF4", "DM8%d" % h, T.LMF[:, 4 + h:5 + h], ALU.mult)
+            tt(SM[64 * h:64 * h + 64, 0, 0:8], b[64 * h:64 * h + 64, h:16:2], SM[64 * h:64 * h + 64, 5, h:16:2], SUB, "b r16@", "BL%d@" % h)
+        tt(SM[:, 6, :], b[:, 0:16], SM[:, 5, :], SUB, "b r16@", "B16@")
+        ts(OS[:, 1, :], SM[:, 6, :], 2047.5, ADD, "B16@", "BU@")
+        for m_ in range(8):
+            ts(E[:, m_, 0:256 - 32 * m_], KB[:, 32 * m_:256], 0.5, ADD, "KB@ BL0@ BL1@", "E%d@" % m_, SM[:, 0, m_:m_ + 1], EQ, max(64, 128 - 16 * m_))
+            if m_ < 7:
+                mm(c[:, 32 * m_ + 32:256], B4, E[:, m_, 32:256 - 32 * m_], "B4 E%d@" % m_, "c", False, False, max(64, 224 - 32 * m_))
+        act(UG[:, :], X("USED")[:, :].indirect(OS[:, 1, :]), AF.Copy, "US@ BU@", "UG@", c=75 + 256 * GATHER)
+        mm(c[:, 0:256], W04, UG[:, :], "W04 UG@", "c", False, False, 256)
+        mm(c[:, 0:256], BW, E[:, 0:8, 0:32], "BW " + " ".join("E%d@" % k for k in range(8)), "c", False, True, 256)
+        P = CS[:, 22:23]
+        do("A", lambda q: q.activation(PK[:, 0, :], c[:, 0:256], AF.Sign, bias=0.0, scale=-1.0, accum_out=P), "c", "KP@ P@", 280)
+        scan(PK[:, 1, :], T.ONE[:, 0:256], PK[:, 0, :], MUL, ADD, "ONE KP@", "PS@", 128)
+        if last:
+            mm(d[:, 0:256], D512, PK[:, 0, :], "D512 KP@", "d", False, True, 256)
+            act(LF[:, :], d[:, 0:256], AF.Relu, "d", "LF@", c=256)
+        else:
+            ts(X("WI")[:, :], P, F[:, 4:5], MUL, "P@ a0@ b0@", "w0@", F[:, 5:6], ADD)
+            ts(CS[:, 2:3], X("WI")[:, :], 2.0, MUL, "w0@ SB%d@" % (t + 1), "Ct@", ST[:, t + 1, 5:6], ADD)
+            ts(CS[:, 1:2], X("WI")[:, :], ST[:, t + 1, 4:5], ADD, "w0@ SA%d@" % (t + 1), "Cl@")
+            lin("A", CS[:, 10:11], P, 1.0 / 8192, CS[:, 9:10], "P@ T4b@ TB@", "T4@")
+            for q in (0, 1):
+                lin("A", CS[:, 12 + q:13 + q], P, MQ[:, 4 + t, 4 * t + 4 + q:4 * t + 5 + q], ST[:, t + 1, q:q + 1], "P@ SV%d@ CF%d" % (t + 1, 4 + t), "VL%d@" % q)
+        for i in range(16):
+            mm(b[:, 32:64], T.LP[:, 15 - i:143 - i], PK[:, :, i:256:16], "LP KP@ PS@", "b", i == 0, i == 15)
+        tt(SM[:, 1, :], b[:, 32:48], T.WJ[:, :], MUL, "b WJ", "D1@")
+        tt(SM[:, 2, :], b[:, 48:64], SM[:, 1, :], ADD, "b D1@", "D2@")
+        ts(OS[:, 2, :], SM[:, 2, :], 0.5, MUL, "D2@ TB@", "DU@", CS[:, 11:12], ADD)
+        cp(X("bank")[:, B:B + 256 * t + 256].indirect(OS[:, 2, :]), LF[:, :], "LF@ DU@" + (" bz1@ bz2@" if t else ""), "bk@", 50 + 256 * SCATTER)
+        if last:
+            return
+        for h in (0, 1):
+            tt(SM[64 * h:64 * h + 64, 3, 0:8], b[64 * h:64 * h + 64, 32 + h:48:2], T.ND[64 * h:64 * h + 64, :], MUL, "b ND", "E1%d@" % h)
+        tt(SM[:, 4, 0:8], SM[:, 3, 0:8], SM[:, 0, 0:8], ALU.max, "E10@ E11@ BL0@ BL1@", "Em@")
+        ts(OS[:, 3, 0:8], SM[:, 4, 0:8], 2047.5, ADD, "Em@", "EU@")
+        cp(X("USED")[:, :].indirect(OS[:, 3, 0:8]), T.ONE[:, 0:128], "EU@ ONE", "US@", 50 + 128 * SCATTER)
+        if t < 2:
+            act(CS[:, 14:15], P, AF.Copy, "P@", "nf@", 0.5, 128.0)
+            act(CS[:, 16:18], F[:, 6:8], AF.Copy, "nf@ F12@ p3@", "x12@", CS[:, 14:15], HALF)
+            ts(CS[:, 18:20], CS[:, 16:18], M1, ADD, "x12@ p3@", "w12@", M1, SUB)
+            act(UP[:, t + 2:4, 0:4], MQ[:, 4 + t, 4 * t + 8:16], AF.Copy, "P@ CF%d" % (4 + t), "UP@", P)
+            for u in range(t + 2, 4):
+                k = u - t - 1
+                act(UP[:, u, 4:6], T.KN[:, :, 4 * u + k], AF.Copy, "KN0 KN1 w12@", "UP%d@" % u, CS[:, 17 + k:18 + k])
+            tt(ST[:, t + 2:4, :], ST[:, t + 2:4, :], UP[:, t + 2:4, :], ADD, "UP@ UP2@ UP3@", " ".join("S%s%d@" % (k, u) for k in "VAB" for u in range(t + 2, 4)))
 
-    def h2():
-        ms(T.RS[:, :], 1.0, "RS")
-        ms(T.RSS[:, :], 1.0, "RSS")
-        ms(T.ZERO[:, :], 0.0, "ZERO")
-        ms(T.RS[:, 0:512:32], 0.0, "RS")
-        ms(T.RSS[:, 0:144:9], 0.0, "RSS")
-        ms(T.K[:, 4096:4112], -32.0, "kinv")
-        cp(T.OC[:, :], T.IR[:, 0:16], "IR", "OC")
-        ts(T.MSK[:, :], T.I9[:, :], col["p8"], ALU.is_equal, "I9 CC", "MSK")
-        ts(T.MI[:, :], T.IF[:, :], col["c16"], ALU.is_equal, "IF CC", "MI")
-        ts(T.RP[:, :], T.IR[:, 0:8], col["p8"], ALU.is_equal, "IR CC", "RP")
-        ts(T.W0C[:, :], T.IR[:, 0:8], col["grp"], ALU.is_equal, "IR CC CCi", "W0C", col["i0"], ALU.mult)
-    build(0, h0, h1)
-    mm(T.b1[:, :], T.ONEF[0:8, :], T.DM8[:, :], "ONEF DM80 DM81", "b1")
-    act(T.MIDT[:, :], T.b1[:, 0:256], AF.Copy, "b1", "MIDT")
-    act(T.HALF[:, :], T.b1[:, 256:512], AF.Copy, "b1", "HALF")
-    pick(0, h2)
-    for i in range(16):
-        act(T.LI[:, 129 * i:128 * i + 128:16], T.WCP[:, 8:16], AF.Copy, "WCP LI", "LI%d" % i)
-    for i in range(16):
-        act(T.LP[:, 129 * i:128 * i + 128:16], T.W0C[:, :], AF.Copy, "W0C LP", "LP%d" % i)
-    ts(T.WBL[:, :], T.IG[:, :], col["grp"], ALU.is_equal, "IG CC CCw", "WBL", col["wt"], ALU.mult)
-    ts(T.W0[:, :], T.BON[:, :], col["i0"], ALU.mult, "BON CCi", "W0")
-    ts(T.DM[:, :, :], T.I16[:, :, :], col["i"], ALU.is_gt, "I16 CC", "DM")
-    ts(T.JL[:, :], T.JL[:, :], col["i"], ALU.add, "JL CC", "JLx")
-    masks(1)
-    cp(T.RCF[:, 256:1024], T.RC[:, 256:1024], "RC1", "RCF")
-    keep(0)
-    for t in range(1, RO):
-        lists(t)
-        build(t, lambda: None, lambda: None)
-        pick(t, lambda: masks(t + 1) if t + 1 < RO else None)
-        mark(t - 1)
-        keep(t)
-    dma("S", "out", T.y[:, :], T.bankS[:, B:4096], "bk bkz", "out")
-    for t in range(RO):
-        g.wait_ge(T.sem["sent%d" % t], 14)
+    first = []
+    for s in (0, 1):
+        S[0] = s
+        first.append(len(ops))
+        for t in range(RO):
+            lists(t)
+            build(t)
+            pick(t)
+            keep(t)
+        dma("out%d" % s, [(T.y[64 * s:64 * s + 64, :], X("bank")[0:64, B:4096])], "bk@ bz1@ bz2@", "out@")
+
+    n = len(ops)
+    succ, left, level = [[] for _ in ops], [len(o[2]) for o in ops], [0.0] * n
+    for k, o in enumerate(ops):
+        for d in o[2]:
+            succ[d].append(k)
+
+    def gap(d, k):
+        return 0 if (ops[d][0] == ops[k][0] and (ops[d][0] == "P" or not ops[k][2][d]) and not ops[d][5]) else HOP + ops[d][4]
+    for k in range(n - 1, -1, -1):
+        level[k] = ops[k][3] + max([gap(k, j) + level[j] for j in succ[k]] + [ops[k][4] + (LAG if k < first[1] else 0)])
+
+    def place(order, before, wait):
+        start, busy = [0.0] * n, {e: [] for e in eng}
+        for k in order:
+            at, c, row = max([start[d] + ops[d][3] + wait(d, k) for d in before[k]] + [0.0]), ops[k][3], busy[ops[k][0]]
+            i = len(row)
+            while i and row[i - 1][1] > at:
+                i -= 1
+            while i < len(row) and row[i][0] < at + c:
+                at = max(at, row[i][1])
+                i += 1
+            row.insert(i, (at, at + c))
+            start[k] = at
+        return start
+    pred = [list(o[2]) for o in ops]
+    start = place(sorted(range(n), key=lambda k: (-level[k], k)), pred, gap)
+    for _ in range(PASSES):
+        back = place(sorted(range(n), key=lambda k: (-start[k] - ops[k][3], -k)), succ, lambda d, k: gap(k, d))
+        start = place(sorted(range(n), key=lambda k: (-back[k] - ops[k][3], k)), pred, gap)
+    seq = sorted(range(n), key=lambda k: (start[k], k))
+    mark, cnt, seen = {}, {e: 0 for e in eng}, {e: {} for e in eng}
+    for k in seq:
+        e, call, dep, _c, _l, sem = ops[k]
+        need = {}
+        for d, hard in dep.items():
+            if hard and not (e == "P" and ops[d][0] == "P"):
+                need[mark[d][0]] = max(need.get(mark[d][0], 0), mark[d][1])
+        for s_ in sorted(need):
+            if seen[e].get(s_, 0) < need[s_]:
+                eng[e].wait_ge(T.sem[s_], need[s_])
+                seen[e][s_] = need[s_]
+        if sem:
+            call(eng[e])
+            mark[k] = sem
+        else:
+            cnt[e] += 1
+            call(eng[e]).then_inc(T.sem["s" + e], 1)
+            mark[k] = ("s" + e, cnt[e])
+    for s in (0, 1):
+        for t in range(RO):
+            g.wait_ge(T.sem["sent%d%d" % (s, t)], 14)
     for e in ("V", "A", "P", "G"):
         g.wait_ge(T.sem["s" + e], cnt[e])
-    for n in _DMAS:
-        g.wait_ge(T.sem["d_" + n], 16)
+    for o in ops:
+        if o[5] and o[0] == "S":
+            g.wait_ge(T.sem[o[5][0]], o[5][1])

@@ -12,8 +12,10 @@ MID = 1920
 MARK = 74.5
 HALF = -0.5 + 2.0 ** -13
 MODE = "aaca"
-LAG = 14000
+LAG = (12000, 12000, 12000, 12000)
 PASSES = 1
+RQ = "VVAA"
+APP = 1
 ORDER = (0, 1, 3, 2)
 CUT = (2, 1, 1, 1)
 f32, bf, i32, u16, f16 = "float32", "bfloat16", "int32", "uint16", "float16"
@@ -21,18 +23,18 @@ f32, bf, i32, u16, f16 = "float32", "bfloat16", "int32", "uint16", "float16"
 SCRATCH = {}
 _SET = (
     (bf, "bank 4096,K 4112,XG 2048,YG 2048,ZG 2048,FX 2048,V 128,IND 128,DS 256,O 32 32,S4 128,U 32 32,Z 164,EC 256,WN 528,RJ 192,"
-         "send 1024,land 1024,LF 256,E 9 256,PK 2 256,USED 4224"),
+         "send 1024,land 1024,LF 256,E 9 256,PK 256 2"),
     (i32, "R 3 1024,WI 1"),
-    (f32, "F 8,ST 4 6,UP 4 6,CS 24,W 384,SM 8 16"),
+    (f32, "USED 4224,F 8,ST 4 6,UP 4 6,CS 64,W 384,SM 8 16"),
     (u16, "OF 384,OS 4 16"),
     (f16, "KB 256"),
 )
 _ALL = (
     (bf, "ONE 512,MX 15 128,WCP 24,LP 144,MI 176,MH 176,RPM 192,"
-         "LI 144,RS32 256,ZERO 32,PRE 768,GB 128,RI 512,LC 128,LY 128,LN 128,NTH 256,UB 256"),
+         "LI 144,RS32 256,ZERO 32,PRE 768,GB 128,RI 512,LC 128,LY 128,LN 128,NTH 256"),
     (i32, "PID 1,TI 12,NL 4,LM 2,UC 256"),
-    (f32, "CC 48,IR 256,IG 128,IL 128,I64 128,IA 28,IB 28,EQ 6 28,MQ 7 16,T5 160,BS 32,RS5 80,HI 32,KA 16,KC 16,KT 2 16,KN 2 16,W16 16,PB 32,RS4 32,POW 32,Q25 32,"
-          "NLF 4,SL 128,LMF 8,WJ 16,ND 8,I8 192,OCF 12"),
+    (f32, "UB 256,CC 48,IR 256,IG 128,IL 128,I64 128,IA 28,IB 28,EQ 6 28,MQ 7 16,T5 160,BS 32,RS5 80,HI 32,KA 16,KC 16,KT 2 16,KN 2 16,W16 16,PB 32,RS4 32,POW 32,Q25 32,"
+          "NLF 4,SL 128,LMF 8,WJ 32,ND 8,I8 192,OCF 12"),
     (u16, "OC 12"),
 )
 for _names, _tab in ((("0", "1"), _SET), (("",), _ALL)):
@@ -69,7 +71,7 @@ def rank_program(g, core, T, topo):
                 dep[d] = True
         for k in w + [k for k in r if k in BANKS]:
             for d in lastw.get(k, ()):
-                dep[d] = True
+                dep[d] = dep.get(d) or k != "q"
             for d in readers.get(k, ()):
                 if ops[d][0] != e or k in w:
                     dep[d] = True
@@ -87,8 +89,8 @@ def rank_program(g, core, T, topo):
     def bank(k):
         return T["b%d" % (4 * S[0] + "abcd".index(k))]
 
-    def dma(name, pairs, r, w, c=2500):
-        do("S", lambda q: [q.dma_start(o, i).then_inc(T.sem["d_" + name], 16) for o, i in pairs], r, w, 60 * len(pairs), c, ("d_" + name, 16 * len(pairs)))
+    def dma(name, pairs, r, w, c=100):
+        do("S", lambda q: [q.dma_start(o, i).then_inc(T.sem["d_" + name], 16) for o, i in pairs], r, w, c, 2200, ("d_" + name, 16 * len(pairs)))
 
     def ts(out, in0, s1, op0, r, w, s2=None, op1=None, c=64):
         if op1 is None:
@@ -130,16 +132,16 @@ def rank_program(g, core, T, topo):
         S[0] = s
         rows = slice(64 * s, 64 * s + 64)
         for k, n in ((1, "rb"), (0, "ra"), (2, "rc")):
-            dma(n + str(s), [(X("R")[0:64, k, 0:256], T[n][rows, 0:256]), (X("R")[64:128, k, 0:255], T[n][rows, 1:256])], "", "R%d0@" % k)
-            if n == "rb":
-                dma("bank%d" % s, [(X("bank")[64 * h:64 * h + 64, 0:B], T.bank[rows, :]) for h in (0, 1)], "", "bk@", 4500)
+            dma(n + str(s), [(X("R")[0:64, k, 0:256], T[n][rows, 0:256]), (X("R")[64:128, k, 0:255], T[n][rows, 1:256])], "", "R%d0@ q" % k, 900)
+        dma("bank%d" % s, [(X("bank")[64 * h:64 * h + 64, 0:B], T.bank[rows, :]) for h in (0, 1)], "", "bk@ q", 3300)
         if s == 0:
-            dma("lim", [(T.LM[8 * h:8 * h + 8, :], T.lim[:, :]) for h in (0, 1)], "", "LM")
+            dma("lim", [(T.LM[8 * h:8 * h + 8, :], T.lim[:, :]) for h in (0, 1)], "", "LM q")
     for s in (0, 1):
         S[0] = s
         rows = slice(64 * s, 64 * s + 64)
-        dma("rl%d" % s, [(X("R")[64 * h:64 * h + 64, k, 256:1024 - h], T[n][rows, 256 + h:1024]) for k, n in enumerate(("ra", "rb", "rc")) for h in (0, 1)], "bk1", "R01@ R11@ R21@", 6000)
-    dma("uc", [(T.UC[:, :], T.used[:, :])], "bk1", "UC")
+        dma("rl%d" % s, [(X("R")[64 * h:64 * h + 64, k, 256:1024 - h], T[n][rows, 256 + h:1024]) for k, n in enumerate(("ra", "rb", "rc")) for h in (0, 1)], "", "R01@ R11@ R21@ q", 5600)
+        if s == 0:
+            dma("uc", [(T.UC[:, :], T.used[:, :])], "", "UC q", 900)
     cp(T.UB[:, :], T.UC[:, :], "UC", "UB", 256)
 
     iota(T.PID[:, :], [[1, 1]], "PID", 1)
@@ -154,7 +156,8 @@ def rank_program(g, core, T, topo):
     iota(T.GB[0:16, :], [[1, 4], [0, 32]], "GB")
     iota(T.I8[:, :], [[0, 24], [1, 8]], "I8")
     iota(T.OCF[:, :], [[0, 3], [1, 4]], "OCF")
-    iota(T.WJ[:, :], [[16, 16]], "WJ0", 0, -256)
+    iota(T.WJ[:, 1:32:2], [[16, 16]], "WJ0", 0, -256)
+    iota(T.WJ[:, 0:32:2], [[0, 16]], "WJz")
     iota(T.ND[:, :], [[-16, 8]], "ND0", 0, -2048)
     iota(T.ZERO[:, :], [[0, 32]], "ZERO")
     ms(T.ONE[:, :], 1.0, "ONE", 256)
@@ -174,7 +177,7 @@ def rank_program(g, core, T, topo):
 
     CC = T.CC
     names = ["pid", "i", "m", "typ", "g", "h", "p8", "c32", "p64", "p4", "q8", "b3", "wt", "w8", "l", "sg", "off", "nsg", "sg4", "tm", "i0", "n7", "h1", "hs", "pv0", "pv1", "lpc", "mic",
-             "pw", "mk", "cP", "t0", "t1", "G8", "pt", "pts", "r0", "hc", "G0", "G1", "lic"]
+             "pw", "mk", "cP", "t0", "t1", "G8", "pt", "pts", "r0", "hc", "G0", "G1", "lic", "s256", "k63"]
     col = {n: CC[:, k:k + 1] for k, n in enumerate(names)}
     for k, (sh, an) in enumerate([(0, 255), (0, 15), (1, 7), (0, 1), (4, 3), (6, 1), (0, 7), (0, 31), (0, 63), (5, 3), (4, 7), (3, 1)]):
         ts(T.TI[:, k:k + 1], T.PID[:, :], sh, ALU.arith_shift_right, "PID", "TI%d" % k, an, ALU.bitwise_and)
@@ -187,7 +190,7 @@ def rank_program(g, core, T, topo):
         else:
             ts(col[n], col[src], a, MUL, "CC c" + src, "c" + n, b, ADD)
     for x in (("wt", "i", 14.0, 9.0), ("w8", "i", 14 / 8, 9 / 8), ("sg", "typ", 2.0, -1.0), ("off", "typ", 2.0 ** -12, -2.0 ** -12), ("nsg", "typ", -2.0, 1.0),
-              ("sg4", "typ", 2.0 / 4096, -1.0 / 4096), ("tm", "typ", 1.0 / 128, -1.0 / 128), ("h1", "h", -1.0, 1.0), ("hs", "h", -2.0, 1.0), ("pv0", "p4", 1.0, -3.875),
+              ("sg4", "typ", 2.0 / 4096, -1.0 / 4096), ("tm", "typ", 1.0 / 128, -0.5 - 0.5 / 4096), ("s256", "typ", 2.0 / 256, -1.0 / 256), ("k63", "typ", -1.0 / 128, -512 + 1.0 / 128), ("h1", "h", -1.0, 1.0), ("hs", "h", -2.0, 1.0), ("pv0", "p4", 1.0, -3.875),
               ("pv1", "p4", 1.0, 0.125), ("mic", "i", 1.0, 48.0), ("hc", "b3", 4.0, 0.0), ("lic", "g", 16.0, 15.0)):
         cl(*x)
     lin("A", col["l"], col["h"], 16.0, col["i"], "CC", "cl")
@@ -196,10 +199,11 @@ def rank_program(g, core, T, topo):
     ts(col["t0"], col["m"], 0.0, ALU.not_equal, "CC cn7", "ct0", col["n7"], MUL)
     cl("cP", "t0", 256.0, -256.0)
     ts(BON, T.IG[:, :], col["g"], EQ, "IG CC", "BON", c=128)
-    ts(T.IL[:, :], T.IL[:, :], col["sg4"], MUL, "IL csg4", "ITF", 1.0, ADD, 128)
+    ts(T.IL[:, :], T.IL[:, :], col["sg4"], MUL, "IL csg4", "ITF", 512.0, ADD, 128)
     tt(T.IL[:, :], T.IL[:, :], BON, MUL, "ITF BON", "ITF", 256)
-    ts(IT, T.IL[:, :], -1.0, ADD, "ITF", "IT", c=128)
-    act(COLT, T.IR[:, 0:128], AF.Identity, "IR ctm", "COLT", 1.0 / 128, col["tm"], 128)
+    lin("A", T.IL[:, :], T.IL[:, :], 1.0, col["k63"], "ITF ck63", "IT", 128)
+    ts(FOLD, T.I64[:, :], col["p64"], EQ, "I64 CD", "FOLD", c=128)
+    act(T.I64[:, :], T.IR[:, 0:128], AF.Identity, "IR ctm", "COLT I64", 1.0 / 128, col["tm"], 128)
     ms(T.RI[0:3, 0:256], 0.0, "RIa", 128)
     ms(T.RI[0:3, 256:512], 1.0, "RI", 128)
     for n, x in ((3, 2.0 ** -13), (2, -float(MID)), (1, -0.5)):
@@ -234,7 +238,7 @@ def rank_program(g, core, T, topo):
     ts(E6[:, 5, 16:28], E6[:, 5, 16:28], col["r0"], MUL, "E5 E0 cr0", "E5")
     tt(MQ[:, 4:7, 3:16:4], MQ[:, 4:7, 3:16:4], E6[:, 5, 16:28], ADD, "MQ3 E5 HI", "MQn")
     for a in (4, 5, 6):
-        ts(MQ[:, a, :], MQ[:, a, :], col["h" if a % 2 == 0 else "h1"], MUL, MQk + " MQn HI CC ch1", "CF%d" % a, 0.5, MUL)
+        ts(MQ[:, a, :], MQ[:, a, :], col["h" if a % 2 == 0 else "h1"], MUL, MQk + " MQn HI CC ch1", "CF%d" % a, 0.25, MUL)
         for q in (0, 1):
             act(MQ[:, a, q:16:4], MQ[:, a, q:16:4], AF.Copy, "CF%d" % a, "CF%d" % a, 1.0 / 4096)
     ts(T.KN[:, 0, :], T.KA[:, :], m, ALU.is_lt, "KA CC cn7", "KN0", col["n7"], MUL)
@@ -242,6 +246,8 @@ def rank_program(g, core, T, topo):
     tt(T.W16[:, :], T.KA[:, :], T.KC[:, :], ALU.not_equal, "KA KC", "NE")
     tt(T.KN[:, 1, :], T.KN[:, 1, :], T.W16[:, :], MUL, "KN1 NE", "KN1")
     tt(T.KN[:, 0, :], T.KN[:, 0, :], T.KN[:, 1, :], ADD, "KN0 KN1", "KN0")
+    ts(T.KN[:, 1, :], T.W16[:, :], 0.5, MUL, "NE", "KN1", 0.5, ADD)
+    tt(T.KN[:, 0, :], T.KN[:, 1, :], T.KN[:, 0, :], SUB, "KN0 KN1", "KN0")
     ts(T.KN[:, 1, :], T.W16[:, :], 1.0, ADD, "NE", "KN1")
     act(T.KT[:, :, :], T.KN[:, :, :], AF.Copy, "KN0 KN1", "KT", 1.0 / 4096)
     ms(T.RS5[:, :], 1.0, "RS5", 80)
@@ -264,7 +270,8 @@ def rank_program(g, core, T, topo):
         act(T.HI[:, o], base, AF.Copy, "W@ CC T5c0 T5c1 MQn", "T5h@", col["h"])
         ts(T.BS[:, o], T.BS[:, o], col["hs"], MUL, "BS@ chs", "BS@")
         tt(ST[:, :, 0:4], T.BS[:, o], T.HI[:, o], ADD, "BS@ T5h@", "ST@")
-        ts(ST[:, :, 0:2], ST[:, :, 0:2], 1.0 / 4096, MUL, "ST@", "ST@ SV0@ SV1@ SV2@ SV3@")
+        ts(ST[:, :, 0:2], ST[:, :, 0:2], 0.5 / 4096, MUL, "ST@", "STa@")
+        ts(ST[:, :, 2:4], ST[:, :, 2:4], 0.5, MUL, "ST@ STa@", "SV0@ SV1@ SV2@ SV3@")
         ts(CS[:, 16:20], F[:, 0:4], F[:, 3:4], MUL, "F@", "p3@", -2047.5, ADD)
         ts(CS[:, 20:22], F[:, 1:3], F[:, 2:3], MUL, "F@", "p2@", -2047.5, ADD)
         ts(T.W16[:, 0:16:5], CS[:, 16:20], M4096, ADD, "p3@ W16", "W16a", M4096, SUB)
@@ -273,10 +280,9 @@ def rank_program(g, core, T, topo):
             tt(T.PB[:, 16 * k:16 * k + 16], T.KT[:, k, :], T.W16[:, :], MUL, "KT W16a W16b", "PB%d" % k)
         PB = X("W")
         scan(PB[:, 256:288], T.RS4[:, :], T.PB[:, :], MUL, ADD, "RS4 PB0 PB1", "Wz@")
-        ts(CS[:, 1:2], PB[:, 259:260], col["cP"], ADD, "Wz@ ccP", "Cl@")
         cp(CS[:, 2:3], PB[:, 275:276], "Wz@", "Ct@")
         act(ST[:, :, 5], PB[:, 275:288:4], AF.Copy, "Wz@", "SB1@ SB2@ SB3@")
-        lin("A", ST[:, :, 4], PB[:, 259:272:4], 1.0, col["cP"], "Wz@ ccP", "SA1@ SA2@ SA3@")
+        ts(ST[:, :, 4], PB[:, 259:272:4], col["cP"], SUB, "Wz@ ccP", "SA0@ SA1@ SA2@ SA3@")
         act(F[:, 4:5], F[:, 0:1], AF.Copy, "F@", "a0@", 1.0 / 8192)
         act(F[:, 5:6], F[:, 0:1], AF.Copy, "F@", "b0@", 1.0 / 32, HALF)
         act(F[:, 6:8], F[:, 1:3], AF.Copy, "F@", "F12@", 1.0 / 4096)
@@ -302,7 +308,6 @@ def rank_program(g, core, T, topo):
         ts(CC[0:16, 38 + s:39 + s], CC[0:16, 6:7], -4.0 * s, ADD, "CD", "cG%d" % s)
         for k in range(3):
             ts(T.PRE[0:16, 384 * s + 128 * k:384 * s + 128 * k + 128], T.GB[0:16, :], CC[0:16, 38 + s:39 + s], EQ, "GB LM4 LM6 cG%d" % s, "PRE%d%d" % (k, s), LMF[0:16, 4 + k:5 + k], MUL)
-    ts(FOLD, T.I64[:, :], col["p64"], EQ, "I64 CD", "FOLD", c=128)
     ts(W8, BON, col["w8"], MUL, "BON cw8", "W8")
     ts(B4, BON, 4.0, MUL, "BON", "B4")
     ts(W04, BON, col["i0"], MUL, "BON ci0", "W04", 4.0, MUL)
@@ -332,7 +337,7 @@ def rank_program(g, core, T, topo):
         ts(T.OC[:, 4 * k:4 * k + 4], T.OCF[:, 4 * k:4 * k + 4], x, MUL, "OCF", "OC%d" % k, y, ADD)
     ms(T.RS32[:, :], 1.0, "RS32", 128)
     ms(T.RS32[:, 0:256:32], 0.0, "RS32")
-    ts(T.WJ[:, :], T.WJ[:, :], col["i"], ADD, "WJ0 CC", "WJ")
+    ts(T.WJ[:, 1:32:2], T.WJ[:, 1:32:2], col["i"], ADD, "WJ0 CC", "WJ")
     ts(T.ND[:, :], T.ND[:, :], col["i"], SUB, "ND0 CC", "ND", -0.5, ADD)
     ts(col["G8"], col["l"], 31.0, EQ, "cl", "cG8", MARK, MUL)
     for s in (0, 1):
@@ -344,28 +349,27 @@ def rank_program(g, core, T, topo):
     def lists(t):
         CS, ST, W, OF, R, d = X("CS"), X("ST"), X("W"), X("OF"), X("R"), bank("d")
         k, c = "%d@" % (t > 0), slice(256 * t, 256 * t + 256, 2)
-        cl_, ct = CS[:, 1:2], CS[:, 2:3]
+        cl_, ct = ST[:, t, 4:5], CS[:, 2:3]
+        lin("A", CS[:, 4:5], cl_, col["sg"], col["off"], "SA%d@ csg coff" % t, "SC@")
         mm(d[:, :], T.LC[0:3, :], T.RI[0:3, :], "LC RI RIa", "d", True, False, 512)
-        do("V", lambda v: v.reciprocal(CS[:, 3:4], ct), "Ct@", "rc@", 240)
-        lin("A", CS[:, 6:7], ct, -0.484375 / 128, cl_, "Cl@ Ct@", "c1@")
-        lin("A", CS[:, 4:5], cl_, col["nsg"], col["off"], "Cl@ cnsg coff", "SC@")
-        act(CS[:, 5:6], ct, AF.Copy, "Ct@ cnsg", "NC@", col["nsg"])
-        ts(CS[:, 0:1], CS[:, 6:7], CS[:, 3:4], MUL, "c1@ rc@", "cb@", M7, ADD)
-        lin("A", W[:, 0:128], IT, ct, CS[:, 4:5], "IT Ct@ SC@", "W@", 128)
-        ts(CS[:, 8:9], CS[:, 0:1], M7, SUB, "cb@ NC@", "X@", CS[:, 5:6], MUL)
-        ts(CS[:, 7:8], CS[:, 0:1], M7, SUB, "cb@", "c2@")
+        sign = X("V")[:, :]
+        do("A", lambda q: q.activation(sign, T.I64[:, :], AF.Sign, bias=cl_, scale=ct, accum_out=CS[:, 3:4]), "COLT Ct@ SA%d@" % t, "V@ ac@", 150)
+        lin("A", W[:, 0:128], T.IL[:, :], ct, CS[:, 4:5], "IT Ct@ SC@", "W@", 128)
+        ts(CS[:, 8:9], CS[:, 3:4], ct, MUL, "ac@ Ct@ cs256", "X@", col["s256"], MUL)
         ts(X("IND")[:, :], W[:, 0:128], CS[:, 8:9], ALU.is_ge, "W@ X@", "IND@", c=128)
         for q in range(4):
             val = CS[:, 12 + q:13 + q] if t and q < 2 else ST[:, t, q:q + 1]
-            ts(X("ZG")[:, 128 * q:128 * q + 128], COLT, CS[:, 7:8], ALU.is_ge, "COLT c2@ SV%d@ VL%d@" % (t, q), "RQ%d@" % q, val, MUL)
-        mm(d[:, 0:256], X("IND")[:, :], X("ZG")[:, 0:256], "IND@ RQ0@ RQ1@", "d", False, False, 256)
-        mm(d[:, 256:512], X("IND")[:, :], X("ZG")[:, 256:512], "IND@ RQ2@ RQ3@", "d", False, True, 256)
+            lin(RQ[q], X("XG")[:, 128 * q:128 * q + 128], X("V")[:, :], val, val, "V@ SV%d@ VL%d@" % (t, q), "RQ%d@" % q, 128 if RQ[q] == "A" else 64)
+        mm(d[:, 0:256], X("IND")[:, :], X("XG")[:, 0:256], "IND@ RQ0@ RQ1@", "d", False, False, 256)
+        mm(d[:, 256:512], X("IND")[:, :], X("XG")[:, 256:512], "IND@ RQ2@ RQ3@", "d", False, True, 256)
         ts(W[:, 256:384], R[:, 2, c], CS[:, 10:11], MUL, "R2" + k + " T4@", "Wz@", HALF - MID, ADD, 128)
         ts(OF[:, 256:384], W[:, 256:384], M1, ADD, "Wz@", "OZ@", M1 - MID, SUB, 128)
-        tt(W[:, 0:256], d[:, 0:256], R[:, 0:2, c], MUL, "d R0" + k + " R1" + k, "W@", 256)
-        tt(W[:, 0:256], W[:, 0:256], d[:, 256:512], ADD, "W@ d", "W@", 256)
-        ts(OF[:, 128:256], W[:, 128:256], M1, ADD, "W@", "OY@", M1 - MID, SUB, 128)
-        ts(OF[:, 0:128], W[:, 0:128], M1, ADD, "W@", "OX@", M1 - MID, SUB, 128)
+        for n, w_ in ((0, "W@"), (1, "Wy@")):
+            tt(W[:, 128 * n:128 * n + 128], d[:, 128 * n:128 * n + 128], R[:, n, c], MUL, "d R%d" % n + k, w_, 128)
+        for n, w_ in ((0, "W@"), (1, "Wy@")):
+            tt(W[:, 128 * n:128 * n + 128], W[:, 128 * n:128 * n + 128], d[:, 256 + 128 * n:384 + 128 * n], ADD, "d " + w_, w_, 128)
+        for n, w_ in ((0, "W@"), (1, "Wy@")):
+            ts(OF[:, 128 * n:128 * n + 128], W[:, 128 * n:128 * n + 128], M1, ADD, w_, ("OX@", "OY@")[n], M1 - MID, SUB, 128)
 
     def pieces(q):
         return [(p, 512 // CUT[q]) for p in range(0, 512, 512 // CUT[q])]
@@ -383,7 +387,10 @@ def rank_program(g, core, T, topo):
                 o, k = 512 * q + p, "%d%d@" % (q, p)
                 c, ko = slice(o, o + PIECE), K[:, 2 * o + 1:2 * (o + PIECE):2]
                 x, y, z = [win.indirect(OF[:, b + o // 16:b + (o + PIECE) // 16]) for b in (0, 128, 256)]
-                act(YG[:, c], y, AF.Copy, "OY@" + bk, "YG" + k, c=gc_)
+                ky, kz = "OY@", "OZ@"
+                if q == 0:
+                    y, z, ky, kz = z, y, kz, ky
+                act(YG[:, c], y, AF.Copy, ky + bk, "YG" + k, c=gc_)
                 if mode == "a":
                     tt(FX[:, c], x, YG[:, c], op, "OX@ YG" + k + bk, "FX" + k, gc_)
                 else:
@@ -405,7 +412,7 @@ def rank_program(g, core, T, topo):
                     act(ZG[:, c], z, AF.Copy, "OZ@" + bk, "ZG" + k, c=gc_)
                     tt(ko, pb, ZG[:, c], ALU.min, b + " ZG" + k, "K" + k, PIECE)
                 else:
-                    tt(ko, z, FX[:, c], ALU.min, "OZ@ FX" + k + bk, "K" + k, gc_)
+                    tt(ko, z, FX[:, c], ALU.min, kz + " FX" + k + bk, "K" + k, gc_)
             for b_ in range(16):
                 kq, kk = K[:, 1024 * q + 2 * b_ + 1:1024 * q + 1024:32], " ".join("K%d%d@" % (q, p) for p, _ in pieces(q))
                 mm(a[32 * q:32 * q + 32, b_:256:16], kq, T.WCP[:, 0:16], "WCa WCb WCc " + kk, "a", False, b_ == 15, 32)
@@ -414,8 +421,10 @@ def rank_program(g, core, T, topo):
                 mm(bank("d")[32 * q:32 * q + 32, b_:128:16], kq, T.WCP[:, 16:24], "WCP " + kk, "d", False, b_ == 15, 32)
         for e in "VA":
             row = [k for k in range(n0, len(ops)) if ops[k][0] == e and ops[k][3] > 70 + GATHER * 100 and ops[k][3] not in (256, 512)]
+            if e == "V":
+                row = row[0:1] + [k for x, z in zip(row[2::2], row[1::2]) for k in (x, z)] + row[-1:]
             for k, j in zip(row, row[1:]):
-                ops[j][2].setdefault(k, False)
+                late.append((k, j))
 
     def pick(t):
         a, b, c, d = [bank(k) for k in "abcd"]
@@ -478,7 +487,7 @@ def rank_program(g, core, T, topo):
         act(CS[:, 11:12], CS[:, 10:11], AF.Copy, "T4@", "TB@", 4096.0, 127.5 - B)
         act(CS[:, 9:10], CS[:, 10:11], AF.Copy, "T4@", "T4b@", 1.0, 1.0 / 32)
         mm(a[:, :], T.LY[0:2, :], T.ONE[0:2, :], "LY ONE", "a", True, False, 512)
-        mm(a[:, :], T.LC[0:1, :], T.RI[0:1, :], "LC RI RIa", "a", False, False, 512)
+        mm(a[:, 256:512], T.LC[0:1, :], T.ONE[0:1, 0:256], "LC ONE", "a", False, False, 256)
         mm(a[:, 0:256], W8, lnd, "W8" + lk, "a", False, False, 256)
         mm(a[:, 256:512], W8, lnd, "W8" + lk, "a", False, True, 256)
         if last:
@@ -487,51 +496,53 @@ def rank_program(g, core, T, topo):
         if not last:
             act(LF[:, :], d[:, 0:256], AF.Copy, "d", "LF@", c=256)
         mm(c[:, 0:256], T.ONE[0:1, 0:128], T.NTH[0:1, :], "ONE NTH", "c", True, False, 256)
-        ts(RR[:, 0:256], a[:, 0:256], M4096, ADD, "a", "RR@", M4096, SUB, 256)
-        tt(KB[:, :], a[:, 256:512], RR[:, 0:256], SUB, "a RR@", "KB@", 256)
+        for h, w_ in ((1, "Wy@"), (0, "W@")):
+            ts(RR[:, 128 * h:128 * h + 128], a[:, 128 * h:128 * h + 128], M4096, ADD, "a", w_, M4096, SUB, 128)
+        for h, w_ in ((1, "Wy@"), (0, "W@")):
+            tt(KB[:, 128 * h:128 * h + 128], a[:, 256 + 128 * h:384 + 128 * h], RR[:, 128 * h:128 * h + 128], SUB, "a " + w_, "KB%d@" % h, 128)
         mm(b[:, 0:16], T.LY[0:2, :], T.ONE[0:2, 0:16], "LY ONE", "b", True, False)
         for i in range(16):
             mm(b[:, 0:16], T.LI[:, 15 - i:143 - i], X("land")[:, 256 * t + i:256 * t + 256:16], "LI" + lk, "b", False, i == 15)
         ts(SM[:, 5, :], b[:, 0:16], M4096, ADD, "b", "r16@", M4096, SUB)
-        ts(E[:, 8, :], KB[:, :], MARK * 219 / 8 - rank / 8 - 2048, EQ, "KB@", "EM@", c=128)
+        ts(E[:, 8, :], KB[:, :], MARK * 219 / 8 - rank / 8 - 2048, EQ, "KB0@ KB1@", "EM@", c=128)
         mm(c[:, 0:256], W04, E[:, 8, :], "W04 EM@", "c", False, False, 256)
         for h in (0, 1):
             tt(SM[64 * h:64 * h + 64, 0, 0:8], b[64 * h:64 * h + 64, h:16:2], SM[64 * h:64 * h + 64, 5, h:16:2], SUB, "b r16@", "BL%d@" % h)
         tt(SM[:, 6, :], b[:, 0:16], SM[:, 5, :], SUB, "b r16@", "B16@")
         ts(OS[:, 1, :], SM[:, 6, :], 2047.5, ADD, "B16@", "BU@")
         for m_ in range(8):
-            ts(E[:, m_, 0:256 - 32 * m_], KB[:, 32 * m_:256], 0.5, ADD, "KB@ BL0@ BL1@", "E%d@" % m_, SM[:, 0, m_:m_ + 1], EQ, max(64, 128 - 16 * m_))
+            ts(E[:, m_, 0:256 - 32 * m_], KB[:, 32 * m_:256], 0.5, ADD, "KB1@ BL0@ BL1@" + (" KB0@" if m_ < 4 else ""), "E%d@" % m_, SM[:, 0, m_:m_ + 1], EQ, max(64, 128 - 16 * m_))
             if m_ < 7:
                 mm(c[:, 32 * m_ + 32:256], B4, E[:, m_, 32:256 - 32 * m_], "B4 E%d@" % m_, "c", False, False, max(64, 224 - 32 * m_))
         act(UG[:, :], X("USED")[:, :].indirect(OS[:, 1, :]), AF.Copy, "US@ BU@", "UG@", c=75 + 256 * GATHER)
         mm(c[:, 0:256], W04, UG[:, :], "W04 UG@", "c", False, False, 256)
         mm(c[:, 0:256], BW, E[:, 0:8, 0:32], "BW " + " ".join("E%d@" % k for k in range(8)), "c", False, True, 256)
         P = CS[:, 22:23]
-        do("A", lambda q: q.activation(PK[:, 0, :], c[:, 0:256], AF.Sign, bias=0.0, scale=-1.0, accum_out=P), "c", "KP@ P@", 280)
-        scan(PK[:, 1, :], T.ONE[:, 0:256], PK[:, 0, :], MUL, ADD, "ONE KP@", "PS@", 128)
+        do("A", lambda q: q.activation(PK[:, :, 0], c[:, 0:256], AF.Sign, bias=0.0, scale=-1.0, accum_out=P), "c", "KP@ P@", 280)
+        scan(PK[:, :, 1], T.ONE[:, 0:256], PK[:, :, 0], MUL, ADD, "ONE KP@", "PS@", 128)
         if last:
-            mm(d[:, 0:256], D512, PK[:, 0, :], "D512 KP@", "d", False, True, 256)
+            mm(d[:, 0:256], D512, PK[:, :, 0], "D512 KP@", "d", False, True, 256)
             act(LF[:, :], d[:, 0:256], AF.Relu, "d", "LF@", c=256)
         else:
             ts(X("WI")[:, :], P, F[:, 4:5], MUL, "P@ a0@ b0@", "w0@", F[:, 5:6], ADD)
             ts(CS[:, 2:3], X("WI")[:, :], 2.0, MUL, "w0@ SB%d@" % (t + 1), "Ct@", ST[:, t + 1, 5:6], ADD)
-            ts(CS[:, 1:2], X("WI")[:, :], ST[:, t + 1, 4:5], ADD, "w0@ SA%d@" % (t + 1), "Cl@")
             lin("A", CS[:, 10:11], P, 1.0 / 8192, CS[:, 9:10], "P@ T4b@ TB@", "T4@")
             for q in (0, 1):
                 lin("A", CS[:, 12 + q:13 + q], P, MQ[:, 4 + t, 4 * t + 4 + q:4 * t + 5 + q], ST[:, t + 1, q:q + 1], "P@ SV%d@ CF%d" % (t + 1, 4 + t), "VL%d@" % q)
         for i in range(16):
-            mm(b[:, 32:64], T.LP[:, 15 - i:143 - i], PK[:, :, i:256:16], "LP KP@ PS@", "b", i == 0, i == 15)
-        tt(SM[:, 1, :], b[:, 32:48], T.WJ[:, :], MUL, "b WJ", "D1@")
-        tt(SM[:, 2, :], b[:, 48:64], SM[:, 1, :], ADD, "b D1@", "D2@")
-        ts(OS[:, 2, :], SM[:, 2, :], 0.5, MUL, "D2@ TB@", "DU@", CS[:, 11:12], ADD)
-        cp(X("bank")[:, B:B + 256 * t + 256].indirect(OS[:, 2, :]), LF[:, :], "LF@ DU@" + (" bz1@ bz2@" if t else ""), "bk@", 50 + 256 * SCATTER)
+            mm(b[:, 32:64], T.LP[:, 15 - i:143 - i], PK[:, i:256:16, :], "LP KP@ PS@", "b", i == 0, i == 15)
+        scan(CS[:, 32:64], T.WJ[:, :], b[:, 32:64], MUL, ADD, "b WJ WJz", "D2@")
+        ts(OS[:, 2, :], CS[:, 33:64:2], 0.5, MUL, "D2@ TB@", "DU@", CS[:, 11:12], ADD)
+        for k in range(0, 16, 16 // APP):
+            cp(X("bank")[:, B:B + 256 * t + 256].indirect(OS[:, 2, k:k + 16 // APP]), LF[:, 16 * k:16 * k + 256 // APP], "LF@ DU@" + (" bz1@ bz2@" if t else ""), "bk@", 60 + 256 // APP * SCATTER)
         if last:
             return
         for h in (0, 1):
-            tt(SM[64 * h:64 * h + 64, 3, 0:8], b[64 * h:64 * h + 64, 32 + h:48:2], T.ND[64 * h:64 * h + 64, :], MUL, "b ND", "E1%d@" % h)
+            tt(SM[64 * h:64 * h + 64, 3, 0:8], b[64 * h:64 * h + 64, 32 + 2 * h:64:4], T.ND[64 * h:64 * h + 64, :], MUL, "b ND", "E1%d@" % h)
         tt(SM[:, 4, 0:8], SM[:, 3, 0:8], SM[:, 0, 0:8], ALU.max, "E10@ E11@ BL0@ BL1@", "Em@")
         ts(OS[:, 3, 0:8], SM[:, 4, 0:8], 2047.5, ADD, "Em@", "EU@")
-        cp(X("USED")[:, :].indirect(OS[:, 3, 0:8]), T.ONE[:, 0:128], "EU@ ONE", "US@", 50 + 128 * SCATTER)
+        taken = X("USED")[:, :].indirect(OS[:, 3, 0:8])
+        do("A", lambda q: q.activation(taken, T.IR[:, 128:256], AF.Sigmoid), "EU@ IR", "US@", 80 + 128 * SCATTER + (1600 if t + S[0] == 0 else 0))
         if t < 2:
             act(CS[:, 14:15], P, AF.Copy, "P@", "nf@", 0.5, 128.0)
             act(CS[:, 16:18], F[:, 6:8], AF.Copy, "nf@ F12@ p3@", "x12@", CS[:, 14:15], HALF)
@@ -542,7 +553,7 @@ def rank_program(g, core, T, topo):
                 act(UP[:, u, 4:6], T.KN[:, :, 4 * u + k], AF.Copy, "KN0 KN1 w12@", "UP%d@" % u, CS[:, 17 + k:18 + k])
             tt(ST[:, t + 2:4, :], ST[:, t + 2:4, :], UP[:, t + 2:4, :], ADD, "UP@ UP2@ UP3@", " ".join("S%s%d@" % (k, u) for k in "VAB" for u in range(t + 2, 4)))
 
-    first = []
+    first, more, late = [], {}, []
     for s in (0, 1):
         S[0] = s
         first.append(len(ops))
@@ -550,19 +561,28 @@ def rank_program(g, core, T, topo):
             lists(t)
             build(t)
             pick(t)
+            more[len(ops) - 2] = (LAG[t + 1] - LAG[t] if s else 0) if t < 3 else 0
             keep(t)
-        dma("out%d" % s, [(T.y[64 * s:64 * s + 64, :], X("bank")[0:64, B:4096])], "bk@ bz1@ bz2@", "out@")
+        dma("out%d" % s, [(T.y[64 * s:64 * s + 64, :], X("bank")[0:64, B:4096])], "bk@ bz1@ bz2@", "out@", 700)
 
     n = len(ops)
-    succ, left, level = [[] for _ in ops], [len(o[2]) for o in ops], [0.0] * n
+    succ, level, lead = [[] for _ in ops], [0.0] * n, [LAG[3] if k < first[1] else 0 for k in range(n)]
+    for k, j in late:
+        ops[j][2].setdefault(k, False)
     for k, o in enumerate(ops):
         for d in o[2]:
             succ[d].append(k)
+    topo_, left = [k for k in range(n) if not ops[k][2]], [len(o[2]) for o in ops]
+    for k in topo_:
+        for j in succ[k]:
+            left[j] -= 1
+            if not left[j]:
+                topo_.append(j)
 
     def gap(d, k):
-        return 0 if (ops[d][0] == ops[k][0] and (ops[d][0] == "P" or not ops[k][2][d]) and not ops[d][5]) else HOP + ops[d][4]
-    for k in range(n - 1, -1, -1):
-        level[k] = ops[k][3] + max([gap(k, j) + level[j] for j in succ[k]] + [ops[k][4] + (LAG if k < first[1] else 0)])
+        return 0 if ops[d][0] == ops[k][0] and (ops[d][0] == "P" or not ops[k][2][d]) else HOP + ops[d][4]
+    for k in topo_[::-1]:
+        level[k] = ops[k][3] + max([gap(k, j) + level[j] for j in succ[k]] + [ops[k][4]]) + (lead[k] if not succ[k] else 0) + more.get(k, 0)
 
     def place(order, before, wait):
         start, busy = [0.0] * n, {e: [] for e in eng}

@@ -11,18 +11,22 @@ M4096 = 1.5 * 2.0 ** 35
 MID = 1920
 MARK = 74.5
 HALF = -0.5 + 2.0 ** -13
-MODE = "aaca"
-LAG = (12000, 12000, 12000, 12000)
-PASSES = 1
-RQ = "VVAA"
+MODE = ("aa", "a", "cc", "a")
+LAG = (14000, 12500, 12500, 12500)
+PASSES = 2
+EARLY = 3000
+DRAIN = 200
+AHEAD = {"pAZv": -1200}
+RQ = "AAAA"
+SQ = "AAAAV"
+ON = "AVVVA"
 APP = 1
 ORDER = (0, 1, 3, 2)
-CUT = (2, 1, 1, 1)
 f32, bf, i32, u16, f16 = "float32", "bfloat16", "int32", "uint16", "float16"
 
 SCRATCH = {}
 _SET = (
-    (bf, "bank 4096,K 4112,XG 2048,YG 2048,ZG 2048,FX 2048,V 128,IND 128,DS 256,O 32 32,S4 128,U 32 32,Z 164,EC 256,WN 528,RJ 192,"
+    (bf, "bank 4096,K 4112,XG 2048,YG 2048,ZG 2048,FX 2048,V 128,IND 128,DS 256,O 32 32,S4 128,U 32 32,Z 32 34,WN 816,RJ 192,"
          "send 1024,land 1024,LF 256,E 9 256,PK 256 2"),
     (i32, "R 3 1024,WI 1"),
     (f32, "USED 4224,F 8,ST 4 6,UP 4 6,CS 64,W 384,SM 8 16"),
@@ -31,7 +35,7 @@ _SET = (
 )
 _ALL = (
     (bf, "ONE 512,MX 15 128,WCP 24,LP 144,MI 176,MH 176,RPM 192,"
-         "LI 144,RS32 256,ZERO 32,PRE 768,GB 128,RI 512,LC 128,LY 128,LN 128,NTH 256"),
+         "LI 144,RS34 306,RS2 64,ZERO 32,PRE 768,GB 384,RI 512,LC 128,LY 256,NTH 256"),
     (i32, "PID 1,TI 12,NL 4,LM 2,UC 256"),
     (f32, "UB 256,CC 48,IR 256,IG 128,IL 128,I64 128,IA 28,IB 28,EQ 6 28,MQ 7 16,T5 160,BS 32,RS5 80,HI 32,KA 16,KC 16,KT 2 16,KN 2 16,W16 16,PB 32,RS4 32,POW 32,Q25 32,"
           "NLF 4,SL 128,LMF 8,WJ 32,ND 8,I8 192,OCF 12"),
@@ -48,7 +52,7 @@ for _k in range(8):
 _DMAS = ["ncl", "lim", "uc"] + [n + s for s in "01" for n in ("bank", "ra", "rb", "rc", "rl", "used", "out")]
 SEMAPHORES = ["sV", "sA", "sP", "sG"] + ["d_" + n for n in _DMAS] + [n + "%d%d" % (s, t) for n in ("arr", "sent") for s in (0, 1) for t in range(RO)]
 BANKS = tuple("b%d" % k for k in range(8))
-HOP, GATHER, SCATTER, PE, FLIGHT = 240, 1.56, 3.8, 0.54, 5700
+HOP, ACT, GATHER, SCATTER, PE, FLIGHT = 230, 10, 1.56, 3.8, 0.5, 2000
 
 
 def rank_program(g, core, T, topo):
@@ -56,15 +60,16 @@ def rank_program(g, core, T, topo):
     if rank is None:
         return
     eng = {"V": g.vector, "A": g.scalar, "P": g.tensor, "G": g, "S": g.sync}
-    ops, lastw, readers, S = [], {}, {}, [0]
+    ops, lastw, readers, S, step = [], {}, {}, [0], ["s"]
 
-    share = {"UG": "DS", "RR": "W", "OW": "IND", "CU": "LF"}
+    share = {"UG": "DS", "RR": "W", "OW": "IND"}
     DG, NDG, D512, D4, D8, TRI, BID, BON, FOLD, W8, BW, B4, W04, COLT, IT = [T.MX[:, k, :] for k in range(15)]
 
     def keys(s):
         return ["b%d" % (4 * S[0] + "abcd".index(k)) if k in ("a", "b", "c", "d") else share.get(k[:-1], k[:-1]) + k[-1].replace("@", str(S[0])) for k in s.split()]
 
     def do(e, call, r, w, c, lat=0, sem=None):
+        name = step[0] + e + (w or r).split()[0].strip("@0123456789")
         r, w, dep = keys(r), keys(w), {}
         for k in r:
             for d in lastw.get(k, ()):
@@ -76,7 +81,7 @@ def rank_program(g, core, T, topo):
                 if ops[d][0] != e or k in w:
                     dep[d] = True
         n = len(ops)
-        ops.append((e, call, dep, c, lat, sem))
+        ops.append((e, call, dep, c, lat, sem, name))
         for k in r:
             readers.setdefault(k, []).append(n)
         for k in w:
@@ -111,7 +116,7 @@ def rank_program(g, core, T, topo):
         do("P", lambda p: p.matmul(out, l, rh, start, stop), r, w, c * PE)
 
     def act(out, a, fn, r, w, scale=1.0, bias=0.0, c=64):
-        do("A", lambda s: s.activation(out, a, fn, bias=bias, scale=scale), r, w, c)
+        do("A", lambda s: s.activation(out, a, fn, bias=bias, scale=scale), r, w, c + (ACT if c == int(c) else 0.0))
 
     def lin(e, out, a, scale, bias, r, w, c=64):
         if e == "V":
@@ -127,15 +132,14 @@ def rank_program(g, core, T, topo):
 
     EQ, MUL, ADD, SUB = ALU.is_equal, ALU.mult, ALU.add, ALU.subtract
 
-    dma("ncl", [(T.NL[0:8, :], T.ncl[:, :])], "", "NL")
+    dma("ncl", [(T.NL[0:8, :], T.ncl[:, :])], "", "NL q")
+    dma("lim", [(T.LM[8 * h:8 * h + 8, :], T.lim[:, :]) for h in (0, 1)], "", "LM q")
     for s in (0, 1):
         S[0] = s
         rows = slice(64 * s, 64 * s + 64)
         for k, n in ((1, "rb"), (0, "ra"), (2, "rc")):
             dma(n + str(s), [(X("R")[0:64, k, 0:256], T[n][rows, 0:256]), (X("R")[64:128, k, 0:255], T[n][rows, 1:256])], "", "R%d0@ q" % k, 900)
         dma("bank%d" % s, [(X("bank")[64 * h:64 * h + 64, 0:B], T.bank[rows, :]) for h in (0, 1)], "", "bk@ q", 3300)
-        if s == 0:
-            dma("lim", [(T.LM[8 * h:8 * h + 8, :], T.lim[:, :]) for h in (0, 1)], "", "LM q")
     for s in (0, 1):
         S[0] = s
         rows = slice(64 * s, 64 * s + 64)
@@ -153,7 +157,7 @@ def rank_program(g, core, T, topo):
     iota(T.KC[:, :], [[1, 4], [-1, 4]], "KC", 0, 3)
     iota(T.IL[:, :], [[16, 2], [0, 4], [1, 16]], "IL")
     iota(T.I64[:, :], [[0, 2], [1, 64]], "I64")
-    iota(T.GB[0:16, :], [[1, 4], [0, 32]], "GB")
+    iota(T.GB[0:16, 0:128], [[1, 4], [0, 32]], "GB")
     iota(T.I8[:, :], [[0, 24], [1, 8]], "I8")
     iota(T.OCF[:, :], [[0, 3], [1, 4]], "OCF")
     iota(T.WJ[:, 1:32:2], [[16, 16]], "WJ0", 0, -256)
@@ -177,7 +181,7 @@ def rank_program(g, core, T, topo):
 
     CC = T.CC
     names = ["pid", "i", "m", "typ", "g", "h", "p8", "c32", "p64", "p4", "q8", "b3", "wt", "w8", "l", "sg", "off", "nsg", "sg4", "tm", "i0", "n7", "h1", "hs", "pv0", "pv1", "lpc", "mic",
-             "pw", "mk", "cP", "t0", "t1", "G8", "pt", "pts", "r0", "hc", "G0", "G1", "lic", "s256", "k63"]
+             "pw", "mk", "cP", "t0", "t1", "G8", "pt", "pts", "r0", "hc", "G0", "G1", "lic", "s256", "k63", "h16"]
     col = {n: CC[:, k:k + 1] for k, n in enumerate(names)}
     for k, (sh, an) in enumerate([(0, 255), (0, 15), (1, 7), (0, 1), (4, 3), (6, 1), (0, 7), (0, 31), (0, 63), (5, 3), (4, 7), (3, 1)]):
         ts(T.TI[:, k:k + 1], T.PID[:, :], sh, ALU.arith_shift_right, "PID", "TI%d" % k, an, ALU.bitwise_and)
@@ -190,8 +194,8 @@ def rank_program(g, core, T, topo):
         else:
             ts(col[n], col[src], a, MUL, "CC c" + src, "c" + n, b, ADD)
     for x in (("wt", "i", 14.0, 9.0), ("w8", "i", 14 / 8, 9 / 8), ("sg", "typ", 2.0, -1.0), ("off", "typ", 2.0 ** -12, -2.0 ** -12), ("nsg", "typ", -2.0, 1.0),
-              ("sg4", "typ", 2.0 / 4096, -1.0 / 4096), ("tm", "typ", 1.0 / 128, -0.5 - 0.5 / 4096), ("s256", "typ", 2.0 / 256, -1.0 / 256), ("k63", "typ", -1.0 / 128, -512 + 1.0 / 128), ("h1", "h", -1.0, 1.0), ("hs", "h", -2.0, 1.0), ("pv0", "p4", 1.0, -3.875),
-              ("pv1", "p4", 1.0, 0.125), ("mic", "i", 1.0, 48.0), ("hc", "b3", 4.0, 0.0), ("lic", "g", 16.0, 15.0)):
+              ("sg4", "typ", 2.0 / 4096, -1.0 / 4096), ("tm", "typ", 1.0 / 128, -0.5 - 0.5 / 4096), ("s256", "typ", 2.0 / 256, -1.0 / 256), ("k63", "typ", -1.0 / 128, -512 + 1.0 / 128), ("h1", "h", -1.0, 1.0), ("hs", "h", -2.0, 1.0),
+              ("mic", "i", 1.0, 48.0), ("hc", "b3", 4.0, 0.0), ("lic", "g", 16.0, 15.0)):
         cl(*x)
     lin("A", col["l"], col["h"], 16.0, col["i"], "CC", "cl")
     ts(col["i0"], col["i"], 0.0, EQ, "CC", "ci0")
@@ -209,8 +213,8 @@ def rank_program(g, core, T, topo):
     for n, x in ((3, 2.0 ** -13), (2, -float(MID)), (1, -0.5)):
         ms(T.LC[0:n, :], x, "LC")
     for n, x in ((2, 0.5 - rank / 8), (1, -2048.0)):
-        ms(T.LY[0:n, :], x, "LY")
-    ms(T.LN[0:1, :], -512.0, "LN")
+        ms(T.LY[0:n, 0:128], x, "LY")
+    ms(T.LY[0:1, 128:256], -512.0, "LN")
     m, E6, MQ = col["m"], T.EQ, T.MQ
     ts(E6[:, 0, :], T.IA[:, :], m, EQ, "IA CC", "E0")
     ts(E6[:, 1, :], T.IA[:, :], 1.0, ADD, "IA CC", "E1", m, EQ)
@@ -268,10 +272,10 @@ def rank_program(g, core, T, topo):
         scan(X("W")[:, 0:80], T.RS5[:, :], T.T5[:, 80 * s:80 * s + 80], MUL, ADD, "RS5 T5c@ T50@ T51@ T52@ T53@", "W@", 80)
         ts(T.BS[:, o], base, M32, ADD, "W@", "BS@", M32, SUB)
         act(T.HI[:, o], base, AF.Copy, "W@ CC T5c0 T5c1 MQn", "T5h@", col["h"])
-        ts(T.BS[:, o], T.BS[:, o], col["hs"], MUL, "BS@ chs", "BS@")
+        act(T.BS[:, o], T.BS[:, o], AF.Copy, "BS@ chs", "BS@", col["hs"])
         tt(ST[:, :, 0:4], T.BS[:, o], T.HI[:, o], ADD, "BS@ T5h@", "ST@")
-        ts(ST[:, :, 0:2], ST[:, :, 0:2], 0.5 / 4096, MUL, "ST@", "STa@")
-        ts(ST[:, :, 2:4], ST[:, :, 2:4], 0.5, MUL, "ST@ STa@", "SV0@ SV1@ SV2@ SV3@")
+        act(ST[:, :, 0:2], ST[:, :, 0:2], AF.Copy, "ST@", "SU0@ SU1@ SU2@ SU3@", 0.5 / 4096)
+        ts(ST[:, :, 2:4], ST[:, :, 2:4], 0.5, MUL, "ST@", "SV0@ SV1@ SV2@ SV3@")
         ts(CS[:, 16:20], F[:, 0:4], F[:, 3:4], MUL, "F@", "p3@", -2047.5, ADD)
         ts(CS[:, 20:22], F[:, 1:3], F[:, 2:3], MUL, "F@", "p2@", -2047.5, ADD)
         ts(T.W16[:, 0:16:5], CS[:, 16:20], M4096, ADD, "p3@ W16", "W16a", M4096, SUB)
@@ -292,36 +296,34 @@ def rank_program(g, core, T, topo):
     act(T.WCP[:, 8:16], T.WCP[:, 0:8], AF.Copy, "WCa WCb", "WCc", -1.0)
     act(T.WCP[:, 16:24], T.WCP[:, 0:8], AF.Copy, "WCa WCb cwt", "WCP", col["wt"])
     for ap, k, x in ((NDG, "NDG", -1.0), (D512, "D512", 512.0), (D4, "D4", 0.25), (D8, "D8", 0.125)):
-        ts(ap, DG, x, MUL, "DG", k)
-    LMF = T.LMF
-    cp(LMF[0:16, 0:2], T.LM[0:16, :], "LM", "LMF")
-    ts(LMF[0:16, 2:3], LMF[0:16, 1:2], -1.0, MUL, "LMF", "LM2", -0.5, ADD)
-    ts(LMF[0:16, 3:4], LMF[0:16, 0:1], -0.5, ADD, "LMF", "LM3")
+        act(ap, DG, AF.Copy, "DG", k, x, c=128)
+    LMF, pt, pts = T.LMF, CC[0:16, 11:12], CC[0:16, 35:36]
+    ts(LMF[0:16, 2:3], T.LM[0:16, 1:2], -1.0, MUL, "LM", "LM2", -0.5, ADD)
+    ts(LMF[0:16, 3:4], T.LM[0:16, 0:1], -0.5, ADD, "LM", "LM3")
     ts(LMF[0:16, 4:6], LMF[0:16, 2:4], M32, ADD, "LM2 LM3", "LM4", M32, SUB)
-    ts(CC[0:16, 34:35], CC[0:16, 0:1], 8.0, ALU.is_ge, "CC", "cpt")
-    ts(CC[0:16, 35:36], CC[0:16, 34:35], -2.0, MUL, "cpt", "cpts", 1.0, ADD)
-    ts(LMF[0:16, 4:6], LMF[0:16, 4:6], CC[0:16, 35:36], MUL, "LM4 cpts", "LM4")
-    ts(LMF[0:16, 2:4], LMF[0:16, 2:4], CC[0:16, 34:35], MUL, "LM2 LM3 LM4 cpt", "LM2 LM3")
-    tt(LMF[0:16, 4:6], LMF[0:16, 4:6], LMF[0:16, 2:4], ADD, "LM2 LM4", "LM4")
-    ts(LMF[0:16, 6:7], CC[0:16, 34:35], 3.5, MUL, "cpt", "LM6", -3.5, ADD)
+    act(pts, pt, AF.Copy, "CD", "cpts", -2.0, 1.0)
+    act(LMF[0:16, 0:2], LMF[0:16, 2:4], AF.Copy, "LM2 LM3 CD", "LM0", pt)
+    for k in (0, 1):
+        lin("A", LMF[0:16, 4 + k:5 + k], LMF[0:16, 4 + k:5 + k], pts, LMF[0:16, k:k + 1], "LM4 LM0 cpts", "LMx%d" % k)
+    act(LMF[0:16, 6:7], pt, AF.Copy, "CD", "LMx2", 3.5, -3.5)
     for s in (0, 1):
-        ts(CC[0:16, 38 + s:39 + s], CC[0:16, 6:7], -4.0 * s, ADD, "CD", "cG%d" % s)
+        ts(T.GB[0:16, 128 * s + 128:128 * s + 256], T.GB[0:16, 0:128], 4.0 * s, ADD, "GB CD", "GM%d" % s, CC[0:16, 6:7], EQ)
         for k in range(3):
-            ts(T.PRE[0:16, 384 * s + 128 * k:384 * s + 128 * k + 128], T.GB[0:16, :], CC[0:16, 38 + s:39 + s], EQ, "GB LM4 LM6 cG%d" % s, "PRE%d%d" % (k, s), LMF[0:16, 4 + k:5 + k], MUL)
-    ts(W8, BON, col["w8"], MUL, "BON cw8", "W8")
-    ts(B4, BON, 4.0, MUL, "BON", "B4")
+            act(T.PRE[0:16, 384 * s + 128 * k:384 * s + 128 * k + 128], T.GB[0:16, 128 * s + 128:128 * s + 256], AF.Copy, "GM%d LMx%d" % (s, k), "PRE%d%d" % (k, s), LMF[0:16, 4 + k:5 + k], c=128)
+    act(W8, BON, AF.Copy, "BON cw8", "W8", col["w8"], c=128)
+    act(B4, BON, AF.Copy, "BON", "B4", 4.0, c=128)
     ts(W04, BON, col["i0"], MUL, "BON ci0", "W04", 4.0, MUL)
     ms(T.Q25[:, :], 0.25, "Q25")
     scan(T.POW[:, :], T.Q25[:, :], T.ZERO[:, 0:32], MUL, ADD, "Q25 ZERO", "POW", init=4.0)
     ts(T.Q25[:, :], T.IR[:, 0:32], col["l"], EQ, "IR cl POW", "Q25")
     tt(T.Q25[:, :], T.Q25[:, :], T.POW[:, :], MUL, "Q25 POW", "Q25")
     do("V", lambda v: v.tensor_reduce(col["pw"], T.Q25[:, :], AX.X, ADD), "Q25", "cpw", 64)
-    ts(BW, BON, col["pw"], MUL, "BON cpw", "BW")
+    act(BW, BON, AF.Copy, "BON cpw", "BW", col["pw"], c=128)
     act(T.NTH[0:1, 0:32], T.POW[0:1, :], AF.Copy, "POW", "NTH", -2.0)
     for n in (32, 64, 128):
         act(T.NTH[0:1, n:2 * n], T.NTH[0:1, 0:n], AF.Copy, "NTH", "NTH", c=max(64, n))
-    lin("V", col["lpc"], col["pid"], 1.0, 15.0, "CC", "clpc")
-    ts(col["mk"], col["i0"], col["h1"], MUL, "ci0 ch1", "cmk")
+    cl("lpc", "pid", 1.0, 15.0)
+    act(col["mk"], col["i0"], AF.Copy, "ci0 ch1", "cmk", col["h1"])
     ts(T.LP[:, 0:80], T.IR[:, 0:80], col["lpc"], EQ, "IR clpc cmk", "LPa", col["mk"], MUL, 80)
     ts(T.LP[:, 79:144], T.IR[:, 15:80], col["lpc"], EQ, "IR clpc cmk LPa", "LP", col["mk"], MUL)
     ts(T.LI[:, 0:80], T.IR[:, 0:80], col["lic"], EQ, "IR clic cw8", "LIa", col["w8"], MUL, 80)
@@ -332,19 +334,19 @@ def rank_program(g, core, T, topo):
     act(T.MH[:, 112:176], T.MI[:, 112:176], AF.Copy, "MIb", "MHb", -31.0)
     for k, x in enumerate((2.0, 32.0, 1.0)):
         ts(T.RPM[:, 64 * k:64 * k + 64], T.I8[:, 64 * k:64 * k + 64], col["q8"], EQ, "I8 CD", "RPM%d" % k, x, MUL)
-    ts(T.OCF[:, :], T.OCF[:, :], col["hc"], ADD, "OCF chc", "OCF")
-    for k, (x, y) in enumerate(((32.0, 256.0 + 31), (1.0, 512.0), (32.0, 15.0))):
+    lin("A", T.OCF[:, :], T.OCF[:, :], 1.0, col["hc"], "OCF chc", "OCF")
+    for k, (x, y) in enumerate(((34.0, 33.0), (34.0, 0.0), (34.0, 17.0))):
         ts(T.OC[:, 4 * k:4 * k + 4], T.OCF[:, 4 * k:4 * k + 4], x, MUL, "OCF", "OC%d" % k, y, ADD)
-    ms(T.RS32[:, :], 1.0, "RS32", 128)
-    ms(T.RS32[:, 0:256:32], 0.0, "RS32")
-    ts(T.WJ[:, 1:32:2], T.WJ[:, 1:32:2], col["i"], ADD, "WJ0 CC", "WJ")
+    iota(T.RS2[:, :], [[0, 32], [1, 2]], "RS2")
+    do("G", lambda q: q.affine_select(T.RS34[:, :], T.ONE[:, 0:306], [[0, 9], [1, 34]], ALU.not_equal, 0.0, -1, 0), "ONE", "RS34", 820)
+    do("G", lambda q: q.affine_select(T.RS34[:, :], T.RS34[:, :], [[0, 9], [1, 34]], ALU.not_equal, 0.0, -2, 0), "RS34", "RS34", 820)
+    lin("A", T.WJ[:, 1:32:2], T.WJ[:, 1:32:2], 1.0, col["i"], "WJ0 CC", "WJ")
     ts(T.ND[:, :], T.ND[:, :], col["i"], SUB, "ND0 CC", "ND", -0.5, ADD)
     ts(col["G8"], col["l"], 31.0, EQ, "cl", "cG8", MARK, MUL)
     for s in (0, 1):
         S[0] = s
-        cp(X("K")[:, 4097:4098], col["G8"], "cG8 Ke@", "Km@")
-        ts(X("Z")[:, 160:161], T.ONE[:, 0:1], col["pid"], MUL, "ONE CC", "Zr@", 0.5, ALU.is_gt)
-        ms(X("WN")[:, 520:528], 0.0, "WNz@")
+        act(X("K")[:, 4097:4098], col["G8"], AF.Copy, "cG8 Ke@", "Km@")
+        act(X("Z")[:, :, 0], T.ONE[:, 0:32], AF.Sign, "ONE CC", "Zr@", col["pid"])
 
     def lists(t):
         CS, ST, W, OF, R, d = X("CS"), X("ST"), X("W"), X("OF"), X("R"), bank("d")
@@ -353,13 +355,13 @@ def rank_program(g, core, T, topo):
         lin("A", CS[:, 4:5], cl_, col["sg"], col["off"], "SA%d@ csg coff" % t, "SC@")
         mm(d[:, :], T.LC[0:3, :], T.RI[0:3, :], "LC RI RIa", "d", True, False, 512)
         sign = X("V")[:, :]
-        do("A", lambda q: q.activation(sign, T.I64[:, :], AF.Sign, bias=cl_, scale=ct, accum_out=CS[:, 3:4]), "COLT Ct@ SA%d@" % t, "V@ ac@", 150)
-        lin("A", W[:, 0:128], T.IL[:, :], ct, CS[:, 4:5], "IT Ct@ SC@", "W@", 128)
+        do("A", lambda q: q.activation(sign, T.I64[:, :], AF.Sign, bias=cl_, scale=ct, accum_out=CS[:, 3:4]), "COLT Ct@ SA%d@" % t, "V@ ac@", 150 + ACT)
+        lin(ON[3], W[:, 0:128], T.IL[:, :], ct, CS[:, 4:5], "IT Ct@ SC@", "W@", 128)
         ts(CS[:, 8:9], CS[:, 3:4], ct, MUL, "ac@ Ct@ cs256", "X@", col["s256"], MUL)
         ts(X("IND")[:, :], W[:, 0:128], CS[:, 8:9], ALU.is_ge, "W@ X@", "IND@", c=128)
         for q in range(4):
             val = CS[:, 12 + q:13 + q] if t and q < 2 else ST[:, t, q:q + 1]
-            lin(RQ[q], X("XG")[:, 128 * q:128 * q + 128], X("V")[:, :], val, val, "V@ SV%d@ VL%d@" % (t, q), "RQ%d@" % q, 128 if RQ[q] == "A" else 64)
+            lin(RQ[q], X("XG")[:, 128 * q:128 * q + 128], X("V")[:, :], val, val, "V@ S%s%d@ VL%d@" % ("UUVV"[q], t, q), "RQ%d@" % q, 128 if RQ[q] == "A" else 64)
         mm(d[:, 0:256], X("IND")[:, :], X("XG")[:, 0:256], "IND@ RQ0@ RQ1@", "d", False, False, 256)
         mm(d[:, 256:512], X("IND")[:, :], X("XG")[:, 256:512], "IND@ RQ2@ RQ3@", "d", False, True, 256)
         ts(W[:, 256:384], R[:, 2, c], CS[:, 10:11], MUL, "R2" + k + " T4@", "Wz@", HALF - MID, ADD, 128)
@@ -372,17 +374,19 @@ def rank_program(g, core, T, topo):
             ts(OF[:, 128 * n:128 * n + 128], W[:, 128 * n:128 * n + 128], M1, ADD, w_, ("OX@", "OY@")[n], M1 - MID, SUB, 128)
 
     def pieces(q):
-        return [(p, 512 // CUT[q]) for p in range(0, 512, 512 // CUT[q])]
+        return [(p, 512 // len(MODE[q])) for p in range(0, 512, 512 // len(MODE[q]))]
 
     def build(t):
         win, OF, K, XG, YG, ZG, FX, a = X("bank")[:, 0:B + 256 * t], X("OF"), X("K"), X("XG"), X("YG"), X("ZG"), X("FX"), bank("a")
         bk = " bk@ bz1@ bz2@" if t > 1 else " bk@"
         mm(a[:, 0:256], T.ONE[0:16, 0:128], T.PRE[0:16, 384 * S[0]:384 * S[0] + 256], "ONE PRE0@ PRE1@", "a", True, False, 256)
         mm(bank("d")[:, 0:128], T.ONE[0:16, 0:128], T.PRE[0:16, 384 * S[0] + 256:384 * S[0] + 384], "ONE PRE2@", "d", True, False, 128)
+        if t == 0:
+            more[len(ops) - 2] = more[len(ops) - 1] = EARLY
         tmp, n0 = 0, len(ops)
         for q in ORDER:
-            mode, op = MODE[q], (ALU.min, ALU.max, None, ADD)[q]
-            for p, PIECE in pieces(q):
+            op = (ALU.min, ALU.max, None, ADD)[q]
+            for (p, PIECE), mode in zip(pieces(q), MODE[q]):
                 gc_ = 70 + GATHER * PIECE
                 o, k = 512 * q + p, "%d%d@" % (q, p)
                 c, ko = slice(o, o + PIECE), K[:, 2 * o + 1:2 * (o + PIECE):2]
@@ -420,7 +424,7 @@ def rank_program(g, core, T, topo):
                 kq = K[:, 1024 * q + 2 * b_ + 1:1024 * q + 1024:32]
                 mm(bank("d")[32 * q:32 * q + 32, b_:128:16], kq, T.WCP[:, 16:24], "WCP " + kk, "d", False, b_ == 15, 32)
         for e in "VA":
-            row = [k for k in range(n0, len(ops)) if ops[k][0] == e and ops[k][3] > 70 + GATHER * 100 and ops[k][3] not in (256, 512)]
+            row = [k for k in range(n0, len(ops)) if ops[k][0] == e and ops[k][3] != int(ops[k][3])]
             if e == "V":
                 row = row[0:1] + [k for x, z in zip(row[2::2], row[1::2]) for k in (x, z)] + row[-1:]
             for k, j in zip(row, row[1:]):
@@ -428,7 +432,7 @@ def rank_program(g, core, T, topo):
 
     def pick(t):
         a, b, c, d = [bank(k) for k in "abcd"]
-        DS, V, O, S4, U, Z, EC, CU, WN, RJ, RR = [X(n) for n in ("DS", "V", "O", "S4", "U", "Z", "EC", "CU", "WN", "RJ", "RR")]
+        DS, V, O, S4, U, Z, WN, RJ, RR = [X(n) for n in ("DS", "V", "O", "S4", "U", "Z", "WN", "RJ", "RR")]
         act(DS[:, :], a[:, 0:256], AF.Sign, "a", "DS@", c=256)
         mm(b[:, 0:128], D4, DS[:, 0:128], "D4 DS@", "b", True, False, 128)
         mm(b[:, 0:128], D8, DS[:, 128:256], "D8 DS@", "b", False, True, 128)
@@ -437,34 +441,33 @@ def rank_program(g, core, T, topo):
         tt(V[:, :], b[:, 0:128], X("OW")[:, :], ADD, "b OW@", "V@", 128)
         for p in range(8):
             ts(O[:, 16 * (p // 4) + p % 4:16 * (p // 4) + 16:4, :], V[:, :], p - 3.875, EQ, "V@", "O%d@" % p)
-        mm(c[:, 0:128], BID, V[:, :], "BID V@", "c", c=128)
-        act(Z[:, 0:128], c[:, 0:128], AF.Copy, "c", "Zv@", c=128)
-        for k in range(32):
-            mm(b[:, 0:32], TRI, O[:, :, k], "TRI " + " ".join("O%d@" % p for p in range(8)), "b", k == 0, k == 31)
+        for k in range(16):
+            mm(b[:, 0:64], TRI, O[:, :, k:32:16], "TRI " + " ".join("O%d@" % p for p in range(8)), "b", k == 0, k == 15)
+        for h, e in enumerate("cd"):
+            mm(bank(e)[:, :], BID, O[:, 16 * h:16 * h + 16, :], "BID " + " ".join("O%d@" % p for p in range(4 * h, 4 * h + 4)), e, c=512)
+            act(Z[:, 16 * h:16 * h + 16, 2:34], bank(e)[:, :], AF.Copy, e, "Zv%d@" % h, c=512)
+        scan(RJ[:, 0:64], T.RS2[:, :], b[:, 0:64], MUL, ADD, "b RS2", "RJ@")
         for r in range(4):
-            act(S4[:, r:128:4], b[:, 0:32], AF.Copy, "b", "S%d@" % r, 1.0, -float(r))
-        mm(c[:, 128:160], BID, S4[:, 0:128:4], "BID S0@", "c")
-        act(Z[:, 128:160], c[:, 128:160], AF.Copy, "c", "Zs@")
+            lin(SQ[r], S4[:, r:128:4], RJ[:, 1:64:2], 1.0, -float(r), "RJ@", "S%d@" % r)
+        mm(a[:, 0:32], BID, RJ[:, 1:64:2], "BID RJ@", "a")
+        if SQ[4] == "A":
+            act(Z[:, :, 1], a[:, 0:32], AF.Copy, "a", "Zs@")
+        else:
+            cp(Z[:, :, 1], a[:, 0:32], "a", "Zs@")
         for k in range(8):
             ts(U[:, :, 4 * k:4 * k + 4], S4[:, :], 4.0 * k, ALU.is_le, "S0@ S1@ S2@ S3@", "U%d@" % k)
         uk = " " + " ".join("U%d@" % k for k in range(8))
-        for n in range(8):
-            mm(b[:, 32 * n:32 * n + 32], U[:, 4 * n:4 * n + 4, :], Z[:, 32 * (n % 4):32 * (n % 4) + 32], "Zv@" + uk, "b")
-        for n in range(8):
-            for p in range(4):
-                k = 4 * n + p
-                mm(d[32 * p:32 * p + 32, n:16:8], U[:, k, :], Z[:, 128 + k:161:32 - k], "Zs@ Zr@" + uk, "d", c=32)
-        for h in (0, 1):
-            ts(EC[:, 128 * h:128 * h + 128], b[:, 128 * h:128 * h + 128], col["pv%d" % h], EQ, "b cpv%d" % h, "EO%d@" % h, c=128)
-        tt(EC[:, 0:256:32], d[:, 0:8], EC[:, 0:256:32], ADD, "EO0@ EO1@ d", "EO0@ EO1@")
-        act(WN[:, 512:520], d[:, 8:16], AF.Copy, "d", "WR@")
-        scan(CU[:, :], T.RS32[:, :], EC[:, :], MUL, ADD, "RS32 EO0@ EO1@", "CU@", 128)
-        ts(WN[:, 0:256], CU[:, :], col["c32"], ALU.is_le, "CU@ CD", "IN@", c=128)
-        scan(WN[:, 256:512], T.RS32[:, :], WN[:, 0:256], MUL, ADD, "RS32 IN@", "C2@", 128)
-        tt(RJ[:, :], WN[:, :].indirect(T.OC[:, :]), T.RPM[:, :], MUL, "IN@ C2@ WR@ WNz@ OC0 OC1 OC2 RPM0 RPM1 RPM2", "RJ@", 50 + 192 * GATHER)
-        for n in range(12):
-            q = n % 4
-            mm(c[:, 0:16], (T.MH if n >= 8 else T.MI)[:, 48 - 16 * q:176 - 16 * q], RJ[:, 16 * n:16 * n + 16], "MIa MIb MHa MHb RJ@", "c", n == 0, n == 11)
+        for k in range(32):
+            mm(b[32 * (k % 4):32 * (k % 4) + 32, 34 * (k // 4):34 * (k // 4) + 34], U[:, k, :], Z[:, k, :], "Zv%d@ Zs@ Zr@" % (k // 16) + uk, "b", c=34)
+        scan(WN[:, 0:272], T.RS34[:, 1:273], b[:, 0:272], MUL, ADD, "RS34 b", "CU@", 272)
+        ts(WN[:, 544:816], WN[:, 0:272], col["c32"], ALU.is_le, "CU@ CD", "IN@", c=136)
+        scan(WN[:, 272:544], T.RS34[:, 0:272], WN[:, 544:816], MUL, ADD, "RS34 IN@", "C2@", 136)
+        for k, (o, r) in ((1, (0, "CU@")), (2, (544, "IN@")), (0, (272, "C2@"))):
+            tt(RJ[:, 64 * k:64 * k + 64], WN[:, o:o + 272].indirect(T.OC[:, 4 * k:4 * k + 4]), T.RPM[:, 64 * k:64 * k + 64], MUL, r + " OC%d RPM%d" % (k, k),
+               "RJ@" if k == 0 else "RK%d@" % k, 60 + 64 * GATHER)
+            for q in range(4):
+                mm(c[:, 0:16], (T.MH if k == 2 else T.MI)[:, 48 - 16 * q:176 - 16 * q], RJ[:, 64 * k + 16 * q:64 * k + 16 * q + 16], "MIa MIb MHa MHb " + ("RJ@" if k == 0 else "RK%d@" % k), "c",
+                   k == 1 and q == 0, k == 0 and q == 3)
         ts(X("OS")[:, 0, :], c[:, 0:16], col["h1"], ADD, "c ch1", "OJ@")
         o, send, land = 256 * t, X("send"), X("land")
         kk = " ".join("K%d%d@" % (q, p) for q in range(4) for p, _ in pieces(q)) + " Kz0@ Kz1024@ Kz2048@ Kz3072@ Ke@ Km@"
@@ -477,8 +480,8 @@ def rank_program(g, core, T, topo):
                 tr.append(RemoteDMATransfer(dst_ids=[DstId(rid=rid, pnc=pid)], dma_engine_mask=(1 << e[2 * k]) | (1 << e[2 * k + 1]), remote_sem=T.sem["arr" + name],
                                             srcs=[send[:, o + 32 * p:o + 32 * p + 32]], dsts=[land[:, o + 32 * rank:o + 32 * rank + 32]]))
                 k += 1
-        do("G", lambda q: g.remote_dma_fused(tr, local_sem=T.sem["sent" + name]), "snd%d@" % t, "arr%d@" % t, 600, FLIGHT, ("arr" + name, 14))
-        act(land[:, o + 32 * rank:o + 32 * rank + 32], send[:, o + 32 * rank:o + 32 * rank + 32], AF.Copy, "snd%d@" % t, "own%d@" % t)
+        do("G", lambda q: g.remote_dma_fused(tr, local_sem=T.sem["sent" + name]), "snd%d@" % t, "arr%d@" % t, 600 if t + S[0] else 2400, FLIGHT, ("arr" + name, 14))
+        lin(ON[4], land[:, o + 32 * rank:o + 32 * rank + 32], send[:, o + 32 * rank:o + 32 * rank + 32], 1.0, 0.0, "snd%d@" % t, "own%d@" % t)
 
     def keep(t):
         a, b, c, d = [bank(k) for k in "abcd"]
@@ -486,12 +489,12 @@ def rank_program(g, core, T, topo):
         last, lnd, lk = t == RO - 1, X("land")[:, 256 * t:256 * t + 256], " arr%d@ own%d@" % (t, t)
         act(CS[:, 11:12], CS[:, 10:11], AF.Copy, "T4@", "TB@", 4096.0, 127.5 - B)
         act(CS[:, 9:10], CS[:, 10:11], AF.Copy, "T4@", "T4b@", 1.0, 1.0 / 32)
-        mm(a[:, :], T.LY[0:2, :], T.ONE[0:2, :], "LY ONE", "a", True, False, 512)
+        mm(a[:, :], T.LY[0:2, 0:128], T.ONE[0:2, :], "LY ONE", "a", True, False, 512)
         mm(a[:, 256:512], T.LC[0:1, :], T.ONE[0:1, 0:256], "LC ONE", "a", False, False, 256)
         mm(a[:, 0:256], W8, lnd, "W8" + lk, "a", False, False, 256)
         mm(a[:, 256:512], W8, lnd, "W8" + lk, "a", False, True, 256)
         if last:
-            mm(d[:, 0:256], T.LN[0:1, :], T.ONE[0:1, 0:256], "LN ONE", "d", True, False, 256)
+            mm(d[:, 0:256], T.LY[0:1, 128:256], T.ONE[0:1, 0:256], "LN ONE", "d", True, False, 256)
         mm(d[:, 0:256], FOLD, lnd, "FOLD" + lk, "d", not last, not last, 256)
         if not last:
             act(LF[:, :], d[:, 0:256], AF.Copy, "d", "LF@", c=256)
@@ -500,12 +503,12 @@ def rank_program(g, core, T, topo):
             ts(RR[:, 128 * h:128 * h + 128], a[:, 128 * h:128 * h + 128], M4096, ADD, "a", w_, M4096, SUB, 128)
         for h, w_ in ((1, "Wy@"), (0, "W@")):
             tt(KB[:, 128 * h:128 * h + 128], a[:, 256 + 128 * h:384 + 128 * h], RR[:, 128 * h:128 * h + 128], SUB, "a " + w_, "KB%d@" % h, 128)
-        mm(b[:, 0:16], T.LY[0:2, :], T.ONE[0:2, 0:16], "LY ONE", "b", True, False)
+        mm(b[:, 0:16], T.LY[0:2, 0:128], T.ONE[0:2, 0:16], "LY ONE", "b", True, False)
         for i in range(16):
             mm(b[:, 0:16], T.LI[:, 15 - i:143 - i], X("land")[:, 256 * t + i:256 * t + 256:16], "LI" + lk, "b", False, i == 15)
         ts(SM[:, 5, :], b[:, 0:16], M4096, ADD, "b", "r16@", M4096, SUB)
         ts(E[:, 8, :], KB[:, :], MARK * 219 / 8 - rank / 8 - 2048, EQ, "KB0@ KB1@", "EM@", c=128)
-        mm(c[:, 0:256], W04, E[:, 8, :], "W04 EM@", "c", False, False, 256)
+        mm(c[:, 0:256], W04, E[:, 8, :], "W04 EM@ c", "", False, False, 256)
         for h in (0, 1):
             tt(SM[64 * h:64 * h + 64, 0, 0:8], b[64 * h:64 * h + 64, h:16:2], SM[64 * h:64 * h + 64, 5, h:16:2], SUB, "b r16@", "BL%d@" % h)
         tt(SM[:, 6, :], b[:, 0:16], SM[:, 5, :], SUB, "b r16@", "B16@")
@@ -513,12 +516,14 @@ def rank_program(g, core, T, topo):
         for m_ in range(8):
             ts(E[:, m_, 0:256 - 32 * m_], KB[:, 32 * m_:256], 0.5, ADD, "KB1@ BL0@ BL1@" + (" KB0@" if m_ < 4 else ""), "E%d@" % m_, SM[:, 0, m_:m_ + 1], EQ, max(64, 128 - 16 * m_))
             if m_ < 7:
-                mm(c[:, 32 * m_ + 32:256], B4, E[:, m_, 32:256 - 32 * m_], "B4 E%d@" % m_, "c", False, False, max(64, 224 - 32 * m_))
+                mm(c[:, 32 * m_ + 32:256], B4, E[:, m_, 32:256 - 32 * m_], "B4 E%d@ c" % m_, "", False, False, max(64, 224 - 32 * m_))
+            if m_ == 3:
+                mm(c[:, 0:128], BW, E[:, 0:4, 0:32], "BW E0@ E1@ E2@ E3@ c", "", False, False, 128)
         act(UG[:, :], X("USED")[:, :].indirect(OS[:, 1, :]), AF.Copy, "US@ BU@", "UG@", c=75 + 256 * GATHER)
-        mm(c[:, 0:256], W04, UG[:, :], "W04 UG@", "c", False, False, 256)
-        mm(c[:, 0:256], BW, E[:, 0:8, 0:32], "BW " + " ".join("E%d@" % k for k in range(8)), "c", False, True, 256)
+        mm(c[:, 128:256], BW, E[:, 4:8, 0:32], "BW E4@ E5@ E6@ E7@ c", "", False, False, 128)
+        mm(c[:, 0:256], W04, UG[:, :], "W04 UG@", "c", False, True, 256)
         P = CS[:, 22:23]
-        do("A", lambda q: q.activation(PK[:, :, 0], c[:, 0:256], AF.Sign, bias=0.0, scale=-1.0, accum_out=P), "c", "KP@ P@", 280)
+        do("A", lambda q: q.activation(PK[:, :, 0], c[:, 0:256], AF.Sign, bias=0.0, scale=-1.0, accum_out=P), "c", "KP@ P@", 280 + ACT)
         scan(PK[:, :, 1], T.ONE[:, 0:256], PK[:, :, 0], MUL, ADD, "ONE KP@", "PS@", 128)
         if last:
             mm(d[:, 0:256], D512, PK[:, :, 0], "D512 KP@", "d", False, True, 256)
@@ -526,9 +531,9 @@ def rank_program(g, core, T, topo):
         else:
             ts(X("WI")[:, :], P, F[:, 4:5], MUL, "P@ a0@ b0@", "w0@", F[:, 5:6], ADD)
             ts(CS[:, 2:3], X("WI")[:, :], 2.0, MUL, "w0@ SB%d@" % (t + 1), "Ct@", ST[:, t + 1, 5:6], ADD)
-            lin("A", CS[:, 10:11], P, 1.0 / 8192, CS[:, 9:10], "P@ T4b@ TB@", "T4@")
+            lin(ON[0], CS[:, 10:11], P, 1.0 / 8192, CS[:, 9:10], "P@ T4b@ TB@", "T4@")
             for q in (0, 1):
-                lin("A", CS[:, 12 + q:13 + q], P, MQ[:, 4 + t, 4 * t + 4 + q:4 * t + 5 + q], ST[:, t + 1, q:q + 1], "P@ SV%d@ CF%d" % (t + 1, 4 + t), "VL%d@" % q)
+                lin(ON[1 + q], CS[:, 12 + q:13 + q], P, MQ[:, 4 + t, 4 * t + 4 + q:4 * t + 5 + q], ST[:, t + 1, q:q + 1], "P@ SU%d@ CF%d" % (t + 1, 4 + t), "VL%d@" % q)
         for i in range(16):
             mm(b[:, 32:64], T.LP[:, 15 - i:143 - i], PK[:, i:256:16, :], "LP KP@ PS@", "b", i == 0, i == 15)
         scan(CS[:, 32:64], T.WJ[:, :], b[:, 32:64], MUL, ADD, "b WJ WJz", "D2@")
@@ -542,7 +547,9 @@ def rank_program(g, core, T, topo):
         tt(SM[:, 4, 0:8], SM[:, 3, 0:8], SM[:, 0, 0:8], ALU.max, "E10@ E11@ BL0@ BL1@", "Em@")
         ts(OS[:, 3, 0:8], SM[:, 4, 0:8], 2047.5, ADD, "Em@", "EU@")
         taken = X("USED")[:, :].indirect(OS[:, 3, 0:8])
-        do("A", lambda q: q.activation(taken, T.IR[:, 128:256], AF.Sigmoid), "EU@ IR", "US@", 80 + 128 * SCATTER + (1600 if t + S[0] == 0 else 0))
+        k = do("A", lambda q: q.activation(taken, T.IR[:, 128:256], AF.Sigmoid), "EU@ IR", "US@", 80 + 128 * SCATTER + (1600 if t + S[0] == 0 else 0))
+        if t == 0:
+            late.append((marks[0], k)) if marks else marks.append(k)
         if t < 2:
             act(CS[:, 14:15], P, AF.Copy, "P@", "nf@", 0.5, 128.0)
             act(CS[:, 16:18], F[:, 6:8], AF.Copy, "nf@ F12@ p3@", "x12@", CS[:, 14:15], HALF)
@@ -551,18 +558,17 @@ def rank_program(g, core, T, topo):
             for u in range(t + 2, 4):
                 k = u - t - 1
                 act(UP[:, u, 4:6], T.KN[:, :, 4 * u + k], AF.Copy, "KN0 KN1 w12@", "UP%d@" % u, CS[:, 17 + k:18 + k])
-            tt(ST[:, t + 2:4, :], ST[:, t + 2:4, :], UP[:, t + 2:4, :], ADD, "UP@ UP2@ UP3@", " ".join("S%s%d@" % (k, u) for k in "VAB" for u in range(t + 2, 4)))
+            tt(ST[:, t + 2:4, :], ST[:, t + 2:4, :], UP[:, t + 2:4, :], ADD, "UP@ UP2@ UP3@", " ".join("S%s%d@" % (k, u) for k in "UVAB" for u in range(t + 2, 4)))
 
-    first, more, late = [], {}, []
+    first, more, late, marks, ahead = [], {}, [], [], {}
     for s in (0, 1):
         S[0] = s
         first.append(len(ops))
         for t in range(RO):
-            lists(t)
-            build(t)
-            pick(t)
-            more[len(ops) - 2] = (LAG[t + 1] - LAG[t] if s else 0) if t < 3 else 0
-            keep(t)
+            for step[0], f in (("l", lists), ("b", build), ("p", pick), ("k", keep)):
+                f(t)
+                if f is pick:
+                    more[len(ops) - 2] = (LAG[t + 1] - LAG[t] if s else 0) if t < 3 else 0
         dma("out%d" % s, [(T.y[64 * s:64 * s + 64, :], X("bank")[0:64, B:4096])], "bk@ bz1@ bz2@", "out@", 700)
 
     n = len(ops)
@@ -580,7 +586,7 @@ def rank_program(g, core, T, topo):
                 topo_.append(j)
 
     def gap(d, k):
-        return 0 if ops[d][0] == ops[k][0] and (ops[d][0] == "P" or not ops[k][2][d]) else HOP + ops[d][4]
+        return 0 if ops[d][0] == ops[k][0] and (ops[d][0] == "P" or not ops[k][2][d]) else HOP + ops[d][4] + (DRAIN if ops[d][0] == "P" else 0)
     for k in topo_[::-1]:
         level[k] = ops[k][3] + max([gap(k, j) + level[j] for j in succ[k]] + [ops[k][4]]) + (lead[k] if not succ[k] else 0) + more.get(k, 0)
 
@@ -601,11 +607,14 @@ def rank_program(g, core, T, topo):
     start = place(sorted(range(n), key=lambda k: (-level[k], k)), pred, gap)
     for _ in range(PASSES):
         back = place(sorted(range(n), key=lambda k: (-start[k] - ops[k][3], -k)), succ, lambda d, k: gap(k, d))
-        start = place(sorted(range(n), key=lambda k: (-back[k] - ops[k][3], k)), pred, gap)
+        turn = [-back[k] - ops[k][3] - AHEAD.get(ops[k][6], 0) for k in range(n)]
+        for k in topo_:
+            turn[k] = max([turn[k]] + [turn[d] + 0.001 for d in pred[k]])
+        start = place(sorted(range(n), key=lambda k: (turn[k], k)), pred, gap)
     seq = sorted(range(n), key=lambda k: (start[k], k))
     mark, cnt, seen = {}, {e: 0 for e in eng}, {e: {} for e in eng}
     for k in seq:
-        e, call, dep, _c, _l, sem = ops[k]
+        e, call, dep, _c, _l, sem, _n = ops[k]
         need = {}
         for d, hard in dep.items():
             if hard and not (e == "P" and ops[d][0] == "P"):

import math
from concourse.bass import DstId, RemoteDMATransfer
from concourse.mybir import dt, AluOpType as ALU, AxisListType as AX, ActivationFunctionType as AF

B, CAP, RO, NR = 3072, 32, 4, 8
M1 = 1.5 * 2.0 ** 23
M7 = 1.5 * 2.0 ** 16
M8 = 1.5 * 2.0 ** 26
M32 = 1.5 * 2.0 ** 28
M4096 = 1.5 * 2.0 ** 35
MID = 1920
MARK = 74.5
HALF = -0.5 + 2.0 ** -13
MODE = ("aa", "a", "cc", "a")
LAG = (14000, 12500, 12500, 12500)
PASSES = 2
EARLY = 3000
DRAIN = 200
AHEAD = {"pAZv": -1200}
RQ = "AAAA"
SQ = "AAAAV"
ON = "AVVVA"
APP = 1
ORDER = (0, 1, 3, 2)
f32, bf, i32, u16, f16 = "float32", "bfloat16", "int32", "uint16", "float16"

SCRATCH = {}
_SET = (
    (bf, "bank 4096,K 4112,XG 2048,YG 2048,ZG 2048,FX 2048,V 128,IND 128,DS 256,O 32 32,S4 128,U 32 32,Z 32 34,WN 816,RJ 192,"
         "send 1024,land 1024,LF 256,E 9 256,PK 256 2"),
    (i32, "R 3 1024,WI 1"),
    (f32, "USED 4224,F 8,ST 4 6,UP 4 6,CS 64,W 384,SM 8 16"),
    (u16, "OF 384,OS 4 16"),
    (f16, "KB 256"),
)
_ALL = (
    (bf, "ONE 512,MX 15 128,WCP 24,LP 144,MI 176,MH 176,RPM 192,"
         "LI 144,RS34 306,RS2 64,ZERO 32,PRE 768,GB 384,RI 512,LC 128,LY 256,NTH 256"),
    (i32, "PID 1,TI 12,NL 4,LM 2,UC 256"),
    (f32, "UB 256,CC 48,IR 256,IG 128,IL 128,I64 128,IA 28,IB 28,EQ 6 28,MQ 7 16,T5 160,BS 32,RS5 80,HI 32,KA 16,KC 16,KT 2 16,KN 2 16,W16 16,PB 32,RS4 32,POW 32,Q25 32,"
          "NLF 4,SL 128,LMF 8,WJ 32,ND 8,I8 192,OCF 12"),
    (u16, "OC 12"),
)
for _names, _tab in ((("0", "1"), _SET), (("",), _ALL)):
    for _d, _l in _tab:
        for _x in _l.split(","):
            _x = _x.split()
            for _s in _names:
                SCRATCH[_x[0] + _s] = ("sbuf", [128] + [int(v) for v in _x[1:]], _d)
for _k in range(8):
    SCRATCH["b%d" % _k] = ("psum", [128, 512], f32)
_DMAS = ["ncl", "lim", "uc"] + [n + s for s in "01" for n in ("bank", "ra", "rb", "rc", "rl", "used", "out")]
SEMAPHORES = ["sV", "sA", "sP", "sG"] + ["d_" + n for n in _DMAS] + [n + "%d%d" % (s, t) for n in ("arr", "sent") for s in (0, 1) for t in range(RO)]
BANKS = tuple("b%d" % k for k in range(8))
HOP, ACT, GATHER, SCATTER, PE, FLIGHT = 230, 10, 1.56, 3.8, 0.5, 2000


def rank_program(g, core, T, topo):
    rank = T.rank_of(core)
    if rank is None:
        return
    eng = {"V": g.vector, "A": g.scalar, "P": g.tensor, "G": g, "S": g.sync}
    ops, lastw, readers, S, step = [], {}, {}, [0], ["s"]

    share = {"UG": "DS", "RR": "W", "OW": "IND"}
    DG, NDG, D512, D4, D8, TRI, BID, BON, FOLD, W8, BW, B4, W04, COLT, IT = [T.MX[:, k, :] for k in range(15)]

    def keys(s):
        return ["b%d" % (4 * S[0] + "abcd".index(k)) if k in ("a", "b", "c", "d") else share.get(k[:-1], k[:-1]) + k[-1].replace("@", str(S[0])) for k in s.split()]

    def do(e, call, r, w, c, lat=0, sem=None):
        name = step[0] + e + (w or r).split()[0].strip("@0123456789")
        r, w, dep = keys(r), keys(w), {}
        for k in r:
            for d in lastw.get(k, ()):
                dep[d] = True
        for k in w + [k for k in r if k in BANKS]:
            for d in lastw.get(k, ()):
                dep[d] = dep.get(d) or k != "q"
            for d in readers.get(k, ()):
                if ops[d][0] != e or k in w:
                    dep[d] = True
        n = len(ops)
        ops.append((e, call, dep, c, lat, sem, name))
        for k in r:
            readers.setdefault(k, []).append(n)
        for k in w:
            lastw[k], readers[k] = [n], []
        return n

    def X(name):
        return T[share.get(name, name) + str(S[0])]

    def bank(k):
        return T["b%d" % (4 * S[0] + "abcd".index(k))]

    def dma(name, pairs, r, w, c=100):
        do("S", lambda q: [q.dma_start(o, i).then_inc(T.sem["d_" + name], 16) for o, i in pairs], r, w, c, 2200, ("d_" + name, 16 * len(pairs)))

    def ts(out, in0, s1, op0, r, w, s2=None, op1=None, c=64):
        if op1 is None:
            do("V", lambda v: v.tensor_scalar(out, in0, s1, None, op0), r, w, c)
        else:
            do("V", lambda v: v.tensor_scalar(out, in0, s1, s2, op0, op1), r, w, c)

    def tt(out, a, b, op, r, w, c=64):
        do("V", lambda v: v.tensor_tensor(out, a, b, op), r, w, c)

    def cp(out, a, r, w, c=64):
        do("V", lambda v: v.tensor_copy(out, a), r, w, c)

    def ms(ap, x, w, c=64):
        do("V", lambda v: v.memset(ap, x), "", w, c)

    def mm(out, l, rh, r, w, start=True, stop=True, c=64):
        do("P", lambda p: p.matmul(out, l, rh, start, stop), r, w, c * PE)

    def act(out, a, fn, r, w, scale=1.0, bias=0.0, c=64):
        do("A", lambda s: s.activation(out, a, fn, bias=bias, scale=scale), r, w, c + (ACT if c == int(c) else 0.0))

    def lin(e, out, a, scale, bias, r, w, c=64):
        if e == "V":
            ts(out, a, scale, ALU.mult, r, w, bias, ALU.add, c)
        else:
            act(out, a, AF.Identity, r, w, scale, bias, c)

    def iota(ap, pat, w, cm=0, base=0):
        do("G", lambda q: q.iota(ap, pat, base, cm, allow_small_or_imprecise_dtypes=True), "", w, 160 + 2 * math.prod(p[1] for p in pat))

    def scan(out, d0, d1, op0, op1, r, w, c=64, init=0.0):
        do("V", lambda v: v.tensor_tensor_scan(out, d0, d1, init, op0, op1), r, w, c)

    EQ, MUL, ADD, SUB = ALU.is_equal, ALU.mult, ALU.add, ALU.subtract

    dma("ncl", [(T.NL[0:8, :], T.ncl[:, :])], "", "NL q")
    dma("lim", [(T.LM[8 * h:8 * h + 8, :], T.lim[:, :]) for h in (0, 1)], "", "LM q")
    for s in (0, 1):
        S[0] = s
        rows = slice(64 * s, 64 * s + 64)
        for k, n in ((1, "rb"), (0, "ra"), (2, "rc")):
            dma(n + str(s), [(X("R")[0:64, k, 0:256], T[n][rows, 0:256]), (X("R")[64:128, k, 0:255], T[n][rows, 1:256])], "", "R%d0@ q" % k, 900)
        dma("bank%d" % s, [(X("bank")[64 * h:64 * h + 64, 0:B], T.bank[rows, :]) for h in (0, 1)], "", "bk@ q", 3300)
    for s in (0, 1):
        S[0] = s
        rows = slice(64 * s, 64 * s + 64)
        dma("rl%d" % s, [(X("R")[64 * h:64 * h + 64, k, 256:1024 - h], T[n][rows, 256 + h:1024]) for k, n in enumerate(("ra", "rb", "rc")) for h in (0, 1)], "", "R01@ R11@ R21@ q", 5600)
        if s == 0:
            dma("uc", [(T.UC[:, :], T.used[:, :])], "", "UC q", 900)
    cp(T.UB[:, :], T.UC[:, :], "UC", "UB", 256)

    iota(T.PID[:, :], [[1, 1]], "PID", 1)
    iota(T.IR[:, :], [[1, 256]], "IR")
    iota(T.IA[:, :], [[1, 7], [0, 4]], "IA")
    iota(T.IB[:, :], [[-1, 7], [1, 4]], "IB", 0, 3)
    iota(T.IG[:, :], [[0, 2], [1, 4], [0, 16]], "IG")
    iota(T.KA[:, :], [[0, 4], [1, 4]], "KA")
    iota(T.KC[:, :], [[1, 4], [-1, 4]], "KC", 0, 3)
    iota(T.IL[:, :], [[16, 2], [0, 4], [1, 16]], "IL")
    iota(T.I64[:, :], [[0, 2], [1, 64]], "I64")
    iota(T.GB[0:16, 0:128], [[1, 4], [0, 32]], "GB")
    iota(T.I8[:, :], [[0, 24], [1, 8]], "I8")
    iota(T.OCF[:, :], [[0, 3], [1, 4]], "OCF")
    iota(T.WJ[:, 1:32:2], [[16, 16]], "WJ0", 0, -256)
    iota(T.WJ[:, 0:32:2], [[0, 16]], "WJz")
    iota(T.ND[:, :], [[-16, 8]], "ND0", 0, -2048)
    iota(T.ZERO[:, :], [[0, 32]], "ZERO")
    ms(T.ONE[:, :], 1.0, "ONE", 256)
    do("G", lambda q: q.affine_select(DG, T.ONE[:, 0:128], [[1, 128]], EQ, 0.0, 0, -1), "ONE", "DG", 460)
    do("G", lambda q: q.affine_select(TRI, T.ONE[:, 0:128], [[1, 128]], ALU.is_gt, 0.0, 0, -1), "ONE", "TRI", 460)
    do("G", lambda q: q.affine_select(BID, DG, [[1, 128]], ALU.not_equal, -1.0, -1, -1), "DG", "BID", 460)
    for s in (0, 1):
        S[0] = s
        for a in range(0, 4096, 1024):
            iota(X("K")[:, a:a + 1024:2], [[0, 512]], "Kz%d@" % a)
        iota(X("K")[:, 4096:4112], [[0, 16]], "Ke@")
        for a in range(0, 4224, 528):
            iota(X("USED")[:, a:a + 528], [[0, 528]], "Uz%d@" % a)
        dma("used%d" % s, [(X("USED")[64 * h:64 * h + 64:16, 0:4096], T.UB[64 * s:64 * s + 64, :]) for h in (0, 1)], "UB", " ".join("Uz%d@" % a for a in range(0, 4224, 528)) + " US@")
        iota(X("bank")[:, B + 256:B + 640], [[0, 384]], "bz1@")
        iota(X("bank")[:, B + 640:4096], [[0, 384]], "bz2@")

    CC = T.CC
    names = ["pid", "i", "m", "typ", "g", "h", "p8", "c32", "p64", "p4", "q8", "b3", "wt", "w8", "l", "sg", "off", "nsg", "sg4", "tm", "i0", "n7", "h1", "hs", "pv0", "pv1", "lpc", "mic",
             "pw", "mk", "cP", "t0", "t1", "G8", "pt", "pts", "r0", "hc", "G0", "G1", "lic", "s256", "k63", "h16"]
    col = {n: CC[:, k:k + 1] for k, n in enumerate(names)}
    for k, (sh, an) in enumerate([(0, 255), (0, 15), (1, 7), (0, 1), (4, 3), (6, 1), (0, 7), (0, 31), (0, 63), (5, 3), (4, 7), (3, 1)]):
        ts(T.TI[:, k:k + 1], T.PID[:, :], sh, ALU.arith_shift_right, "PID", "TI%d" % k, an, ALU.bitwise_and)
    cp(CC[:, 0:6], T.TI[:, 0:6], " ".join("TI%d" % k for k in range(6)), "CC")
    cp(CC[:, 6:12], T.TI[:, 6:12], " ".join("TI%d" % k for k in range(6, 12)), "CD cp4 cb3")

    def cl(n, src, a, b, e="A"):
        if e == "A":
            act(col[n], col[src], AF.Copy, "CC c" + src, "c" + n, a, b)
        else:
            ts(col[n], col[src], a, MUL, "CC c" + src, "c" + n, b, ADD)
    for x in (("wt", "i", 14.0, 9.0), ("w8", "i", 14 / 8, 9 / 8), ("sg", "typ", 2.0, -1.0), ("off", "typ", 2.0 ** -12, -2.0 ** -12), ("nsg", "typ", -2.0, 1.0),
              ("sg4", "typ", 2.0 / 4096, -1.0 / 4096), ("tm", "typ", 1.0 / 128, -0.5 - 0.5 / 4096), ("s256", "typ", 2.0 / 256, -1.0 / 256), ("k63", "typ", -1.0 / 128, -512 + 1.0 / 128), ("h1", "h", -1.0, 1.0), ("hs", "h", -2.0, 1.0),
              ("mic", "i", 1.0, 48.0), ("hc", "b3", 4.0, 0.0), ("lic", "g", 16.0, 15.0)):
        cl(*x)
    lin("A", col["l"], col["h"], 16.0, col["i"], "CC", "cl")
    ts(col["i0"], col["i"], 0.0, EQ, "CC", "ci0")
    ts(col["n7"], col["m"], 7.0, ALU.not_equal, "CC", "cn7")
    ts(col["t0"], col["m"], 0.0, ALU.not_equal, "CC cn7", "ct0", col["n7"], MUL)
    cl("cP", "t0", 256.0, -256.0)
    ts(BON, T.IG[:, :], col["g"], EQ, "IG CC", "BON", c=128)
    ts(T.IL[:, :], T.IL[:, :], col["sg4"], MUL, "IL csg4", "ITF", 512.0, ADD, 128)
    tt(T.IL[:, :], T.IL[:, :], BON, MUL, "ITF BON", "ITF", 256)
    lin("A", T.IL[:, :], T.IL[:, :], 1.0, col["k63"], "ITF ck63", "IT", 128)
    ts(FOLD, T.I64[:, :], col["p64"], EQ, "I64 CD", "FOLD", c=128)
    act(T.I64[:, :], T.IR[:, 0:128], AF.Identity, "IR ctm", "COLT I64", 1.0 / 128, col["tm"], 128)
    ms(T.RI[0:3, 0:256], 0.0, "RIa", 128)
    ms(T.RI[0:3, 256:512], 1.0, "RI", 128)
    for n, x in ((3, 2.0 ** -13), (2, -float(MID)), (1, -0.5)):
        ms(T.LC[0:n, :], x, "LC")
    for n, x in ((2, 0.5 - rank / 8), (1, -2048.0)):
        ms(T.LY[0:n, 0:128], x, "LY")
    ms(T.LY[0:1, 128:256], -512.0, "LN")
    m, E6, MQ = col["m"], T.EQ, T.MQ
    ts(E6[:, 0, :], T.IA[:, :], m, EQ, "IA CC", "E0")
    ts(E6[:, 1, :], T.IA[:, :], 1.0, ADD, "IA CC", "E1", m, EQ)
    ts(E6[:, 2, :], T.IB[:, :], m, EQ, "IB CC", "E2")
    ts(E6[:, 3, :], T.IB[:, :], 1.0, ADD, "IB CC", "E3", m, EQ)
    ts(E6[:, 3, :], E6[:, 3, :], m, MUL, "E3 CC", "E3", 0.0, ALU.is_gt)
    tt(E6[:, 4, :], T.IA[:, :], T.IB[:, :], ADD, "IA IB", "E4")
    ts(E6[:, 5, :], T.IB[:, :], 1.0, ALU.is_ge, "IB", "E5")
    ts(E6[:, 4, :], E6[:, 4, :], m, ALU.is_ge, "E4 CC", "E4")
    tt(E6[:, 0, :], E6[:, 0, :], E6[:, 1, :], SUB, "E0 E1", "E0")
    tt(E6[:, 3, :], E6[:, 2, :], E6[:, 3, :], SUB, "E2 E3", "E3")
    ts(col["t1"], m, 0.0, EQ, "CC", "ct1")
    tt(MQ[:, :, 0:16:4], E6[:, 0, :], E6[:, 4, :], MUL, "E0 E4", "MQ0")
    tt(MQ[:, :, 1:16:4], E6[:, 3, :], E6[:, 4, :], MUL, "E3 E4", "MQ1")
    tt(MQ[:, :, 2:16:4], E6[:, 1, :], E6[:, 4, :], MUL, "E1 E4", "MQ2")
    ts(E6[:, 2, :], E6[:, 2, :], m, MUL, "E2 E3 CC", "E2", 0.0, ALU.is_gt)
    ts(E6[:, 0, :], E6[:, 5, :], col["t1"], MUL, "E5 ct1 MQ0", "E0")
    tt(MQ[:, :, 3:16:4], E6[:, 0, :], E6[:, 2, :], SUB, "E0 E2", "MQ3")
    MQk = "MQ0 MQ1 MQ2 MQ3"
    tt(T.HI[:, 0:16], MQ[:, 4, :], MQ[:, 5, :], ADD, MQk, "HI")
    tt(T.HI[:, 0:16], T.HI[:, 0:16], MQ[:, 6, :], ADD, MQk + " HI", "HI")
    for s in (0, 1):
        act(T.T5[:, 80 * s + 4:80 * s + 80:5], T.HI[:, 0:16], AF.Copy, "HI", "T5c%d" % s, 128.0)
    ts(col["r0"], m, 7.0, EQ, "CC ct1", "cr0", col["t1"], SUB)
    ts(E6[:, 5, 16:28], E6[:, 5, 16:28], col["r0"], MUL, "E5 E0 cr0", "E5")
    tt(MQ[:, 4:7, 3:16:4], MQ[:, 4:7, 3:16:4], E6[:, 5, 16:28], ADD, "MQ3 E5 HI", "MQn")
    for a in (4, 5, 6):
        ts(MQ[:, a, :], MQ[:, a, :], col["h" if a % 2 == 0 else "h1"], MUL, MQk + " MQn HI CC ch1", "CF%d" % a, 0.25, MUL)
        for q in (0, 1):
            act(MQ[:, a, q:16:4], MQ[:, a, q:16:4], AF.Copy, "CF%d" % a, "CF%d" % a, 1.0 / 4096)
    ts(T.KN[:, 0, :], T.KA[:, :], m, ALU.is_lt, "KA CC cn7", "KN0", col["n7"], MUL)
    ts(T.KN[:, 1, :], T.KC[:, :], m, ALU.is_lt, "KC CC cn7", "KN1", col["n7"], MUL)
    tt(T.W16[:, :], T.KA[:, :], T.KC[:, :], ALU.not_equal, "KA KC", "NE")
    tt(T.KN[:, 1, :], T.KN[:, 1, :], T.W16[:, :], MUL, "KN1 NE", "KN1")
    tt(T.KN[:, 0, :], T.KN[:, 0, :], T.KN[:, 1, :], ADD, "KN0 KN1", "KN0")
    ts(T.KN[:, 1, :], T.W16[:, :], 0.5, MUL, "NE", "KN1", 0.5, ADD)
    tt(T.KN[:, 0, :], T.KN[:, 1, :], T.KN[:, 0, :], SUB, "KN0 KN1", "KN0")
    ts(T.KN[:, 1, :], T.W16[:, :], 1.0, ADD, "NE", "KN1")
    act(T.KT[:, :, :], T.KN[:, :, :], AF.Copy, "KN0 KN1", "KT", 1.0 / 4096)
    ms(T.RS5[:, :], 1.0, "RS5", 80)
    ms(T.RS5[:, 0:80:5], 0.0, "RS5")
    ms(T.RS4[:, :], 1.0, "RS4")
    ms(T.RS4[:, 0:32:4], 0.0, "RS4")
    cp(T.NLF[0:8, :], T.NL[0:8, :], "NL", "NLF")
    ms(T.W16[:, :], 0.0, "NE W16")
    for s in (0, 1):
        S[0] = s
        F, ST, CS = X("F"), X("ST"), X("CS")
        ts(T.SL[0:8, :], T.IG[0:8, :], 4.0 * s, ADD, "IG CC", "SL", CC[0:8, 0:1], EQ, 128)
        mm(bank("a")[:, 0:4], T.SL[0:8, :], T.NLF[0:8, :], "SL NLF", "a", c=256)
        cp(F[:, 0:4], bank("a")[:, 0:4], "a", "F@")
        for a in range(4):
            act(T.T5[:, 80 * s + a:80 * s + 80:5], MQ[:, a, :], AF.Copy, MQk + " F@", "T5%d@" % a, F[:, a:a + 1])
        o, base = slice(16 * s, 16 * s + 16), X("W")[:, 4:80:5]
        scan(X("W")[:, 0:80], T.RS5[:, :], T.T5[:, 80 * s:80 * s + 80], MUL, ADD, "RS5 T5c@ T50@ T51@ T52@ T53@", "W@", 80)
        ts(T.BS[:, o], base, M32, ADD, "W@", "BS@", M32, SUB)
        act(T.HI[:, o], base, AF.Copy, "W@ CC T5c0 T5c1 MQn", "T5h@", col["h"])
        act(T.BS[:, o], T.BS[:, o], AF.Copy, "BS@ chs", "BS@", col["hs"])
        tt(ST[:, :, 0:4], T.BS[:, o], T.HI[:, o], ADD, "BS@ T5h@", "ST@")
        act(ST[:, :, 0:2], ST[:, :, 0:2], AF.Copy, "ST@", "SU0@ SU1@ SU2@ SU3@", 0.5 / 4096)
        ts(ST[:, :, 2:4], ST[:, :, 2:4], 0.5, MUL, "ST@", "SV0@ SV1@ SV2@ SV3@")
        ts(CS[:, 16:20], F[:, 0:4], F[:, 3:4], MUL, "F@", "p3@", -2047.5, ADD)
        ts(CS[:, 20:22], F[:, 1:3], F[:, 2:3], MUL, "F@", "p2@", -2047.5, ADD)
        ts(T.W16[:, 0:16:5], CS[:, 16:20], M4096, ADD, "p3@ W16", "W16a", M4096, SUB)
        ts(T.W16[:, 1:7:5], CS[:, 20:22], M4096, ADD, "p2@ W16", "W16b", M4096, SUB)
        for k in (0, 1):
            tt(T.PB[:, 16 * k:16 * k + 16], T.KT[:, k, :], T.W16[:, :], MUL, "KT W16a W16b", "PB%d" % k)
        PB = X("W")
        scan(PB[:, 256:288], T.RS4[:, :], T.PB[:, :], MUL, ADD, "RS4 PB0 PB1", "Wz@")
        cp(CS[:, 2:3], PB[:, 275:276], "Wz@", "Ct@")
        act(ST[:, :, 5], PB[:, 275:288:4], AF.Copy, "Wz@", "SB1@ SB2@ SB3@")
        ts(ST[:, :, 4], PB[:, 259:272:4], col["cP"], SUB, "Wz@ ccP", "SA0@ SA1@ SA2@ SA3@")
        act(F[:, 4:5], F[:, 0:1], AF.Copy, "F@", "a0@", 1.0 / 8192)
        act(F[:, 5:6], F[:, 0:1], AF.Copy, "F@", "b0@", 1.0 / 32, HALF)
        act(F[:, 6:8], F[:, 1:3], AF.Copy, "F@", "F12@", 1.0 / 4096)
        ms(CS[:, 10:11], B / 4096.0, "T4@")
    ts(T.WCP[:, 0:8:2], T.IR[:, 0:4], col["g"], EQ, "IR CC ch1", "WCa", col["h1"], MUL)
    ts(T.WCP[:, 1:8:2], T.IR[:, 0:4], col["g"], EQ, "IR CC", "WCb", col["h"], MUL)
    act(T.WCP[:, 8:16], T.WCP[:, 0:8], AF.Copy, "WCa WCb", "WCc", -1.0)
    act(T.WCP[:, 16:24], T.WCP[:, 0:8], AF.Copy, "WCa WCb cwt", "WCP", col["wt"])
    for ap, k, x in ((NDG, "NDG", -1.0), (D512, "D512", 512.0), (D4, "D4", 0.25), (D8, "D8", 0.125)):
        act(ap, DG, AF.Copy, "DG", k, x, c=128)
    LMF, pt, pts = T.LMF, CC[0:16, 11:12], CC[0:16, 35:36]
    ts(LMF[0:16, 2:3], T.LM[0:16, 1:2], -1.0, MUL, "LM", "LM2", -0.5, ADD)
    ts(LMF[0:16, 3:4], T.LM[0:16, 0:1], -0.5, ADD, "LM", "LM3")
    ts(LMF[0:16, 4:6], LMF[0:16, 2:4], M32, ADD, "LM2 LM3", "LM4", M32, SUB)
    act(pts, pt, AF.Copy, "CD", "cpts", -2.0, 1.0)
    act(LMF[0:16, 0:2], LMF[0:16, 2:4], AF.Copy, "LM2 LM3 CD", "LM0", pt)
    for k in (0, 1):
        lin("A", LMF[0:16, 4 + k:5 + k], LMF[0:16, 4 + k:5 + k], pts, LMF[0:16, k:k + 1], "LM4 LM0 cpts", "LMx%d" % k)
    act(LMF[0:16, 6:7], pt, AF.Copy, "CD", "LMx2", 3.5, -3.5)
    for s in (0, 1):
        ts(T.GB[0:16, 128 * s + 128:128 * s + 256], T.GB[0:16, 0:128], 4.0 * s, ADD, "GB CD", "GM%d" % s, CC[0:16, 6:7], EQ)
        for k in range(3):
            act(T.PRE[0:16, 384 * s + 128 * k:384 * s + 128 * k + 128], T.GB[0:16, 128 * s + 128:128 * s + 256], AF.Copy, "GM%d LMx%d" % (s, k), "PRE%d%d" % (k, s), LMF[0:16, 4 + k:5 + k], c=128)
    act(W8, BON, AF.Copy, "BON cw8", "W8", col["w8"], c=128)
    act(B4, BON, AF.Copy, "BON", "B4", 4.0, c=128)
    ts(W04, BON, col["i0"], MUL, "BON ci0", "W04", 4.0, MUL)
    ms(T.Q25[:, :], 0.25, "Q25")
    scan(T.POW[:, :], T.Q25[:, :], T.ZERO[:, 0:32], MUL, ADD, "Q25 ZERO", "POW", init=4.0)
    ts(T.Q25[:, :], T.IR[:, 0:32], col["l"], EQ, "IR cl POW", "Q25")
    tt(T.Q25[:, :], T.Q25[:, :], T.POW[:, :], MUL, "Q25 POW", "Q25")
    do("V", lambda v: v.tensor_reduce(col["pw"], T.Q25[:, :], AX.X, ADD), "Q25", "cpw", 64)
    act(BW, BON, AF.Copy, "BON cpw", "BW", col["pw"], c=128)
    act(T.NTH[0:1, 0:32], T.POW[0:1, :], AF.Copy, "POW", "NTH", -2.0)
    for n in (32, 64, 128):
        act(T.NTH[0:1, n:2 * n], T.NTH[0:1, 0:n], AF.Copy, "NTH", "NTH", c=max(64, n))
    cl("lpc", "pid", 1.0, 15.0)
    act(col["mk"], col["i0"], AF.Copy, "ci0 ch1", "cmk", col["h1"])
    ts(T.LP[:, 0:80], T.IR[:, 0:80], col["lpc"], EQ, "IR clpc cmk", "LPa", col["mk"], MUL, 80)
    ts(T.LP[:, 79:144], T.IR[:, 15:80], col["lpc"], EQ, "IR clpc cmk LPa", "LP", col["mk"], MUL)
    ts(T.LI[:, 0:80], T.IR[:, 0:80], col["lic"], EQ, "IR clic cw8", "LIa", col["w8"], MUL, 80)
    ts(T.LI[:, 79:144], T.IR[:, 15:80], col["lic"], EQ, "IR clic cw8 LIa", "LI", col["w8"], MUL)
    ts(T.MI[:, 0:112], T.IR[:, 0:112], col["mic"], EQ, "IR cmic", "MIa", c=112)
    ts(T.MI[:, 112:176], T.IR[:, 48:112], col["mic"], EQ, "IR cmic", "MIb")
    act(T.MH[:, 0:112], T.MI[:, 0:112], AF.Copy, "MIa", "MHa", -33.0, c=112)
    act(T.MH[:, 112:176], T.MI[:, 112:176], AF.Copy, "MIb", "MHb", -31.0)
    for k, x in enumerate((2.0, 32.0, 1.0)):
        ts(T.RPM[:, 64 * k:64 * k + 64], T.I8[:, 64 * k:64 * k + 64], col["q8"], EQ, "I8 CD", "RPM%d" % k, x, MUL)
    lin("A", T.OCF[:, :], T.OCF[:, :], 1.0, col["hc"], "OCF chc", "OCF")
    for k, (x, y) in enumerate(((34.0, 33.0), (34.0, 0.0), (34.0, 17.0))):
        ts(T.OC[:, 4 * k:4 * k + 4], T.OCF[:, 4 * k:4 * k + 4], x, MUL, "OCF", "OC%d" % k, y, ADD)
    iota(T.RS2[:, :], [[0, 32], [1, 2]], "RS2")
    do("G", lambda q: q.affine_select(T.RS34[:, :], T.ONE[:, 0:306], [[0, 9], [1, 34]], ALU.not_equal, 0.0, -1, 0), "ONE", "RS34", 820)
    do("G", lambda q: q.affine_select(T.RS34[:, :], T.RS34[:, :], [[0, 9], [1, 34]], ALU.not_equal, 0.0, -2, 0), "RS34", "RS34", 820)
    lin("A", T.WJ[:, 1:32:2], T.WJ[:, 1:32:2], 1.0, col["i"], "WJ0 CC", "WJ")
    ts(T.ND[:, :], T.ND[:, :], col["i"], SUB, "ND0 CC", "ND", -0.5, ADD)
    ts(col["G8"], col["l"], 31.0, EQ, "cl", "cG8", MARK, MUL)
    for s in (0, 1):
        S[0] = s
        act(X("K")[:, 4097:4098], col["G8"], AF.Copy, "cG8 Ke@", "Km@")
        act(X("Z")[:, :, 0], T.ONE[:, 0:32], AF.Sign, "ONE CC", "Zr@", col["pid"])

    def lists(t):
        CS, ST, W, OF, R, d = X("CS"), X("ST"), X("W"), X("OF"), X("R"), bank("d")
        k, c = "%d@" % (t > 0), slice(256 * t, 256 * t + 256, 2)
        cl_, ct = ST[:, t, 4:5], CS[:, 2:3]
        lin("A", CS[:, 4:5], cl_, col["sg"], col["off"], "SA%d@ csg coff" % t, "SC@")
        mm(d[:, :], T.LC[0:3, :], T.RI[0:3, :], "LC RI RIa", "d", True, False, 512)
        sign = X("V")[:, :]
        do("A", lambda q: q.activation(sign, T.I64[:, :], AF.Sign, bias=cl_, scale=ct, accum_out=CS[:, 3:4]), "COLT Ct@ SA%d@" % t, "V@ ac@", 150 + ACT)
        lin(ON[3], W[:, 0:128], T.IL[:, :], ct, CS[:, 4:5], "IT Ct@ SC@", "W@", 128)
        ts(CS[:, 8:9], CS[:, 3:4], ct, MUL, "ac@ Ct@ cs256", "X@", col["s256"], MUL)
        ts(X("IND")[:, :], W[:, 0:128], CS[:, 8:9], ALU.is_ge, "W@ X@", "IND@", c=128)
        for q in range(4):
            val = CS[:, 12 + q:13 + q] if t and q < 2 else ST[:, t, q:q + 1]
            lin(RQ[q], X("XG")[:, 128 * q:128 * q + 128], X("V")[:, :], val, val, "V@ S%s%d@ VL%d@" % ("UUVV"[q], t, q), "RQ%d@" % q, 128 if RQ[q] == "A" else 64)
        mm(d[:, 0:256], X("IND")[:, :], X("XG")[:, 0:256], "IND@ RQ0@ RQ1@", "d", False, False, 256)
        mm(d[:, 256:512], X("IND")[:, :], X("XG")[:, 256:512], "IND@ RQ2@ RQ3@", "d", False, True, 256)
        ts(W[:, 256:384], R[:, 2, c], CS[:, 10:11], MUL, "R2" + k + " T4@", "Wz@", HALF - MID, ADD, 128)
        ts(OF[:, 256:384], W[:, 256:384], M1, ADD, "Wz@", "OZ@", M1 - MID, SUB, 128)
        for n, w_ in ((0, "W@"), (1, "Wy@")):
            tt(W[:, 128 * n:128 * n + 128], d[:, 128 * n:128 * n + 128], R[:, n, c], MUL, "d R%d" % n + k, w_, 128)
        for n, w_ in ((0, "W@"), (1, "Wy@")):
            tt(W[:, 128 * n:128 * n + 128], W[:, 128 * n:128 * n + 128], d[:, 256 + 128 * n:384 + 128 * n], ADD, "d " + w_, w_, 128)
        for n, w_ in ((0, "W@"), (1, "Wy@")):
            ts(OF[:, 128 * n:128 * n + 128], W[:, 128 * n:128 * n + 128], M1, ADD, w_, ("OX@", "OY@")[n], M1 - MID, SUB, 128)

    def pieces(q):
        return [(p, 512 // len(MODE[q])) for p in range(0, 512, 512 // len(MODE[q]))]

    def build(t):
        win, OF, K, XG, YG, ZG, FX, a = X("bank")[:, 0:B + 256 * t], X("OF"), X("K"), X("XG"), X("YG"), X("ZG"), X("FX"), bank("a")
        bk = " bk@ bz1@ bz2@" if t > 1 else " bk@"
        mm(a[:, 0:256], T.ONE[0:16, 0:128], T.PRE[0:16, 384 * S[0]:384 * S[0] + 256], "ONE PRE0@ PRE1@", "a", True, False, 256)
        mm(bank("d")[:, 0:128], T.ONE[0:16, 0:128], T.PRE[0:16, 384 * S[0] + 256:384 * S[0] + 384], "ONE PRE2@", "d", True, False, 128)
        if t == 0:
            more[len(ops) - 2] = more[len(ops) - 1] = EARLY
        tmp, n0 = 0, len(ops)
        for q in ORDER:
            op = (ALU.min, ALU.max, None, ADD)[q]
            for (p, PIECE), mode in zip(pieces(q), MODE[q]):
                gc_ = 70 + GATHER * PIECE
                o, k = 512 * q + p, "%d%d@" % (q, p)
                c, ko = slice(o, o + PIECE), K[:, 2 * o + 1:2 * (o + PIECE):2]
                x, y, z = [win.indirect(OF[:, b + o // 16:b + (o + PIECE) // 16]) for b in (0, 128, 256)]
                ky, kz = "OY@", "OZ@"
                if q == 0:
                    y, z, ky, kz = z, y, kz, ky
                act(YG[:, c], y, AF.Copy, ky + bk, "YG" + k, c=gc_)
                if mode == "a":
                    tt(FX[:, c], x, YG[:, c], op, "OX@ YG" + k + bk, "FX" + k, gc_)
                else:
                    b = "bc"[tmp % 2]
                    tmp += 1
                    pb = bank(b)[:, 0:PIECE]
                    act(XG[:, c], x, AF.Copy, "OX@" + bk, "XG" + k, c=gc_)
                    mm(pb, DG, XG[:, c], "DG XG" + k, b, True, False, PIECE)
                    mm(pb, DG if q == 3 else NDG, YG[:, c], "DG NDG YG" + k, b, False, True, PIECE)
                    if q < 2:
                        act(FX[:, c], pb, AF.Relu, b, "FX" + k, c=PIECE)
                        mm(pb, DG, (XG, YG)[q][:, c], "DG XG" + k + " YG" + k, b, True, False, PIECE)
                        mm(pb, (NDG, DG)[q], FX[:, c], "DG NDG FX" + k, b, False, True, PIECE)
                    if mode == "b":
                        act(FX[:, c], pb, AF.Abs, b, "FX" + k, c=PIECE)
                    elif q == 2:
                        act(pb, pb, AF.Abs, b, b, c=PIECE)
                if mode == "c":
                    act(ZG[:, c], z, AF.Copy, "OZ@" + bk, "ZG" + k, c=gc_)
                    tt(ko, pb, ZG[:, c], ALU.min, b + " ZG" + k, "K" + k, PIECE)
                else:
                    tt(ko, z, FX[:, c], ALU.min, kz + " FX" + k + bk, "K" + k, gc_)
            for b_ in range(16):
                kq, kk = K[:, 1024 * q + 2 * b_ + 1:1024 * q + 1024:32], " ".join("K%d%d@" % (q, p) for p, _ in pieces(q))
                mm(a[32 * q:32 * q + 32, b_:256:16], kq, T.WCP[:, 0:16], "WCa WCb WCc " + kk, "a", False, b_ == 15, 32)
            for b_ in range(16):
                kq = K[:, 1024 * q + 2 * b_ + 1:1024 * q + 1024:32]
                mm(bank("d")[32 * q:32 * q + 32, b_:128:16], kq, T.WCP[:, 16:24], "WCP " + kk, "d", False, b_ == 15, 32)
        for e in "VA":
            row = [k for k in range(n0, len(ops)) if ops[k][0] == e and ops[k][3] != int(ops[k][3])]
            if e == "V":
                row = row[0:1] + [k for x, z in zip(row[2::2], row[1::2]) for k in (x, z)] + row[-1:]
            for k, j in zip(row, row[1:]):
                late.append((k, j))

    def pick(t):
        a, b, c, d = [bank(k) for k in "abcd"]
        DS, V, O, S4, U, Z, WN, RJ, RR = [X(n) for n in ("DS", "V", "O", "S4", "U", "Z", "WN", "RJ", "RR")]
        act(DS[:, :], a[:, 0:256], AF.Sign, "a", "DS@", c=256)
        mm(b[:, 0:128], D4, DS[:, 0:128], "D4 DS@", "b", True, False, 128)
        mm(b[:, 0:128], D8, DS[:, 128:256], "D8 DS@", "b", False, True, 128)
        ts(RR[:, 0:128], d[:, 0:128], M8, ADD, "d", "RR@", M8, SUB, 128)
        tt(X("OW")[:, :], d[:, 0:128], RR[:, 0:128], SUB, "d RR@", "OW@", 128)
        tt(V[:, :], b[:, 0:128], X("OW")[:, :], ADD, "b OW@", "V@", 128)
        for p in range(8):
            ts(O[:, 16 * (p // 4) + p % 4:16 * (p // 4) + 16:4, :], V[:, :], p - 3.875, EQ, "V@", "O%d@" % p)
        for k in range(16):
            mm(b[:, 0:64], TRI, O[:, :, k:32:16], "TRI " + " ".join("O%d@" % p for p in range(8)), "b", k == 0, k == 15)
        for h, e in enumerate("cd"):
            mm(bank(e)[:, :], BID, O[:, 16 * h:16 * h + 16, :], "BID " + " ".join("O%d@" % p for p in range(4 * h, 4 * h + 4)), e, c=512)
            act(Z[:, 16 * h:16 * h + 16, 2:34], bank(e)[:, :], AF.Copy, e, "Zv%d@" % h, c=512)
        scan(RJ[:, 0:64], T.RS2[:, :], b[:, 0:64], MUL, ADD, "b RS2", "RJ@")
        for r in range(4):
            lin(SQ[r], S4[:, r:128:4], RJ[:, 1:64:2], 1.0, -float(r), "RJ@", "S%d@" % r)
        mm(a[:, 0:32], BID, RJ[:, 1:64:2], "BID RJ@", "a")
        if SQ[4] == "A":
            act(Z[:, :, 1], a[:, 0:32], AF.Copy, "a", "Zs@")
        else:
            cp(Z[:, :, 1], a[:, 0:32], "a", "Zs@")
        for k in range(8):
            ts(U[:, :, 4 * k:4 * k + 4], S4[:, :], 4.0 * k, ALU.is_le, "S0@ S1@ S2@ S3@", "U%d@" % k)
        uk = " " + " ".join("U%d@" % k for k in range(8))
        for k in range(32):
            mm(b[32 * (k % 4):32 * (k % 4) + 32, 34 * (k // 4):34 * (k // 4) + 34], U[:, k, :], Z[:, k, :], "Zv%d@ Zs@ Zr@" % (k // 16) + uk, "b", c=34)
        scan(WN[:, 0:272], T.RS34[:, 1:273], b[:, 0:272], MUL, ADD, "RS34 b", "CU@", 272)
        ts(WN[:, 544:816], WN[:, 0:272], col["c32"], ALU.is_le, "CU@ CD", "IN@", c=136)
        scan(WN[:, 272:544], T.RS34[:, 0:272], WN[:, 544:816], MUL, ADD, "RS34 IN@", "C2@", 136)
        for k, (o, r) in ((1, (0, "CU@")), (2, (544, "IN@")), (0, (272, "C2@"))):
            tt(RJ[:, 64 * k:64 * k + 64], WN[:, o:o + 272].indirect(T.OC[:, 4 * k:4 * k + 4]), T.RPM[:, 64 * k:64 * k + 64], MUL, r + " OC%d RPM%d" % (k, k),
               "RJ@" if k == 0 else "RK%d@" % k, 60 + 64 * GATHER)
            for q in range(4):
                mm(c[:, 0:16], (T.MH if k == 2 else T.MI)[:, 48 - 16 * q:176 - 16 * q], RJ[:, 64 * k + 16 * q:64 * k + 16 * q + 16], "MIa MIb MHa MHb " + ("RJ@" if k == 0 else "RK%d@" % k), "c",
                   k == 1 and q == 0, k == 0 and q == 3)
        ts(X("OS")[:, 0, :], c[:, 0:16], col["h1"], ADD, "c ch1", "OJ@")
        o, send, land = 256 * t, X("send"), X("land")
        kk = " ".join("K%d%d@" % (q, p) for q in range(4) for p, _ in pieces(q)) + " Kz0@ Kz1024@ Kz2048@ Kz3072@ Ke@ Km@"
        act(send[:, o:o + 256], X("K")[:, :].indirect(X("OS")[:, 0, :]), AF.Copy, "OJ@ " + kk, "snd%d@" % t, c=75 + 256 * GATHER)
        tr, k, name = [], 0, "%d%d" % (S[0], t)
        for p in range(NR):
            if p != rank:
                e = topo.engines(core, T.cores[p])
                rid, pid, _se = topo.addr(T.cores[p])
                tr.append(RemoteDMATransfer(dst_ids=[DstId(rid=rid, pnc=pid)], dma_engine_mask=(1 << e[2 * k]) | (1 << e[2 * k + 1]), remote_sem=T.sem["arr" + name],
                                            srcs=[send[:, o + 32 * p:o + 32 * p + 32]], dsts=[land[:, o + 32 * rank:o + 32 * rank + 32]]))
                k += 1
        do("G", lambda q: g.remote_dma_fused(tr, local_sem=T.sem["sent" + name]), "snd%d@" % t, "arr%d@" % t, 600 if t + S[0] else 2400, FLIGHT, ("arr" + name, 14))
        lin(ON[4], land[:, o + 32 * rank:o + 32 * rank + 32], send[:, o + 32 * rank:o + 32 * rank + 32], 1.0, 0.0, "snd%d@" % t, "own%d@" % t)

    def keep(t):
        a, b, c, d = [bank(k) for k in "abcd"]
        RR, KB, E, UG, PK, SM, OS, LF, CS, ST, UP, F = [X(n) for n in ("RR", "KB", "E", "UG", "PK", "SM", "OS", "LF", "CS", "ST", "UP", "F")]
        last, lnd, lk = t == RO - 1, X("land")[:, 256 * t:256 * t + 256], " arr%d@ own%d@" % (t, t)
        act(CS[:, 11:12], CS[:, 10:11], AF.Copy, "T4@", "TB@", 4096.0, 127.5 - B)
        act(CS[:, 9:10], CS[:, 10:11], AF.Copy, "T4@", "T4b@", 1.0, 1.0 / 32)
        mm(a[:, :], T.LY[0:2, 0:128], T.ONE[0:2, :], "LY ONE", "a", True, False, 512)
        mm(a[:, 256:512], T.LC[0:1, :], T.ONE[0:1, 0:256], "LC ONE", "a", False, False, 256)
        mm(a[:, 0:256], W8, lnd, "W8" + lk, "a", False, False, 256)
        mm(a[:, 256:512], W8, lnd, "W8" + lk, "a", False, True, 256)
        if last:
            mm(d[:, 0:256], T.LY[0:1, 128:256], T.ONE[0:1, 0:256], "LN ONE", "d", True, False, 256)
        mm(d[:, 0:256], FOLD, lnd, "FOLD" + lk, "d", not last, not last, 256)
        if not last:
            act(LF[:, :], d[:, 0:256], AF.Copy, "d", "LF@", c=256)
        mm(c[:, 0:256], T.ONE[0:1, 0:128], T.NTH[0:1, :], "ONE NTH", "c", True, False, 256)
        for h, w_ in ((1, "Wy@"), (0, "W@")):
            ts(RR[:, 128 * h:128 * h + 128], a[:, 128 * h:128 * h + 128], M4096, ADD, "a", w_, M4096, SUB, 128)
        for h, w_ in ((1, "Wy@"), (0, "W@")):
            tt(KB[:, 128 * h:128 * h + 128], a[:, 256 + 128 * h:384 + 128 * h], RR[:, 128 * h:128 * h + 128], SUB, "a " + w_, "KB%d@" % h, 128)
        mm(b[:, 0:16], T.LY[0:2, 0:128], T.ONE[0:2, 0:16], "LY ONE", "b", True, False)
        for i in range(16):
            mm(b[:, 0:16], T.LI[:, 15 - i:143 - i], X("land")[:, 256 * t + i:256 * t + 256:16], "LI" + lk, "b", False, i == 15)
        ts(SM[:, 5, :], b[:, 0:16], M4096, ADD, "b", "r16@", M4096, SUB)
        ts(E[:, 8, :], KB[:, :], MARK * 219 / 8 - rank / 8 - 2048, EQ, "KB0@ KB1@", "EM@", c=128)
        mm(c[:, 0:256], W04, E[:, 8, :], "W04 EM@ c", "", False, False, 256)
        for h in (0, 1):
            tt(SM[64 * h:64 * h + 64, 0, 0:8], b[64 * h:64 * h + 64, h:16:2], SM[64 * h:64 * h + 64, 5, h:16:2], SUB, "b r16@", "BL%d@" % h)
        tt(SM[:, 6, :], b[:, 0:16], SM[:, 5, :], SUB, "b r16@", "B16@")
        ts(OS[:, 1, :], SM[:, 6, :], 2047.5, ADD, "B16@", "BU@")
        for m_ in range(8):
            ts(E[:, m_, 0:256 - 32 * m_], KB[:, 32 * m_:256], 0.5, ADD, "KB1@ BL0@ BL1@" + (" KB0@" if m_ < 4 else ""), "E%d@" % m_, SM[:, 0, m_:m_ + 1], EQ, max(64, 128 - 16 * m_))
            if m_ < 7:
                mm(c[:, 32 * m_ + 32:256], B4, E[:, m_, 32:256 - 32 * m_], "B4 E%d@ c" % m_, "", False, False, max(64, 224 - 32 * m_))
            if m_ == 3:
                mm(c[:, 0:128], BW, E[:, 0:4, 0:32], "BW E0@ E1@ E2@ E3@ c", "", False, False, 128)
        act(UG[:, :], X("USED")[:, :].indirect(OS[:, 1, :]), AF.Copy, "US@ BU@", "UG@", c=75 + 256 * GATHER)
        mm(c[:, 128:256], BW, E[:, 4:8, 0:32], "BW E4@ E5@ E6@ E7@ c", "", False, False, 128)
        mm(c[:, 0:256], W04, UG[:, :], "W04 UG@", "c", False, True, 256)
        P = CS[:, 22:23]
        do("A", lambda q: q.activation(PK[:, :, 0], c[:, 0:256], AF.Sign, bias=0.0, scale=-1.0, accum_out=P), "c", "KP@ P@", 280 + ACT)
        scan(PK[:, :, 1], T.ONE[:, 0:256], PK[:, :, 0], MUL, ADD, "ONE KP@", "PS@", 128)
        if last:
            mm(d[:, 0:256], D512, PK[:, :, 0], "D512 KP@", "d", False, True, 256)
            act(LF[:, :], d[:, 0:256], AF.Relu, "d", "LF@", c=256)
        else:
            ts(X("WI")[:, :], P, F[:, 4:5], MUL, "P@ a0@ b0@", "w0@", F[:, 5:6], ADD)
            ts(CS[:, 2:3], X("WI")[:, :], 2.0, MUL, "w0@ SB%d@" % (t + 1), "Ct@", ST[:, t + 1, 5:6], ADD)
            lin(ON[0], CS[:, 10:11], P, 1.0 / 8192, CS[:, 9:10], "P@ T4b@ TB@", "T4@")
            for q in (0, 1):
                lin(ON[1 + q], CS[:, 12 + q:13 + q], P, MQ[:, 4 + t, 4 * t + 4 + q:4 * t + 5 + q], ST[:, t + 1, q:q + 1], "P@ SU%d@ CF%d" % (t + 1, 4 + t), "VL%d@" % q)
        for i in range(16):
            mm(b[:, 32:64], T.LP[:, 15 - i:143 - i], PK[:, i:256:16, :], "LP KP@ PS@", "b", i == 0, i == 15)
        scan(CS[:, 32:64], T.WJ[:, :], b[:, 32:64], MUL, ADD, "b WJ WJz", "D2@")
        ts(OS[:, 2, :], CS[:, 33:64:2], 0.5, MUL, "D2@ TB@", "DU@", CS[:, 11:12], ADD)
        for k in range(0, 16, 16 // APP):
            cp(X("bank")[:, B:B + 256 * t + 256].indirect(OS[:, 2, k:k + 16 // APP]), LF[:, 16 * k:16 * k + 256 // APP], "LF@ DU@" + (" bz1@ bz2@" if t else ""), "bk@", 60 + 256 // APP * SCATTER)
        if last:
            return
        for h in (0, 1):
            tt(SM[64 * h:64 * h + 64, 3, 0:8], b[64 * h:64 * h + 64, 32 + 2 * h:64:4], T.ND[64 * h:64 * h + 64, :], MUL, "b ND", "E1%d@" % h)
        tt(SM[:, 4, 0:8], SM[:, 3, 0:8], SM[:, 0, 0:8], ALU.max, "E10@ E11@ BL0@ BL1@", "Em@")
        ts(OS[:, 3, 0:8], SM[:, 4, 0:8], 2047.5, ADD, "Em@", "EU@")
        taken = X("USED")[:, :].indirect(OS[:, 3, 0:8])
        k = do("A", lambda q: q.activation(taken, T.IR[:, 128:256], AF.Sigmoid), "EU@ IR", "US@", 80 + 128 * SCATTER + (1600 if t + S[0] == 0 else 0))
        if t == 0:
            late.append((marks[0], k)) if marks else marks.append(k)
        if t < 2:
            act(CS[:, 14:15], P, AF.Copy, "P@", "nf@", 0.5, 128.0)
            act(CS[:, 16:18], F[:, 6:8], AF.Copy, "nf@ F12@ p3@", "x12@", CS[:, 14:15], HALF)
            ts(CS[:, 18:20], CS[:, 16:18], M1, ADD, "x12@ p3@", "w12@", M1, SUB)
            act(UP[:, t + 2:4, 0:4], MQ[:, 4 + t, 4 * t + 8:16], AF.Copy, "P@ CF%d" % (4 + t), "UP@", P)
            for u in range(t + 2, 4):
                k = u - t - 1
                act(UP[:, u, 4:6], T.KN[:, :, 4 * u + k], AF.Copy, "KN0 KN1 w12@", "UP%d@" % u, CS[:, 17 + k:18 + k])
            tt(ST[:, t + 2:4, :], ST[:, t + 2:4, :], UP[:, t + 2:4, :], ADD, "UP@ UP2@ UP3@", " ".join("S%s%d@" % (k, u) for k in "UVAB" for u in range(t + 2, 4)))

    first, more, late, marks, ahead = [], {}, [], [], {}
    for s in (0, 1):
        S[0] = s
        first.append(len(ops))
        for t in range(RO):
            for step[0], f in (("l", lists), ("b", build), ("p", pick), ("k", keep)):
                f(t)
                if f is pick:
                    more[len(ops) - 2] = (LAG[t + 1] - LAG[t] if s else 0) if t < 3 else 0
        dma("out%d" % s, [(T.y[64 * s:64 * s + 64, :], X("bank")[0:64, B:4096])], "bk@ bz1@ bz2@", "out@", 700)

    n = len(ops)
    succ, level, lead = [[] for _ in ops], [0.0] * n, [LAG[3] if k < first[1] else 0 for k in range(n)]
    for k, j in late:
        ops[j][2].setdefault(k, False)
    for k, o in enumerate(ops):
        for d in o[2]:
            succ[d].append(k)
    topo_, left = [k for k in range(n) if not ops[k][2]], [len(o[2]) for o in ops]
    for k in topo_:
        for j in succ[k]:
            left[j] -= 1
            if not left[j]:
                topo_.append(j)

    def gap(d, k):
        return 0 if ops[d][0] == ops[k][0] and (ops[d][0] == "P" or not ops[k][2][d]) else HOP + ops[d][4] + (DRAIN if ops[d][0] == "P" else 0)
    for k in topo_[::-1]:
        level[k] = ops[k][3] + max([gap(k, j) + level[j] for j in succ[k]] + [ops[k][4]]) + (lead[k] if not succ[k] else 0) + more.get(k, 0)

    def place(order, before, wait):
        start, busy = [0.0] * n, {e: [] for e in eng}
        for k in order:
            at, c, row = max([start[d] + ops[d][3] + wait(d, k) for d in before[k]] + [0.0]), ops[k][3], busy[ops[k][0]]
            i = len(row)
            while i and row[i - 1][1] > at:
                i -= 1
            while i < len(row) and row[i][0] < at + c:
                at = max(at, row[i][1])
                i += 1
            row.insert(i, (at, at + c))
            start[k] = at
        return start
    pred = [list(o[2]) for o in ops]
    start = place(sorted(range(n), key=lambda k: (-level[k], k)), pred, gap)
    for _ in range(PASSES):
        back = place(sorted(range(n), key=lambda k: (-start[k] - ops[k][3], -k)), succ, lambda d, k: gap(k, d))
        turn = [-back[k] - ops[k][3] - AHEAD.get(ops[k][6], 0) for k in range(n)]
        for k in topo_:
            turn[k] = max([turn[k]] + [turn[d] + 0.001 for d in pred[k]])
        start = place(sorted(range(n), key=lambda k: (turn[k], k)), pred, gap)
    seq = sorted(range(n), key=lambda k: (start[k], k))
    mark, cnt, seen = {}, {e: 0 for e in eng}, {e: {} for e in eng}
    for k in seq:
        e, call, dep, _c, _l, sem, _n = ops[k]
        need = {}
        for d, hard in dep.items():
            if hard and not (e == "P" and ops[d][0] == "P"):
                need[mark[d][0]] = max(need.get(mark[d][0], 0), mark[d][1])
        for s_ in sorted(need):
            if seen[e].get(s_, 0) < need[s_]:
                eng[e].wait_ge(T.sem[s_], need[s_])
                seen[e][s_] = need[s_]
        if sem:
            call(eng[e])
            mark[k] = sem
        else:
            cnt[e] += 1
            call(eng[e]).then_inc(T.sem["s" + e], 1)
            mark[k] = ("s" + e, cnt[e])
    for s in (0, 1):
        for t in range(RO):
            g.wait_ge(T.sem["sent%d%d" % (s, t)], 14)
    for e in ("V", "A", "P", "G"):
        g.wait_ge(T.sem["s" + e], cnt[e])
    for o in ops:
        if o[5] and o[0] == "S":
            g.wait_ge(T.sem[o[5][0]], o[5][1])
